import numpy as np
import ml_dtypes


def mxq(x, axis, fmt="e4m3"):
    dtype, down = {"e4m3": (ml_dtypes.float8_e4m3fn, 7), "e5m2": (ml_dtypes.float8_e5m2, 14)}[fmt]
    v = np.moveaxis(np.asarray(x, np.float32).astype(ml_dtypes.bfloat16).astype(np.float64), axis, -1)
    blocks = v.reshape(v.shape[:-1] + (-1, 32))
    amax = np.abs(blocks).max(-1, keepdims=True)
    byte = np.maximum(np.where(amax > 0, np.frexp(amax)[1] - 1 + 127, 0) - down, 1)
    scale = np.exp2(byte - 127.0)
    codes = (blocks / scale).astype(np.float32).astype(dtype).astype(np.float64)
    return np.moveaxis((codes * scale).reshape(v.shape), -1, axis)


WIDE = False


def mx_kscale(k):
    if not WIDE:
        return np.ones(k)
    levels = np.array([10, -10, 5, -5, 0])
    if k % 512:
        return np.exp2(np.random.permutation(np.resize(levels, k // 32))).repeat(32)
    a = np.empty((k // 512, 16))
    for p in range(k // 512):
        a[p, :8] = np.random.permutation(np.resize(levels, 8))
        for g in range(8):
            far = levels[np.abs(levels - a[p, g]) >= 10]
            a[p, g + 8] = far[np.random.randint(len(far))]
    return np.exp2(a.ravel()).repeat(32)


def f64(x):
    return np.asarray(x).astype(np.float64)


def striped(idx):
    return np.tile(idx.reshape(-1, 16).T, (8, 1)).astype(np.uint16)


def unstriped(offs):
    return offs[:16].T.reshape(-1).astype(np.int64)


E2M1 = np.array([0.0, 0.5, 1.0, 1.5, 2.0, 3.0, 4.0, 6.0, -0.0, -0.5, -1.0, -1.5, -2.0, -3.0, -4.0, -6.0])


def pack_weight(w, fmt):
    k, n = w.shape
    w = f64(np.asarray(w, np.float32).astype(ml_dtypes.bfloat16)).reshape(k // 32, 32, n)
    amax = np.abs(w).max(1)
    if fmt == "e4m3":
        byte = np.frexp(amax)[1] - 1 + 127 - 7
    else:
        mant, ex = np.frexp(amax / 6.0)
        byte = np.where(mant > 0.5, ex, ex - 1) + 127
    byte = np.clip(np.where(amax > 0, byte, 1), 1, 254)
    scaled = (w * np.exp2(127.0 - byte)[:, None, :]).reshape(k, n).astype(np.float32)
    by_word = np.ascontiguousarray(scaled.reshape(k // 512, 128, 4, n).transpose(0, 1, 3, 2))
    if fmt == "e4m3":
        words = by_word.astype(ml_dtypes.float8_e4m3fn).view(np.uint8)
    else:
        c = by_word.astype(ml_dtypes.float4_e2m1fn).view(np.uint8) & 0xF
        words = (c[..., 0::2] | (c[..., 1::2] << 4)).reshape(k // 512, 128, 2 * n)
    return np.ascontiguousarray(words), np.ascontiguousarray(byte.astype(np.uint8).reshape(k // 512, 16, n))


def unpack_weight(words, scales, fmt):
    g, _, n = scales.shape
    words = np.ascontiguousarray(words).reshape(g, 128, n, -1)
    if fmt == "e4m3":
        vals = words.view(ml_dtypes.float8_e4m3fn).astype(np.float64)
    else:
        nib = np.empty((g, 128, n, 4), np.uint8)
        nib[..., 0::2] = words & 0xF
        nib[..., 1::2] = words >> 4
        vals = E2M1[nib]
    vals = vals * np.repeat(np.exp2(scales.astype(np.float64) - 127.0), 8, axis=1)[..., None]
    return vals.transpose(0, 1, 3, 2).reshape(g * 512, n)


def d_relu(v):
    return (v > 0).astype(np.float64)


K, T, E, C, H, N, TOP = 128, 768, 9, 256, 512, 512, 3


def by_expert(wq, xq):
    return np.concatenate([wq[e].T @ xq[:, e * C:(e + 1) * C] for e in range(E)], axis=1)


def setup_inputs():
    n = np.random.standard_normal
    v = mx_kscale(N)
    u = mx_kscale(H)
    deal = np.repeat(np.arange(E), C).reshape(TOP, T)[:, np.random.permutation(T)]
    deal = np.take_along_axis(deal, np.argsort(np.random.rand(TOP, T), axis=0), axis=0)
    for _ in range(8):
        s_, t_ = np.random.permutation(T).reshape(2, -1); r = np.random.randint(TOP, size=T // 2); x, y = deal[r, s_].copy(), deal[r, t_].copy()
        ok = ~((deal[:, s_] == y).any(0) | (deal[:, t_] == x).any(0)); deal[r[ok], s_[ok]] = y[ok]; deal[r[ok], t_[ok]] = x[ok]
    order = np.lexsort((np.random.rand(TOP * T), deal.reshape(-1)))
    slot_token = order % T; pos = np.empty(TOP * T, np.int64); pos[order] = np.arange(TOP * T); pos = pos.reshape(TOP, T)
    g = np.random.uniform(0.5, 1.5, (TOP, T)); g = g / g.sum(0)
    w_slot = np.empty(E * C)
    for r in range(TOP): w_slot[pos[r]] = g[r]
    dy = pack_weight(n((N, T)) * v[:, None], "e4m3")
    w2t = pack_weight(n((N, H)) / np.sqrt(N) / v[:, None] * u, "e2m1")
    w1t = [pack_weight(m, "e2m1") for m in n((E, H, K)) / np.sqrt(H) / u[None, :, None]]
    return {
        "dy_words": dy[0],
        "dy_scales": dy[1],
        "w2t_words": w2t[0],
        "w2t_scales": w2t[1],
        "w1t_words": np.stack([m[0] for m in w1t]),
        "w1t_scales": np.stack([m[1] for m in w1t]),
        "a": (n((H, E * C))).astype(np.float32),
        "gate": (np.tile(w_slot, (128, 1))).astype(np.float32),
        "offs": striped(slot_token),
        "pos1": striped(pos[0]),
        "pos2": striped(pos[1]),
        "pos3": striped(pos[2]),
    }


def reference(dy_words, dy_scales, w2t_words, w2t_scales, w1t_words, w1t_scales, a, gate, offs, pos1, pos2, pos3):
    w2t = unpack_weight(w2t_words, w2t_scales, "e2m1")
    w1t = np.stack([unpack_weight(w1t_words[e], w1t_scales[e], "e2m1") for e in range(E)])
    idx = unstriped(offs)
    dc = w2t.T @ unpack_weight(dy_words, dy_scales, "e4m3")
    da = f64(gate[:1]) * dc[:, idx] * d_relu(f64(a))
    dx = by_expert(w1t, mxq(da, 0, "e4m3"))
    out = dx[:, unstriped(pos1)] + dx[:, unstriped(pos2)] + dx[:, unstriped(pos3)]
    return out

@@ -1,0 +1,187 @@
+from contextlib import ExitStack
+
+import concourse.mybir as mybir
+
+K, T, E, C, H, N = 128, 768, 9, 256, 512, 512
+S = E * C
+P = 128
+PACK = 4
+FLOPS = 2 * N * H * T + 2 * H * K * S
+
+F32 = mybir.dt.float32
+BF16 = mybir.dt.bfloat16
+I32 = mybir.dt.int32
+U32 = mybir.dt.uint32
+U16 = mybir.dt.uint16
+U8 = mybir.dt.uint8
+FP8X4 = mybir.dt.float8_e4m3fn_x4
+FP4X4 = mybir.dt.float4_e2m1fn_x4
+ALU = mybir.AluOpType
+ACT = mybir.ActivationFunctionType
+
+CHUNKS = [512, 512, 512, 512, 256]
+TOKEN_PARTS = [384, 384]
+
+
+def tile_moe_sdb_relu_kernel(
+    tc, dy_words, dy_scales, w2t_words, w2t_scales, w1t_words, w1t_scales, a, gate, offs, pos1, pos2, pos3, out
+):
+    nc = tc.nc
+    starts = [sum(CHUNKS[:c]) for c in range(len(CHUNKS))]
+
+    with ExitStack() as ctx:
+        keep = ctx.enter_context(tc.tile_pool(name="keep", bufs=1))
+        ring = ctx.enter_context(tc.tile_pool(name="ring", bufs=2))
+        psum = ctx.enter_context(tc.psum_pool(name="psum", bufs=3))
+        psum_dx = ctx.enter_context(tc.psum_pool(name="psum_dx", bufs=2))
+
+        w2_plane_raw = keep.tile([P, H], U8, align_bytes=64)
+        dy_plane = keep.tile([P, T], U8, align_bytes=64)
+        w1_plane = keep.tile([P, E * K], U8, align_bytes=64)
+        nc.vector.memset(w2_plane_raw[:].bitcast(I32), 0)
+        nc.gpsimd.memset(dy_plane[:].bitcast(I32), 0)
+
+        nc.vector.memset(w1_plane[:].bitcast(I32), 0)
+        warm = keep.tile([P, 8], F32)
+        nc.vector.memset(warm[:], 0.0)
+        warm_out = keep.tile([P, 8], BF16)
+        nc.scalar.activation(warm_out[:], warm[:], ACT.Sign)
+
+        w2_raw = keep.tile([P, 2 * H], U8, align_bytes=64)
+        nc.sync.dma_start(w2_raw[:].bitcast(I32), w2t_words[0].bitcast(I32))
+        dy_codes = keep.tile([P, 4 * T], U8, align_bytes=64)
+        nc.sync.dma_start(dy_codes[:].bitcast(I32), dy_words[0].rearrange("p t d -> p (t d)").bitcast(I32))
+        for q in range(4):
+            nc.sync.dma_start(
+                w2_plane_raw[32 * q : 32 * q + 4, :].bitcast(I32), w2t_scales[0, 4 * q : 4 * q + 4, :].bitcast(I32)
+            )
+        for q in range(4):
+            (nc.sync if q < 2 else nc.gpsimd).dma_start(
+                dy_plane[32 * q : 32 * q + 4, :].bitcast(I32), dy_scales[0, 4 * q : 4 * q + 4, :].bitcast(I32)
+            )
+        offs_t = keep.tile([P, S // 16], U16)
+        nc.sync.dma_start(offs_t[:], offs)
+
+        a_rows = a.rearrange("(p t) s -> p t s", t=PACK)
+        a_t = []
+        g_t = []
+        for c, (s0, n) in enumerate(zip(starts, CHUNKS)):
+            g_t.append(keep.tile([P, n], F32, name="gate%d" % c))
+            nc.sync.dma_start(g_t[c][:], gate[:, s0 : s0 + n])
+            a_t.append(keep.tile([P, PACK, n], F32, name="a%d" % c))
+            nc.sync.dma_start(a_t[c][:], a_rows[:, :, s0 : s0 + n])
+            if c == 0:
+                w1_codes = keep.tile([P, E, 2 * K], U8, align_bytes=64)
+                nc.sync.dma_start(
+                    w1_codes[:].bitcast(I32), w1t_words[:, 0].rearrange("e p b -> p e b").bitcast(I32)
+                )
+                for q in range(4):
+                    nc.sync.dma_start(
+                        w1_plane[32 * q : 32 * q + 4, :].rearrange("r (e k) -> r e k", e=E).bitcast(I32),
+                        w1t_scales[:, 0, 4 * q : 4 * q + 4, :].rearrange("e r k -> r e k").bitcast(I32),
+                    )
+        pos_t = []
+        for r, pos in enumerate((pos1, pos2, pos3)):
+            pos_t.append(keep.tile([P, T // 16], U16, name="pos%d" % r))
+            nc.sync.dma_start(pos_t[r][:], pos)
+
+        w2_codes = keep.tile([P, 2 * H], U8, align_bytes=64)
+        w2_plane = keep.tile([P, H], U8, align_bytes=64)
+        for ts in (slice(0, 1), slice(1, PACK)):
+            nc.vector.tensor_copy(
+                w2_codes[:].bitcast(U16).rearrange("p (t m) -> p t m", t=PACK)[:, ts, :],
+                w2_raw[:].bitcast(U16).rearrange("p (m t) -> p t m", t=PACK)[:, ts, :],
+            )
+            nc.vector.tensor_copy(
+                w2_plane[:].rearrange("p (t m) -> p t m", t=PACK)[:, ts, :],
+                w2_plane_raw[:].rearrange("p (m t) -> p t m", t=PACK)[:, ts, :],
+            )
+
+        dc = []
+        for t in range(PACK):
+            dc.append(keep.tile([P, T], F32, name="dc%d" % t))
+            for t0, n in ((0, 512), (512, 256)):
+                acc = psum.tile([P, n], F32, name="dc_acc%d" % n)
+                nc.tensor.matmul_mx(
+                    out=acc[:],
+                    lhsT=w2_codes[:, 2 * P * t : 2 * P * (t + 1)].bitcast(FP4X4),
+                    lhsT_scale=w2_plane[:, P * t : P * (t + 1)],
+                    rhs=dy_codes[:, 4 * t0 : 4 * (t0 + n)].bitcast(FP8X4),
+                    rhs_scale=dy_plane[:, t0 : t0 + n],
+                    start=True,
+                    stop=True,
+                )
+                if t == 0 and t0 > 0:
+                    nc.vector.tensor_copy(dc[t][:, t0 : t0 + n], acc[:])
+                else:
+                    nc.scalar.copy(dc[t][:, t0 : t0 + n], acc[:])
+
+        dx = keep.tile([P, S], F32)
+        steps = {}
+        woven = {}
+
+        def make_mask(c):
+            n = CHUNKS[c]
+            steps[c] = keep.tile([P, PACK * n], BF16, name="mask%d" % c, align_bytes=64)
+            nc.scalar.activation(
+                steps[c][:].rearrange("p (u i t) -> p u t i", i=4, t=PACK),
+                a_t[c][:].rearrange("p t (u i) -> p u t i", i=4),
+                ACT.Sign,
+            )
+            nc.vector.tensor_scalar_max(steps[c][:], steps[c][:], 0.0)
+
+        def gather(c):
+            s0, n = starts[c], CHUNKS[c]
+            gd = ring.tile([P, PACK, n], F32, name="gd")
+            for t in range(PACK):
+                nc.vector.tensor_tensor(
+                    gd[:, t, :], dc[t][:].indirect(offs_t[:, s0 // 16 : (s0 + n) // 16]), g_t[c][:], ALU.mult
+                )
+            woven[c] = ring.tile([P, PACK * n], BF16, name="woven", align_bytes=64)
+            nc.scalar.copy(
+                woven[c][:].rearrange("p (u i t) -> p u t i", i=4, t=PACK),
+                gd[:].rearrange("p t (u i) -> p u t i", i=4),
+            )
+
+        def experts(c, v0, n, empty):
+            s0 = starts[c] + v0
+            cols = slice(PACK * v0, PACK * (v0 + n))
+            da = ring.tile([P, PACK * n], BF16, name="da", align_bytes=64)
+            nc.vector.tensor_tensor(da[:], woven[c][:, cols], steps[c][:, cols], ALU.mult)
+            codes = ring.tile([P, n], U32, name="codes", align_bytes=64)
+            plane = ring.tile([P, n], U8, name="plane", align_bytes=64)
+            nc.vector.quantize_mx(out=codes[:].bitcast(FP8X4), scales=plane[:], in_=da[:])
+            acc = psum_dx.tile([P, n], F32, name="dx_acc")
+            width = min(n, C)
+            for u0 in range(0, n, width):
+                e = (s0 + u0) // C
+                nc.tensor.matmul_mx(
+                    out=acc[:, u0 : u0 + width],
+                    lhsT=w1_codes[:, e, :].bitcast(FP4X4),
+                    lhsT_scale=w1_plane[:, K * e : K * (e + 1)],
+                    rhs=codes[:, u0 : u0 + width].bitcast(FP8X4),
+                    rhs_scale=plane[:, u0 : u0 + width],
+                    start=True,
+                    stop=True,
+                )
+            empty(dx[:, s0 : s0 + n], acc[:])
+
+        for c in range(len(CHUNKS)):
+            gather(c)
+            if c > 0:
+                experts(c - 1, 0, CHUNKS[c - 1], nc.scalar.copy)
+            make_mask(c)
+        experts(len(CHUNKS) - 1, 0, 128, nc.scalar.copy)
+        experts(len(CHUNKS) - 1, 128, 128, nc.vector.tensor_copy)
+
+        t0 = 0
+        for h, n in enumerate(TOKEN_PARTS):
+            cols = slice(t0 // 16, (t0 + n) // 16)
+            first = keep.tile([P, n], F32, name="first%d" % h)
+            nc.vector.tensor_copy(first[:], dx[:].indirect(pos_t[0][:, cols]))
+            second = keep.tile([P, n], F32, name="second%d" % h)
+            nc.vector.tensor_tensor(second[:], dx[:].indirect(pos_t[1][:, cols]), first[:], ALU.add)
+            third = keep.tile([P, n], F32, name="third%d" % h)
+            nc.vector.tensor_tensor(third[:], dx[:].indirect(pos_t[2][:, cols]), second[:], ALU.add)
+            nc.sync.dma_start(out[:, t0 : t0 + n], third[:])
+            t0 = t0 + n

@@ -19,7 +19,7 @@ FP4X4 = mybir.dt.float4_e2m1fn_x4
 ALU = mybir.AluOpType
 ACT = mybir.ActivationFunctionType
 
-CHUNKS = [512, 512, 512, 512, 256]
+CHUNKS = [256, 512, 512, 512, 512]
 TOKEN_PARTS = [384, 384]
 
 
@@ -38,8 +38,6 @@ def tile_moe_sdb_relu_kernel(
         w2_plane_raw = keep.tile([P, H], U8, align_bytes=64)
         dy_plane = keep.tile([P, T], U8, align_bytes=64)
         w1_plane = keep.tile([P, E * K], U8, align_bytes=64)
-        nc.vector.memset(w2_plane_raw[:].bitcast(I32), 0)
-        nc.gpsimd.memset(dy_plane[:].bitcast(I32), 0)
 
         nc.vector.memset(w1_plane[:].bitcast(I32), 0)
         warm = keep.tile([P, 8], F32)
@@ -47,17 +45,19 @@ def tile_moe_sdb_relu_kernel(
         warm_out = keep.tile([P, 8], BF16)
         nc.scalar.activation(warm_out[:], warm[:], ACT.Sign)
 
+        for q in range(4):
+            nc.sync.dma_start(
+                w2_plane_raw[32 * q : 32 * q + 32, :].bitcast(I32),
+                w2t_scales[0, 4 * q : 4 * q + 4, :].bitcast(I32).partition_broadcast(8),
+            )
         w2_raw = keep.tile([P, 2 * H], U8, align_bytes=64)
         nc.sync.dma_start(w2_raw[:].bitcast(I32), w2t_words[0].bitcast(I32))
         dy_codes = keep.tile([P, 4 * T], U8, align_bytes=64)
         nc.sync.dma_start(dy_codes[:].bitcast(I32), dy_words[0].rearrange("p t d -> p (t d)").bitcast(I32))
         for q in range(4):
             nc.sync.dma_start(
-                w2_plane_raw[32 * q : 32 * q + 4, :].bitcast(I32), w2t_scales[0, 4 * q : 4 * q + 4, :].bitcast(I32)
-            )
-        for q in range(4):
-            (nc.sync if q < 2 else nc.gpsimd).dma_start(
-                dy_plane[32 * q : 32 * q + 4, :].bitcast(I32), dy_scales[0, 4 * q : 4 * q + 4, :].bitcast(I32)
+                dy_plane[32 * q : 32 * q + 32, :].bitcast(I32),
+                dy_scales[0, 4 * q : 4 * q + 4, :].bitcast(I32).partition_broadcast(8),
             )
         offs_t = keep.tile([P, S // 16], U16)
         nc.sync.dma_start(offs_t[:], offs)
@@ -70,7 +70,7 @@ def tile_moe_sdb_relu_kernel(
             nc.sync.dma_start(g_t[c][:], gate[:, s0 : s0 + n])
             a_t.append(keep.tile([P, PACK, n], F32, name="a%d" % c))
             nc.sync.dma_start(a_t[c][:], a_rows[:, :, s0 : s0 + n])
-            if c == 0:
+            if c == 1:
                 w1_codes = keep.tile([P, E, 2 * K], U8, align_bytes=64)
                 nc.sync.dma_start(
                     w1_codes[:].bitcast(I32), w1t_words[:, 0].rearrange("e p b -> p e b").bitcast(I32)
@@ -119,28 +119,40 @@ def tile_moe_sdb_relu_kernel(
         dx = keep.tile([P, S], F32)
         steps = {}
         woven = {}
+        gathered = {}
 
-        def make_mask(c):
+        def signs(c):
             n = CHUNKS[c]
-            steps[c] = keep.tile([P, PACK * n], BF16, name="mask%d" % c, align_bytes=64)
-            nc.scalar.activation(
-                steps[c][:].rearrange("p (u i t) -> p u t i", i=4, t=PACK),
-                a_t[c][:].rearrange("p t (u i) -> p u t i", i=4),
-                ACT.Sign,
-            )
-            nc.vector.tensor_scalar_max(steps[c][:], steps[c][:], 0.0)
+            steps[c] = keep.tile([P, PACK * n], BF16, name="mask%d" % c, tag="shared%d" % (c + 2), align_bytes=64)
+            woven_out = steps[c][:].rearrange("p (u i t) -> p u t i", i=4, t=PACK)
+            planes_in = a_t[c][:].rearrange("p t (u i) -> p u t i", i=4)
+            if c == 0:
+                nc.vector.tensor_single_scalar(woven_out, planes_in, 0.0, ALU.is_gt)
+            else:
+                nc.scalar.activation(woven_out, planes_in, ACT.Sign)
+
+        def clip(c):
+            if c == 3:
+                nc.scalar.activation(steps[c][:], steps[c][:], ACT.Relu)
+            else:
+                nc.vector.tensor_scalar_max(steps[c][:], steps[c][:], 0.0)
 
         def gather(c):
             s0, n = starts[c], CHUNKS[c]
-            gd = ring.tile([P, PACK, n], F32, name="gd")
+            gd = keep.tile([P, PACK * n], F32, name="gd%d" % c, tag="shared%d" % c, align_bytes=64)
             for t in range(PACK):
                 nc.vector.tensor_tensor(
-                    gd[:, t, :], dc[t][:].indirect(offs_t[:, s0 // 16 : (s0 + n) // 16]), g_t[c][:], ALU.mult
+                    gd[:, t * n : (t + 1) * n], dc[t][:].indirect(offs_t[:, s0 // 16 : (s0 + n) // 16]), g_t[c][:], ALU.mult
                 )
-            woven[c] = ring.tile([P, PACK * n], BF16, name="woven", align_bytes=64)
+            gathered[c] = gd
+            woven[c] = keep.tile([P, PACK * n], BF16, name="woven%d" % c, align_bytes=64)
+
+        def weave(c, v0, n):
             nc.scalar.copy(
-                woven[c][:].rearrange("p (u i t) -> p u t i", i=4, t=PACK),
-                gd[:].rearrange("p t (u i) -> p u t i", i=4),
+                woven[c][:, PACK * v0 : PACK * (v0 + n)].rearrange("p (u i t) -> p u t i", i=4, t=PACK),
+                gathered[c][:].rearrange("p (t s) -> p t s", t=PACK)[:, :, v0 : v0 + n].rearrange(
+                    "p t (u i) -> p u t i", i=4
+                ),
             )
 
         def experts(c, v0, n, empty):
@@ -166,13 +178,22 @@ def tile_moe_sdb_relu_kernel(
                 )
             empty(dx[:, s0 : s0 + n], acc[:])
 
-        for c in range(len(CHUNKS)):
+        last = len(CHUNKS) - 1
+        signs(0)
+        for c in range(last):
             gather(c)
+            signs(c + 1)
+            weave(c, 0, CHUNKS[c])
+            clip(c + 1)
             if c > 0:
                 experts(c - 1, 0, CHUNKS[c - 1], nc.scalar.copy)
-            make_mask(c)
-        experts(len(CHUNKS) - 1, 0, 128, nc.scalar.copy)
-        experts(len(CHUNKS) - 1, 128, 128, nc.vector.tensor_copy)
+        gather(last)
+        weave(last, 0, 256)
+        weave(last, 256, 256)
+        experts(last - 1, 0, CHUNKS[last - 1], nc.scalar.copy)
+        experts(last, 0, 256, nc.scalar.copy)
+        experts(last, 256, 128, nc.scalar.copy)
+        experts(last, 384, 128, nc.vector.tensor_copy)
 
         t0 = 0
         for h, n in enumerate(TOKEN_PARTS):

@@ -6,6 +6,9 @@ K, T, E, C, H, N = 128, 768, 9, 256, 512, 512
 S = E * C
 P = 128
 PACK = 4
+QUADRANTS = 4
+RUN = 4
+LIST_ROWS = 16
 FLOPS = 2 * N * H * T + 2 * H * K * S
 
 F32 = mybir.dt.float32
@@ -20,7 +23,11 @@ ALU = mybir.AluOpType
 ACT = mybir.ActivationFunctionType
 
 CHUNKS = [256, 512, 512, 512, 512]
-TOKEN_PARTS = [384, 384]
+TOKEN_BANKS = [(0, 512), (512, 256)]
+SCALAR_CLIPS = 3
+LAST_WEAVES = [(0, 256), (256, 256)]
+LAST_EXPERT_PIECES = [(0, 256), (256, 128), (384, 128)]
+TOKEN_HALF = T // 2
 
 
 def tile_moe_sdb_relu_kernel(
@@ -28,6 +35,7 @@ def tile_moe_sdb_relu_kernel(
 ):
     nc = tc.nc
     starts = [sum(CHUNKS[:c]) for c in range(len(CHUNKS))]
+    last = len(CHUNKS) - 1
 
     with ExitStack() as ctx:
         keep = ctx.enter_context(tc.tile_pool(name="keep", bufs=1))
@@ -38,28 +46,24 @@ def tile_moe_sdb_relu_kernel(
         w2_plane_raw = keep.tile([P, H], U8, align_bytes=64)
         dy_plane = keep.tile([P, T], U8, align_bytes=64)
         w1_plane = keep.tile([P, E * K], U8, align_bytes=64)
-
+        nc.gpsimd.memset(w2_plane_raw[:].bitcast(I32), 0)
+        nc.gpsimd.memset(dy_plane[:].bitcast(I32), 0)
         nc.vector.memset(w1_plane[:].bitcast(I32), 0)
         warm = keep.tile([P, 8], F32)
         nc.vector.memset(warm[:], 0.0)
         warm_out = keep.tile([P, 8], BF16)
         nc.scalar.activation(warm_out[:], warm[:], ACT.Sign)
 
-        for q in range(4):
-            nc.sync.dma_start(
-                w2_plane_raw[32 * q : 32 * q + 32, :].bitcast(I32),
-                w2t_scales[0, 4 * q : 4 * q + 4, :].bitcast(I32).partition_broadcast(8),
-            )
         w2_raw = keep.tile([P, 2 * H], U8, align_bytes=64)
         nc.sync.dma_start(w2_raw[:].bitcast(I32), w2t_words[0].bitcast(I32))
         dy_codes = keep.tile([P, 4 * T], U8, align_bytes=64)
         nc.sync.dma_start(dy_codes[:].bitcast(I32), dy_words[0].rearrange("p t d -> p (t d)").bitcast(I32))
-        for q in range(4):
-            nc.sync.dma_start(
-                dy_plane[32 * q : 32 * q + 32, :].bitcast(I32),
-                dy_scales[0, 4 * q : 4 * q + 4, :].bitcast(I32).partition_broadcast(8),
-            )
-        offs_t = keep.tile([P, S // 16], U16)
+        for plane_in, scales in ((w2_plane_raw, w2t_scales), (dy_plane, dy_scales)):
+            for q in range(QUADRANTS):
+                nc.sync.dma_start(
+                    plane_in[32 * q : 32 * q + 4, :].bitcast(I32), scales[0, 4 * q : 4 * q + 4, :].bitcast(I32)
+                )
+        offs_t = keep.tile([P, S // LIST_ROWS], U16)
         nc.sync.dma_start(offs_t[:], offs)
 
         a_rows = a.rearrange("(p t) s -> p t s", t=PACK)
@@ -75,14 +79,14 @@ def tile_moe_sdb_relu_kernel(
                 nc.sync.dma_start(
                     w1_codes[:].bitcast(I32), w1t_words[:, 0].rearrange("e p b -> p e b").bitcast(I32)
                 )
-                for q in range(4):
+                for q in range(QUADRANTS):
                     nc.sync.dma_start(
                         w1_plane[32 * q : 32 * q + 4, :].rearrange("r (e k) -> r e k", e=E).bitcast(I32),
                         w1t_scales[:, 0, 4 * q : 4 * q + 4, :].rearrange("e r k -> r e k").bitcast(I32),
                     )
         pos_t = []
         for r, pos in enumerate((pos1, pos2, pos3)):
-            pos_t.append(keep.tile([P, T // 16], U16, name="pos%d" % r))
+            pos_t.append(keep.tile([P, T // LIST_ROWS], U16, name="pos%d" % r))
             nc.sync.dma_start(pos_t[r][:], pos)
 
         w2_codes = keep.tile([P, 2 * H], U8, align_bytes=64)
@@ -100,7 +104,7 @@ def tile_moe_sdb_relu_kernel(
         dc = []
         for t in range(PACK):
             dc.append(keep.tile([P, T], F32, name="dc%d" % t))
-            for t0, n in ((0, 512), (512, 256)):
+            for t0, n in TOKEN_BANKS:
                 acc = psum.tile([P, n], F32, name="dc_acc%d" % n)
                 nc.tensor.matmul_mx(
                     out=acc[:],
@@ -117,41 +121,41 @@ def tile_moe_sdb_relu_kernel(
                     nc.scalar.copy(dc[t][:, t0 : t0 + n], acc[:])
 
         dx = keep.tile([P, S], F32)
-        steps = {}
+        mask = {}
         woven = {}
         gathered = {}
 
         def signs(c):
             n = CHUNKS[c]
-            steps[c] = keep.tile([P, PACK * n], BF16, name="mask%d" % c, tag="shared%d" % (c + 2), align_bytes=64)
-            woven_out = steps[c][:].rearrange("p (u i t) -> p u t i", i=4, t=PACK)
-            planes_in = a_t[c][:].rearrange("p t (u i) -> p u t i", i=4)
+            mask[c] = keep.tile([P, PACK * n], BF16, name="mask%d" % c, tag="shared%d" % (c + 2), align_bytes=64)
+            mask_out = mask[c][:].rearrange("p (u i t) -> p u t i", i=RUN, t=PACK)
+            a_in = a_t[c][:].rearrange("p t (u i) -> p u t i", i=RUN)
             if c == 0:
-                nc.vector.tensor_single_scalar(woven_out, planes_in, 0.0, ALU.is_gt)
+                nc.vector.tensor_single_scalar(mask_out, a_in, 0.0, ALU.is_gt)
             else:
-                nc.scalar.activation(woven_out, planes_in, ACT.Sign)
+                nc.scalar.activation(mask_out, a_in, ACT.Sign)
 
         def clip(c):
-            if c == 3:
-                nc.scalar.activation(steps[c][:], steps[c][:], ACT.Relu)
+            if c == SCALAR_CLIPS:
+                nc.scalar.activation(mask[c][:], mask[c][:], ACT.Relu)
             else:
-                nc.vector.tensor_scalar_max(steps[c][:], steps[c][:], 0.0)
+                nc.vector.tensor_scalar_max(mask[c][:], mask[c][:], 0.0)
 
         def gather(c):
             s0, n = starts[c], CHUNKS[c]
-            gd = keep.tile([P, PACK * n], F32, name="gd%d" % c, tag="shared%d" % c, align_bytes=64)
+            gathered[c] = keep.tile([P, PACK * n], F32, name="gd%d" % c, tag="shared%d" % c, align_bytes=64)
+            tokens = offs_t[:, s0 // LIST_ROWS : (s0 + n) // LIST_ROWS]
             for t in range(PACK):
                 nc.vector.tensor_tensor(
-                    gd[:, t * n : (t + 1) * n], dc[t][:].indirect(offs_t[:, s0 // 16 : (s0 + n) // 16]), g_t[c][:], ALU.mult
+                    gathered[c][:, t * n : (t + 1) * n], dc[t][:].indirect(tokens), g_t[c][:], ALU.mult
                 )
-            gathered[c] = gd
             woven[c] = keep.tile([P, PACK * n], BF16, name="woven%d" % c, align_bytes=64)
 
         def weave(c, v0, n):
             nc.scalar.copy(
-                woven[c][:, PACK * v0 : PACK * (v0 + n)].rearrange("p (u i t) -> p u t i", i=4, t=PACK),
+                woven[c][:, PACK * v0 : PACK * (v0 + n)].rearrange("p (u i t) -> p u t i", i=RUN, t=PACK),
                 gathered[c][:].rearrange("p (t s) -> p t s", t=PACK)[:, :, v0 : v0 + n].rearrange(
-                    "p t (u i) -> p u t i", i=4
+                    "p t (u i) -> p u t i", i=RUN
                 ),
             )
 
@@ -159,7 +163,7 @@ def tile_moe_sdb_relu_kernel(
             s0 = starts[c] + v0
             cols = slice(PACK * v0, PACK * (v0 + n))
             da = ring.tile([P, PACK * n], BF16, name="da", align_bytes=64)
-            nc.vector.tensor_tensor(da[:], woven[c][:, cols], steps[c][:, cols], ALU.mult)
+            nc.vector.tensor_tensor(da[:], woven[c][:, cols], mask[c][:, cols], ALU.mult)
             codes = ring.tile([P, n], U32, name="codes", align_bytes=64)
             plane = ring.tile([P, n], U8, name="plane", align_bytes=64)
             nc.vector.quantize_mx(out=codes[:].bitcast(FP8X4), scales=plane[:], in_=da[:])
@@ -178,7 +182,6 @@ def tile_moe_sdb_relu_kernel(
                 )
             empty(dx[:, s0 : s0 + n], acc[:])
 
-        last = len(CHUNKS) - 1
         signs(0)
         for c in range(last):
             gather(c)
@@ -188,21 +191,18 @@ def tile_moe_sdb_relu_kernel(
             if c > 0:
                 experts(c - 1, 0, CHUNKS[c - 1], nc.scalar.copy)
         gather(last)
-        weave(last, 0, 256)
-        weave(last, 256, 256)
+        for v0, n in LAST_WEAVES:
+            weave(last, v0, n)
         experts(last - 1, 0, CHUNKS[last - 1], nc.scalar.copy)
-        experts(last, 0, 256, nc.scalar.copy)
-        experts(last, 256, 128, nc.scalar.copy)
-        experts(last, 384, 128, nc.vector.tensor_copy)
+        for v0, n in LAST_EXPERT_PIECES:
+            experts(last, v0, n, nc.vector.tensor_copy if v0 + n == CHUNKS[last] else nc.scalar.copy)
 
-        t0 = 0
-        for h, n in enumerate(TOKEN_PARTS):
-            cols = slice(t0 // 16, (t0 + n) // 16)
-            first = keep.tile([P, n], F32, name="first%d" % h)
+        for h, t0 in enumerate(range(0, T, TOKEN_HALF)):
+            cols = slice(t0 // LIST_ROWS, (t0 + TOKEN_HALF) // LIST_ROWS)
+            first = keep.tile([P, TOKEN_HALF], F32, name="first%d" % h)
             nc.vector.tensor_copy(first[:], dx[:].indirect(pos_t[0][:, cols]))
-            second = keep.tile([P, n], F32, name="second%d" % h)
+            second = keep.tile([P, TOKEN_HALF], F32, name="second%d" % h)
             nc.vector.tensor_tensor(second[:], dx[:].indirect(pos_t[1][:, cols]), first[:], ALU.add)
-            third = keep.tile([P, n], F32, name="third%d" % h)
+            third = keep.tile([P, TOKEN_HALF], F32, name="third%d" % h)
             nc.vector.tensor_tensor(third[:], dx[:].indirect(pos_t[2][:, cols]), second[:], ALU.add)
-            nc.sync.dma_start(out[:, t0 : t0 + n], third[:])
-            t0 = t0 + n
+            nc.sync.dma_start(out[:, t0 : t0 + TOKEN_HALF], third[:])

@@ -22,11 +22,12 @@ FP4X4 = mybir.dt.float4_e2m1fn_x4
 ALU = mybir.AluOpType
 ACT = mybir.ActivationFunctionType
 
-CHUNKS = [256, 512, 512, 512, 512]
+CHUNK = 768
+CHUNKS = S // CHUNK
+WINDOW = T + 32
 TOKEN_BANKS = [(0, 512), (512, 256)]
-SCALAR_CLIPS = 3
-LAST_WEAVES = [(0, 256), (256, 256)]
-LAST_EXPERT_PIECES = [(0, 256), (256, 128), (384, 128)]
+PIECES = [(0, 512), (512, 256)]
+LAST_PIECES = [(0, 256), (256, 256), (512, 256)]
 TOKEN_HALF = T // 2
 
 
@@ -34,56 +35,64 @@ def tile_moe_sdb_relu_kernel(
     tc, dy_words, dy_scales, w2t_words, w2t_scales, w1t_words, w1t_scales, a, gate, offs, pos1, pos2, pos3, out
 ):
     nc = tc.nc
-    starts = [sum(CHUNKS[:c]) for c in range(len(CHUNKS))]
-    last = len(CHUNKS) - 1
+    last = CHUNKS - 1
 
     with ExitStack() as ctx:
         keep = ctx.enter_context(tc.tile_pool(name="keep", bufs=1))
-        ring = ctx.enter_context(tc.tile_pool(name="ring", bufs=2))
-        psum = ctx.enter_context(tc.psum_pool(name="psum", bufs=3))
-        psum_dx = ctx.enter_context(tc.psum_pool(name="psum_dx", bufs=2))
+        psum = ctx.enter_context(tc.psum_pool(name="psum", bufs=8))
 
         w2_plane_raw = keep.tile([P, H], U8, align_bytes=64)
         dy_plane = keep.tile([P, T], U8, align_bytes=64)
         w1_plane = keep.tile([P, E * K], U8, align_bytes=64)
-        nc.gpsimd.memset(w2_plane_raw[:].bitcast(I32), 0)
-        nc.gpsimd.memset(dy_plane[:].bitcast(I32), 0)
+        nc.vector.memset(w2_plane_raw[:].bitcast(I32), 0)
+        nc.vector.memset(dy_plane[:].bitcast(I32), 0)
         nc.vector.memset(w1_plane[:].bitcast(I32), 0)
-        warm = keep.tile([P, 8], F32)
-        nc.vector.memset(warm[:], 0.0)
-        warm_out = keep.tile([P, 8], BF16)
-        nc.scalar.activation(warm_out[:], warm[:], ACT.Sign)
+        dc = []
+        for t in range(PACK):
+            dc.append(keep.tile([P, WINDOW], F32, name="dc%d" % t))
+            nc.gpsimd.memset(dc[t][:, T:], 0.0)
+
+        def load_scale_rows(plane_in, scales, q):
+            nc.sync.dma_start(
+                plane_in[32 * q : 32 * q + 4, :].bitcast(I32), scales[0, 4 * q : 4 * q + 4, :].bitcast(I32)
+            )
 
         w2_raw = keep.tile([P, 2 * H], U8, align_bytes=64)
         nc.sync.dma_start(w2_raw[:].bitcast(I32), w2t_words[0].bitcast(I32))
+        for q in range(QUADRANTS):
+            load_scale_rows(w2_plane_raw, w2t_scales, q)
         dy_codes = keep.tile([P, 4 * T], U8, align_bytes=64)
         nc.sync.dma_start(dy_codes[:].bitcast(I32), dy_words[0].rearrange("p t d -> p (t d)").bitcast(I32))
-        for plane_in, scales in ((w2_plane_raw, w2t_scales), (dy_plane, dy_scales)):
-            for q in range(QUADRANTS):
-                nc.sync.dma_start(
-                    plane_in[32 * q : 32 * q + 4, :].bitcast(I32), scales[0, 4 * q : 4 * q + 4, :].bitcast(I32)
-                )
+        for q in range(QUADRANTS):
+            load_scale_rows(dy_plane, dy_scales, q)
         offs_t = keep.tile([P, S // LIST_ROWS], U16)
         nc.sync.dma_start(offs_t[:], offs)
 
         a_rows = a.rearrange("(p t) s -> p t s", t=PACK)
-        a_t = []
-        g_t = []
-        for c, (s0, n) in enumerate(zip(starts, CHUNKS)):
-            g_t.append(keep.tile([P, n], F32, name="gate%d" % c))
-            nc.sync.dma_start(g_t[c][:], gate[:, s0 : s0 + n])
-            a_t.append(keep.tile([P, PACK, n], F32, name="a%d" % c))
-            nc.sync.dma_start(a_t[c][:], a_rows[:, :, s0 : s0 + n])
-            if c == 1:
-                w1_codes = keep.tile([P, E, 2 * K], U8, align_bytes=64)
-                nc.sync.dma_start(
-                    w1_codes[:].bitcast(I32), w1t_words[:, 0].rearrange("e p b -> p e b").bitcast(I32)
-                )
-                for q in range(QUADRANTS):
-                    nc.sync.dma_start(
-                        w1_plane[32 * q : 32 * q + 4, :].rearrange("r (e k) -> r e k", e=E).bitcast(I32),
-                        w1t_scales[:, 0, 4 * q : 4 * q + 4, :].rearrange("e r k -> r e k").bitcast(I32),
-                    )
+        g_t = [keep.tile([P, CHUNK], F32, name="gate%d" % c) for c in range(CHUNKS)]
+        a_t = [keep.tile([P, PACK * CHUNK], F32, name="a%d" % c, tag="a%d" % c, align_bytes=64) for c in range(CHUNKS)]
+
+        def load_gate(c):
+            nc.sync.dma_start(g_t[c][:], gate[:, c * CHUNK : (c + 1) * CHUNK])
+
+        def load_a(c):
+            nc.sync.dma_start(
+                a_t[c][:].rearrange("p (t s) -> p t s", t=PACK), a_rows[:, :, c * CHUNK : (c + 1) * CHUNK]
+            )
+
+        load_gate(0)
+        load_a(0)
+        for c in range(1, CHUNKS):
+            load_gate(c)
+        for c in range(1, CHUNKS):
+            load_a(c)
+        w1_codes = keep.tile([P, E, 2 * K], U8, align_bytes=64)
+        nc.sync.dma_start(w1_codes[:].bitcast(I32), w1t_words[:, 0].rearrange("e p b -> p e b").bitcast(I32))
+        for q in range(QUADRANTS):
+            nc.sync.dma_start(
+                w1_plane[32 * q : 32 * q + 4, :].rearrange("r (e k) -> r e k", e=E).bitcast(I32),
+                w1t_scales[:, 0, 4 * q : 4 * q + 4, :].rearrange("e r k -> r e k").bitcast(I32),
+            )
         pos_t = []
         for r, pos in enumerate((pos1, pos2, pos3)):
             pos_t.append(keep.tile([P, T // LIST_ROWS], U16, name="pos%d" % r))
@@ -101,13 +110,11 @@ def tile_moe_sdb_relu_kernel(
                 w2_plane_raw[:].rearrange("p (m t) -> p t m", t=PACK)[:, ts, :],
             )
 
-        dc = []
         for t in range(PACK):
-            dc.append(keep.tile([P, T], F32, name="dc%d" % t))
             for t0, n in TOKEN_BANKS:
-                acc = psum.tile([P, n], F32, name="dc_acc%d" % n)
+                acc = psum.tile([P, 512], F32, name="acc")
                 nc.tensor.matmul_mx(
-                    out=acc[:],
+                    out=acc[:, :n],
                     lhsT=w2_codes[:, 2 * P * t : 2 * P * (t + 1)].bitcast(FP4X4),
                     lhsT_scale=w2_plane[:, P * t : P * (t + 1)],
                     rhs=dy_codes[:, 4 * t0 : 4 * (t0 + n)].bitcast(FP8X4),
@@ -116,86 +123,70 @@ def tile_moe_sdb_relu_kernel(
                     stop=True,
                 )
                 if t == 0 and t0 > 0:
-                    nc.vector.tensor_copy(dc[t][:, t0 : t0 + n], acc[:])
+                    nc.vector.tensor_copy(dc[t][:, t0 : t0 + n], acc[:, :n])
                 else:
-                    nc.scalar.copy(dc[t][:, t0 : t0 + n], acc[:])
+                    nc.scalar.copy(dc[t][:, t0 : t0 + n], acc[:, :n])
 
-        dx = keep.tile([P, S], F32)
-        mask = {}
-        woven = {}
-        gathered = {}
-
-        def signs(c):
-            n = CHUNKS[c]
-            mask[c] = keep.tile([P, PACK * n], BF16, name="mask%d" % c, tag="shared%d" % (c + 2), align_bytes=64)
-            mask_out = mask[c][:].rearrange("p (u i t) -> p u t i", i=RUN, t=PACK)
-            a_in = a_t[c][:].rearrange("p t (u i) -> p u t i", i=RUN)
-            if c == 0:
-                nc.vector.tensor_single_scalar(mask_out, a_in, 0.0, ALU.is_gt)
-            else:
-                nc.scalar.activation(mask_out, a_in, ACT.Sign)
-
-        def clip(c):
-            if c == SCALAR_CLIPS:
-                nc.scalar.activation(mask[c][:], mask[c][:], ACT.Relu)
-            else:
-                nc.vector.tensor_scalar_max(mask[c][:], mask[c][:], 0.0)
-
-        def gather(c):
-            s0, n = starts[c], CHUNKS[c]
-            gathered[c] = keep.tile([P, PACK * n], F32, name="gd%d" % c, tag="shared%d" % c, align_bytes=64)
-            tokens = offs_t[:, s0 // LIST_ROWS : (s0 + n) // LIST_ROWS]
+        gathered = []
+        for c in range(CHUNKS):
+            gathered.append(keep.tile([P, PACK * CHUNK], F32, name="gd%d" % c, tag="gd%d" % c, align_bytes=64))
+            tokens = offs_t[:, c * CHUNK // LIST_ROWS : (c + 1) * CHUNK // LIST_ROWS]
             for t in range(PACK):
                 nc.vector.tensor_tensor(
-                    gathered[c][:, t * n : (t + 1) * n], dc[t][:].indirect(tokens), g_t[c][:], ALU.mult
+                    gathered[c][:, t * CHUNK : (t + 1) * CHUNK], dc[t][:].indirect(tokens), g_t[c][:], ALU.mult
                 )
-            woven[c] = keep.tile([P, PACK * n], BF16, name="woven%d" % c, align_bytes=64)
 
-        def weave(c, v0, n):
-            nc.scalar.copy(
-                woven[c][:, PACK * v0 : PACK * (v0 + n)].rearrange("p (u i t) -> p u t i", i=RUN, t=PACK),
-                gathered[c][:].rearrange("p (t s) -> p t s", t=PACK)[:, :, v0 : v0 + n].rearrange(
-                    "p t (u i) -> p u t i", i=RUN
-                ),
-            )
+        def woven_view(tile):
+            return tile[:].rearrange("p (u i t) -> p u t i", i=RUN, t=PACK)
 
-        def experts(c, v0, n, empty):
-            s0 = starts[c] + v0
-            cols = slice(PACK * v0, PACK * (v0 + n))
-            da = ring.tile([P, PACK * n], BF16, name="da", align_bytes=64)
-            nc.vector.tensor_tensor(da[:], woven[c][:, cols], mask[c][:, cols], ALU.mult)
-            codes = ring.tile([P, n], U32, name="codes", align_bytes=64)
-            plane = ring.tile([P, n], U8, name="plane", align_bytes=64)
-            nc.vector.quantize_mx(out=codes[:].bitcast(FP8X4), scales=plane[:], in_=da[:])
-            acc = psum_dx.tile([P, n], F32, name="dx_acc")
-            width = min(n, C)
-            for u0 in range(0, n, width):
-                e = (s0 + u0) // C
-                nc.tensor.matmul_mx(
-                    out=acc[:, u0 : u0 + width],
-                    lhsT=w1_codes[:, e, :].bitcast(FP4X4),
-                    lhsT_scale=w1_plane[:, K * e : K * (e + 1)],
-                    rhs=codes[:, u0 : u0 + width].bitcast(FP8X4),
-                    rhs_scale=plane[:, u0 : u0 + width],
-                    start=True,
-                    stop=True,
-                )
-            empty(dx[:, s0 : s0 + n], acc[:])
+        def planar_view(tile):
+            return tile[:].rearrange("p (t u i) -> p u t i", i=RUN, t=PACK)
 
-        signs(0)
+        mask = []
+        for c in range(CHUNKS):
+            mask.append(keep.tile([P, PACK * CHUNK], BF16, name="mask%d" % c, tag="mask%d" % c, align_bytes=64))
+            nc.scalar.activation(woven_view(mask[c]), planar_view(a_t[c]), ACT.Sign)
+
+        woven = []
+        for c in range(CHUNKS):
+            if c == last:
+                signs = mask[c]
+                mask[c] = keep.tile([P, PACK * CHUNK], BF16, name="clipped", tag="gd%d" % (c - 1), align_bytes=64)
+                nc.scalar.activation(mask[c][:], signs[:], ACT.Relu)
+                woven.append(keep.tile([P, PACK * CHUNK], BF16, name="woven_last", tag="mask%d" % c, align_bytes=64))
+            else:
+                woven.append(keep.tile([P, PACK * CHUNK], BF16, name="woven%d" % c, tag="a%d" % (c + 1), align_bytes=64))
+            nc.scalar.copy(woven_view(woven[c]), planar_view(gathered[c]))
         for c in range(last):
-            gather(c)
-            signs(c + 1)
-            weave(c, 0, CHUNKS[c])
-            clip(c + 1)
-            if c > 0:
-                experts(c - 1, 0, CHUNKS[c - 1], nc.scalar.copy)
-        gather(last)
-        for v0, n in LAST_WEAVES:
-            weave(last, v0, n)
-        experts(last - 1, 0, CHUNKS[last - 1], nc.scalar.copy)
-        for v0, n in LAST_EXPERT_PIECES:
-            experts(last, v0, n, nc.vector.tensor_copy if v0 + n == CHUNKS[last] else nc.scalar.copy)
+            nc.vector.tensor_scalar_max(mask[c][:], mask[c][:], 0.0)
+
+        dx = keep.tile([P, S], F32, name="dx", tag="gd%d" % last, align_bytes=64)
+        for c in range(CHUNKS):
+            da = keep.tile([P, PACK * CHUNK], BF16, name="da%d" % c, align_bytes=64)
+            nc.vector.tensor_tensor(da[:], woven[c][:], mask[c][:], ALU.mult)
+            for v0, n in LAST_PIECES if c == last else PIECES:
+                s0 = c * CHUNK + v0
+                codes = keep.tile([P, n], U32, name="codes%d" % s0, align_bytes=64)
+                plane = keep.tile([P, n], U8, name="plane%d" % s0, align_bytes=64)
+                nc.vector.quantize_mx(
+                    out=codes[:].bitcast(FP8X4), scales=plane[:], in_=da[:, PACK * v0 : PACK * (v0 + n)]
+                )
+                acc = psum.tile([P, 512], F32, name="acc")
+                for u0 in range(0, n, C):
+                    e = (s0 + u0) // C
+                    nc.tensor.matmul_mx(
+                        out=acc[:, u0 : u0 + C],
+                        lhsT=w1_codes[:, e, :].bitcast(FP4X4),
+                        lhsT_scale=w1_plane[:, K * e : K * (e + 1)],
+                        rhs=codes[:, u0 : u0 + C].bitcast(FP8X4),
+                        rhs_scale=plane[:, u0 : u0 + C],
+                        start=True,
+                        stop=True,
+                    )
+                if s0 + n == S:
+                    nc.vector.tensor_copy(dx[:, s0 : s0 + n], acc[:, :n])
+                else:
+                    nc.scalar.copy(dx[:, s0 : s0 + n], acc[:, :n])
 
         for h, t0 in enumerate(range(0, T, TOKEN_HALF)):
             cols = slice(t0 // LIST_ROWS, (t0 + TOKEN_HALF) // LIST_ROWS)

@@ -1,6 +1,7 @@
 from contextlib import ExitStack
 
 import concourse.mybir as mybir
+from concourse.masks import make_identity
 
 K, T, E, C, H, N = 128, 768, 9, 256, 512, 512
 S = E * C
@@ -22,12 +23,11 @@ FP4X4 = mybir.dt.float4_e2m1fn_x4
 ALU = mybir.AluOpType
 ACT = mybir.ActivationFunctionType
 
-CHUNK = 768
-CHUNKS = S // CHUNK
-WINDOW = T + 32
+SIZES = [768, 1024, 512]
+STARTS = [0, 768, 1792]
+WINDOW = 1024 + 32
 TOKEN_BANKS = [(0, 512), (512, 256)]
-PIECES = [(0, 512), (512, 256)]
-LAST_PIECES = [(0, 256), (256, 256), (512, 256)]
+BLOCKS = SIZES[1] // P
 TOKEN_HALF = T // 2
 
 
@@ -35,11 +35,12 @@ def tile_moe_sdb_relu_kernel(
     tc, dy_words, dy_scales, w2t_words, w2t_scales, w1t_words, w1t_scales, a, gate, offs, pos1, pos2, pos3, out
 ):
     nc = tc.nc
-    last = CHUNKS - 1
 
     with ExitStack() as ctx:
         keep = ctx.enter_context(tc.tile_pool(name="keep", bufs=1))
-        psum = ctx.enter_context(tc.psum_pool(name="psum", bufs=8))
+        placed = ctx.enter_context(tc.tile_pool(name="placed", bufs=1))
+        psum = ctx.enter_context(tc.psum_pool(name="psum", bufs=4))
+        psum_back = ctx.enter_context(tc.psum_pool(name="psum_back", bufs=4))
 
         w2_plane_raw = keep.tile([P, H], U8, align_bytes=64)
         dy_plane = keep.tile([P, T], U8, align_bytes=64)
@@ -47,6 +48,8 @@ def tile_moe_sdb_relu_kernel(
         nc.vector.memset(w2_plane_raw[:].bitcast(I32), 0)
         nc.vector.memset(dy_plane[:].bitcast(I32), 0)
         nc.vector.memset(w1_plane[:].bitcast(I32), 0)
+        identity = keep.tile([P, P], F32)
+        make_identity(nc, identity[:])
         dc = []
         for t in range(PACK):
             dc.append(keep.tile([P, WINDOW], F32, name="dc%d" % t))
@@ -69,23 +72,23 @@ def tile_moe_sdb_relu_kernel(
         nc.sync.dma_start(offs_t[:], offs)
 
         a_rows = a.rearrange("(p t) s -> p t s", t=PACK)
-        g_t = [keep.tile([P, CHUNK], F32, name="gate%d" % c) for c in range(CHUNKS)]
-        a_t = [keep.tile([P, PACK * CHUNK], F32, name="a%d" % c, tag="a%d" % c, align_bytes=64) for c in range(CHUNKS)]
+        border = 4 * PACK * SIZES[1]
+        gate0 = placed.tile([P, SIZES[0]], F32, name="gate0", offset=border - 2 * SIZES[0], align_bytes=64)
+        gate2 = keep.tile([P, SIZES[2]], F32, name="gate2")
+        g_col = keep.tile([P, BLOCKS], F32, name="g_col", tag="g_col", align_bytes=64)
+        parts = [(0, 768), (768, 512), (1280, 512), (1792, 512)]
+        a_t = [keep.tile([P, PACK * n], F32, name="a%d" % j, tag="a%d" % j, align_bytes=64) for j, (s0, n) in enumerate(parts)]
 
-        def load_gate(c):
-            nc.sync.dma_start(g_t[c][:], gate[:, c * CHUNK : (c + 1) * CHUNK])
+        def load_a(j):
+            s0, n = parts[j]
+            nc.sync.dma_start(a_t[j][:].rearrange("p (t s) -> p t s", t=PACK), a_rows[:, :, s0 : s0 + n])
 
-        def load_a(c):
-            nc.sync.dma_start(
-                a_t[c][:].rearrange("p (t s) -> p t s", t=PACK), a_rows[:, :, c * CHUNK : (c + 1) * CHUNK]
-            )
-
-        load_gate(0)
-        load_a(0)
-        for c in range(1, CHUNKS):
-            load_gate(c)
-        for c in range(1, CHUNKS):
-            load_a(c)
+        nc.sync.dma_start(gate0[:], gate[:, : SIZES[0]])
+        for j in range(len(parts)):
+            load_a(j)
+        nc.sync.dma_start(gate2[:], gate[:, STARTS[2] :])
+        with nc.allow_non_contiguous_dma(reason="one gate a partition"):
+            nc.sync.dma_start(g_col[:], gate[0, STARTS[1] : STARTS[2]].rearrange("(b p) -> p b", p=P))
         w1_codes = keep.tile([P, E, 2 * K], U8, align_bytes=64)
         nc.sync.dma_start(w1_codes[:].bitcast(I32), w1t_words[:, 0].rearrange("e p b -> p e b").bitcast(I32))
         for q in range(QUADRANTS):
@@ -112,7 +115,10 @@ def tile_moe_sdb_relu_kernel(
 
         for t in range(PACK):
             for t0, n in TOKEN_BANKS:
-                acc = psum.tile([P, 512], F32, name="acc")
+                if n == 512:
+                    acc = psum.tile([P, 512], F32, name="acc")
+                else:
+                    acc = psum_back.tile([P, 512], F32, name="back")
                 nc.tensor.matmul_mx(
                     out=acc[:, :n],
                     lhsT=w2_codes[:, 2 * P * t : 2 * P * (t + 1)].bitcast(FP4X4),
@@ -128,13 +134,18 @@ def tile_moe_sdb_relu_kernel(
                     nc.scalar.copy(dc[t][:, t0 : t0 + n], acc[:, :n])
 
         gathered = []
-        for c in range(CHUNKS):
-            gathered.append(keep.tile([P, PACK * CHUNK], F32, name="gd%d" % c, tag="gd%d" % c, align_bytes=64))
-            tokens = offs_t[:, c * CHUNK // LIST_ROWS : (c + 1) * CHUNK // LIST_ROWS]
+        for c, (s0, n) in enumerate(zip(STARTS, SIZES)):
+            if c == 1:
+                gathered.append(placed.tile([P, PACK * n], F32, name="gd1", offset=0, align_bytes=64))
+            else:
+                gathered.append(keep.tile([P, PACK * n], F32, name="gd%d" % c, tag="gd%d" % c, align_bytes=64))
+            tokens = offs_t[:, s0 // LIST_ROWS : (s0 + n) // LIST_ROWS]
             for t in range(PACK):
-                nc.vector.tensor_tensor(
-                    gathered[c][:, t * CHUNK : (t + 1) * CHUNK], dc[t][:].indirect(tokens), g_t[c][:], ALU.mult
-                )
+                part = gathered[c][:, t * n : (t + 1) * n]
+                if c == 1:
+                    nc.vector.tensor_copy(part, dc[t][:].indirect(tokens))
+                else:
+                    nc.vector.tensor_tensor(part, dc[t][:].indirect(tokens), (gate0 if c == 0 else gate2)[:], ALU.mult)
 
         def woven_view(tile):
             return tile[:].rearrange("p (u i t) -> p u t i", i=RUN, t=PACK)
@@ -142,51 +153,98 @@ def tile_moe_sdb_relu_kernel(
         def planar_view(tile):
             return tile[:].rearrange("p (t u i) -> p u t i", i=RUN, t=PACK)
 
-        mask = []
-        for c in range(CHUNKS):
-            mask.append(keep.tile([P, PACK * CHUNK], BF16, name="mask%d" % c, tag="mask%d" % c, align_bytes=64))
-            nc.scalar.activation(woven_view(mask[c]), planar_view(a_t[c]), ACT.Sign)
+        def bf16_tile(name, tag, n):
+            return keep.tile([P, PACK * n], BF16, name=name, tag=tag, align_bytes=64)
 
-        woven = []
-        for c in range(CHUNKS):
-            if c == last:
-                signs = mask[c]
-                mask[c] = keep.tile([P, PACK * CHUNK], BF16, name="clipped", tag="gd%d" % (c - 1), align_bytes=64)
-                nc.scalar.activation(mask[c][:], signs[:], ACT.Relu)
-                woven.append(keep.tile([P, PACK * CHUNK], BF16, name="woven_last", tag="mask%d" % c, align_bytes=64))
-            else:
-                woven.append(keep.tile([P, PACK * CHUNK], BF16, name="woven%d" % c, tag="a%d" % (c + 1), align_bytes=64))
-            nc.scalar.copy(woven_view(woven[c]), planar_view(gathered[c]))
-        for c in range(last):
-            nc.vector.tensor_scalar_max(mask[c][:], mask[c][:], 0.0)
+        signs = []
+        for j, (s0, n) in enumerate(parts):
+            signs.append(bf16_tile("signs%d" % j, "signs%d" % j, n))
+            nc.scalar.activation(woven_view(signs[j]), planar_view(a_t[j]), ACT.Sign)
+        mask = [placed.tile([P, PACK * 768], BF16, name="mask0", offset=border, align_bytes=64)]
+        mask.append(bf16_tile("mask1", "signs0", 512))
+        mask.append(bf16_tile("mask2", "signs1", 512))
+        for j in range(3):
+            nc.gpsimd.tensor_scalar(mask[j][:], signs[j][:], 1.0, 0.0, ALU.min, ALU.max)
+        mask.append(bf16_tile("mask3", "mask3", 512))
+        nc.scalar.activation(mask[3][:], signs[3][:], ACT.Relu)
+        woven0 = bf16_tile("woven0", "signs3", 768)
+        nc.scalar.copy(woven_view(woven0), planar_view(gathered[0]))
 
-        dx = keep.tile([P, S], F32, name="dx", tag="gd%d" % last, align_bytes=64)
-        for c in range(CHUNKS):
-            da = keep.tile([P, PACK * CHUNK], BF16, name="da%d" % c, align_bytes=64)
-            nc.vector.tensor_tensor(da[:], woven[c][:], mask[c][:], ALU.mult)
-            for v0, n in LAST_PIECES if c == last else PIECES:
-                s0 = c * CHUNK + v0
-                codes = keep.tile([P, n], U32, name="codes%d" % s0, align_bytes=64)
-                plane = keep.tile([P, n], U8, name="plane%d" % s0, align_bytes=64)
-                nc.vector.quantize_mx(
-                    out=codes[:].bitcast(FP8X4), scales=plane[:], in_=da[:, PACK * v0 : PACK * (v0 + n)]
+        turned = bf16_tile("turned", "gd0", SIZES[1])
+        turned_words = turned[:].bitcast(F32)
+        back = []
+        for b in range(BLOCKS):
+            acc = psum.tile([P, 512], F32, name="acc")
+            for t in range(PACK):
+                nc.tensor.transpose(
+                    acc[:, t * P : (t + 1) * P],
+                    gathered[1][:, t * SIZES[1] + b * P : t * SIZES[1] + (b + 1) * P],
+                    identity[:],
                 )
-                acc = psum.tile([P, 512], F32, name="acc")
-                for u0 in range(0, n, C):
-                    e = (s0 + u0) // C
-                    nc.tensor.matmul_mx(
-                        out=acc[:, u0 : u0 + C],
-                        lhsT=w1_codes[:, e, :].bitcast(FP4X4),
-                        lhsT_scale=w1_plane[:, K * e : K * (e + 1)],
-                        rhs=codes[:, u0 : u0 + C].bitcast(FP8X4),
-                        rhs_scale=plane[:, u0 : u0 + C],
-                        start=True,
-                        stop=True,
-                    )
-                if s0 + n == S:
-                    nc.vector.tensor_copy(dx[:, s0 : s0 + n], acc[:, :n])
-                else:
-                    nc.scalar.copy(dx[:, s0 : s0 + n], acc[:, :n])
+            nc.scalar.activation(
+                turned[:, b * H : (b + 1) * H].rearrange("s (u p e) -> s u p e", u=2, e=2),
+                acc[:].rearrange("s (u e p) -> s u p e", u=2, e=2),
+                ACT.Copy,
+                scale=g_col[:, b : b + 1],
+            )
+        for b in range(BLOCKS):
+            if b % 2 == 0:
+                back.append(psum_back.tile([P, 512], F32, name="back"))
+            for u in range(2):
+                nc.tensor.transpose(
+                    back[b // 2][:, u * C + (b % 2) * P : u * C + (b % 2 + 1) * P],
+                    turned_words[:, (2 * b + u) * P : (2 * b + u + 1) * P],
+                    identity[:],
+                )
+
+        woven2 = bf16_tile("woven2", "g_col", 512)
+        nc.scalar.copy(woven_view(woven2), planar_view(gathered[2]))
+
+        dx = keep.tile([P, S], F32, name="dx", tag="gd2", align_bytes=64)
+
+        def experts(s0, n, da, tag, empty):
+            codes = keep.tile([P, n], U32, name="codes%d" % s0, tag=tag, align_bytes=64)
+            plane = keep.tile([P, n], U8, name="plane%d" % s0, align_bytes=64)
+            nc.vector.quantize_mx(out=codes[:].bitcast(FP8X4), scales=plane[:], in_=da)
+            acc = psum.tile([P, 512], F32, name="acc")
+            for u0 in range(0, n, C):
+                e = (s0 + u0) // C
+                nc.tensor.matmul_mx(
+                    out=acc[:, u0 : u0 + C],
+                    lhsT=w1_codes[:, e, :].bitcast(FP4X4),
+                    lhsT_scale=w1_plane[:, K * e : K * (e + 1)],
+                    rhs=codes[:, u0 : u0 + C].bitcast(FP8X4),
+                    rhs_scale=plane[:, u0 : u0 + C],
+                    start=True,
+                    stop=True,
+                )
+            empty(dx[:, s0 : s0 + n], acc[:, :n])
+
+        da0 = bf16_tile("da0", "da0", 768)
+        nc.vector.tensor_tensor(da0[:], woven0[:], mask[0][:], ALU.mult)
+        da1 = [bf16_tile("da1%d" % h, "da1%d" % h, 512) for h in range(2)]
+
+        def masked_back(j):
+            cols = slice(j % 2 * PACK * C, (j % 2 + 1) * PACK * C)
+            nc.vector.tensor_tensor(
+                da1[j // 2][:, cols].rearrange("p (s u e) -> p s u e", u=2, e=2),
+                back[j][:].bitcast(BF16).rearrange("p (u s e) -> p s u e", u=2, e=2),
+                mask[1 + j // 2][:, cols].rearrange("p (s u e) -> p s u e", u=2, e=2),
+                ALU.mult,
+            )
+
+        masked_back(0)
+        experts(0, 512, da0[:, :2048], "c0", nc.scalar.copy)
+        experts(512, 256, da0[:, 2048:], "c1", nc.scalar.copy)
+        masked_back(1)
+        masked_back(2)
+        experts(768, 512, da1[0][:], "c2", nc.scalar.copy)
+        masked_back(3)
+        da2 = bf16_tile("da2", "da2", 512)
+        nc.vector.tensor_tensor(da2[:], woven2[:], mask[3][:], ALU.mult)
+        experts(1280, 512, da1[1][:], "g_col", nc.scalar.copy)
+        experts(1792, 256, da2[:, :1024], "c4", nc.scalar.copy)
+        experts(2048, 256, da2[:, 1024:], "c5", nc.vector.tensor_copy)
 
         for h, t0 in enumerate(range(0, T, TOKEN_HALF)):
             cols = slice(t0 // LIST_ROWS, (t0 + TOKEN_HALF) // LIST_ROWS)

@@ -23,11 +23,12 @@ FP4X4 = mybir.dt.float4_e2m1fn_x4
 ALU = mybir.AluOpType
 ACT = mybir.ActivationFunctionType
 
-SIZES = [768, 1024, 512]
-STARTS = [0, 768, 1792]
-WINDOW = 1024 + 32
+PARTS = [(0, 768), (768, 512), (1280, 512), (1792, 512)]
+FIRST = 768
+TURNED = S - FIRST
+WINDOW = T + 32
 TOKEN_BANKS = [(0, 512), (512, 256)]
-BLOCKS = SIZES[1] // P
+BLOCKS = TURNED // P
 TOKEN_HALF = T // 2
 
 
@@ -72,23 +73,18 @@ def tile_moe_sdb_relu_kernel(
         nc.sync.dma_start(offs_t[:], offs)
 
         a_rows = a.rearrange("(p t) s -> p t s", t=PACK)
-        border = 4 * PACK * SIZES[1]
-        gate0 = placed.tile([P, SIZES[0]], F32, name="gate0", offset=border - 2 * SIZES[0], align_bytes=64)
-        gate2 = keep.tile([P, SIZES[2]], F32, name="gate2")
-        g_col = keep.tile([P, BLOCKS], F32, name="g_col", tag="g_col", align_bytes=64)
-        parts = [(0, 768), (768, 512), (1280, 512), (1792, 512)]
-        a_t = [keep.tile([P, PACK * n], F32, name="a%d" % j, tag="a%d" % j, align_bytes=64) for j, (s0, n) in enumerate(parts)]
-
-        def load_a(j):
-            s0, n = parts[j]
+        border = 4 * PACK * TURNED
+        gate0 = placed.tile([P, FIRST], F32, name="gate0", offset=border - 2 * FIRST, align_bytes=64)
+        g_col = {}
+        a_t = []
+        nc.sync.dma_start(gate0[:], gate[:, :FIRST])
+        for j, (s0, n) in enumerate(PARTS):
+            a_t.append(keep.tile([P, PACK * n], F32, name="a%d" % j, tag="a%d" % j, align_bytes=64))
             nc.sync.dma_start(a_t[j][:].rearrange("p (t s) -> p t s", t=PACK), a_rows[:, :, s0 : s0 + n])
-
-        nc.sync.dma_start(gate0[:], gate[:, : SIZES[0]])
-        for j in range(len(parts)):
-            load_a(j)
-        nc.sync.dma_start(gate2[:], gate[:, STARTS[2] :])
         with nc.allow_non_contiguous_dma(reason="one gate a partition"):
-            nc.sync.dma_start(g_col[:], gate[0, STARTS[1] : STARTS[2]].rearrange("(b p) -> p b", p=P))
+            for j, (s0, n) in list(enumerate(PARTS))[1:]:
+                g_col[j] = keep.tile([P, n // P], F32, name="g_col%d" % j, tag="g_col%d" % j, align_bytes=64)
+                nc.sync.dma_start(g_col[j][:], gate[j, s0 : s0 + n].rearrange("(b p) -> p b", p=P))
         w1_codes = keep.tile([P, E, 2 * K], U8, align_bytes=64)
         nc.sync.dma_start(w1_codes[:].bitcast(I32), w1t_words[:, 0].rearrange("e p b -> p e b").bitcast(I32))
         for q in range(QUADRANTS):
@@ -133,19 +129,16 @@ def tile_moe_sdb_relu_kernel(
                 else:
                     nc.scalar.copy(dc[t][:, t0 : t0 + n], acc[:, :n])
 
-        gathered = []
-        for c, (s0, n) in enumerate(zip(STARTS, SIZES)):
-            if c == 1:
-                gathered.append(placed.tile([P, PACK * n], F32, name="gd1", offset=0, align_bytes=64))
-            else:
-                gathered.append(keep.tile([P, PACK * n], F32, name="gd%d" % c, tag="gd%d" % c, align_bytes=64))
+        gated = keep.tile([P, PACK * FIRST], F32, name="gated", tag="gd0", align_bytes=64)
+        plain = placed.tile([P, PACK * TURNED], F32, name="plain", offset=0, align_bytes=64)
+        for s0, n in PARTS:
             tokens = offs_t[:, s0 // LIST_ROWS : (s0 + n) // LIST_ROWS]
             for t in range(PACK):
-                part = gathered[c][:, t * n : (t + 1) * n]
-                if c == 1:
-                    nc.vector.tensor_copy(part, dc[t][:].indirect(tokens))
+                if s0 == 0:
+                    nc.vector.tensor_tensor(gated[:, t * n : (t + 1) * n], dc[t][:].indirect(tokens), gate0[:], ALU.mult)
                 else:
-                    nc.vector.tensor_tensor(part, dc[t][:].indirect(tokens), (gate0 if c == 0 else gate2)[:], ALU.mult)
+                    at = PACK * (s0 - FIRST) + t * n
+                    nc.vector.tensor_copy(plain[:, at : at + n], dc[t][:].indirect(tokens))
 
         def woven_view(tile):
             return tile[:].rearrange("p (u i t) -> p u t i", i=RUN, t=PACK)
@@ -156,56 +149,72 @@ def tile_moe_sdb_relu_kernel(
         def bf16_tile(name, tag, n):
             return keep.tile([P, PACK * n], BF16, name=name, tag=tag, align_bytes=64)
 
-        signs = []
-        for j, (s0, n) in enumerate(parts):
-            signs.append(bf16_tile("signs%d" % j, "signs%d" % j, n))
-            nc.scalar.activation(woven_view(signs[j]), planar_view(a_t[j]), ACT.Sign)
-        mask = [placed.tile([P, PACK * 768], BF16, name="mask0", offset=border, align_bytes=64)]
-        mask.append(bf16_tile("mask1", "signs0", 512))
-        mask.append(bf16_tile("mask2", "signs1", 512))
-        for j in range(3):
-            nc.gpsimd.tensor_scalar(mask[j][:], signs[j][:], 1.0, 0.0, ALU.min, ALU.max)
-        mask.append(bf16_tile("mask3", "mask3", 512))
-        nc.scalar.activation(mask[3][:], signs[3][:], ACT.Relu)
-        woven0 = bf16_tile("woven0", "signs3", 768)
-        nc.scalar.copy(woven_view(woven0), planar_view(gathered[0]))
-
-        turned = bf16_tile("turned", "gd0", SIZES[1])
-        turned_words = turned[:].bitcast(F32)
+        signs = {}
+        mask = {}
         back = []
-        for b in range(BLOCKS):
-            acc = psum.tile([P, 512], F32, name="acc")
-            for t in range(PACK):
-                nc.tensor.transpose(
-                    acc[:, t * P : (t + 1) * P],
-                    gathered[1][:, t * SIZES[1] + b * P : t * SIZES[1] + (b + 1) * P],
-                    identity[:],
+
+        def make_signs(j, tag):
+            signs[j] = bf16_tile("signs%d" % j, tag, PARTS[j][1])
+            nc.scalar.activation(woven_view(signs[j]), planar_view(a_t[j]), ACT.Sign)
+
+        def clip(j):
+            nc.gpsimd.tensor_scalar(mask[j][:], signs[j][:], 1.0, 0.0, ALU.min, ALU.max)
+
+        def turn(j, tag):
+            s0, n = PARTS[j]
+            turned = bf16_tile("turned%d" % j, tag, n)
+            words = turned[:].bitcast(F32)
+            for b in range(n // P):
+                acc = psum.tile([P, 512], F32, name="acc")
+                for t in range(PACK):
+                    at = PACK * (s0 - FIRST) + t * n + b * P
+                    nc.tensor.transpose(acc[:, t * P : (t + 1) * P], plain[:, at : at + P], identity[:])
+                nc.scalar.activation(
+                    turned[:, b * H : (b + 1) * H].rearrange("s (u p e) -> s u p e", u=2, e=2),
+                    acc[:].rearrange("s (u e p) -> s u p e", u=2, e=2),
+                    ACT.Copy,
+                    scale=g_col[j][:, b : b + 1],
                 )
-            nc.scalar.activation(
-                turned[:, b * H : (b + 1) * H].rearrange("s (u p e) -> s u p e", u=2, e=2),
-                acc[:].rearrange("s (u e p) -> s u p e", u=2, e=2),
-                ACT.Copy,
-                scale=g_col[:, b : b + 1],
-            )
-        for b in range(BLOCKS):
-            if b % 2 == 0:
-                back.append(psum_back.tile([P, 512], F32, name="back"))
-            for u in range(2):
-                nc.tensor.transpose(
-                    back[b // 2][:, u * C + (b % 2) * P : u * C + (b % 2 + 1) * P],
-                    turned_words[:, (2 * b + u) * P : (2 * b + u + 1) * P],
-                    identity[:],
-                )
+            for b in range(n // P):
+                if b % 2 == 0:
+                    back.append(psum_back.tile([P, 512], F32, name="back"))
+                for u in range(2):
+                    nc.tensor.transpose(
+                        back[-1][:, u * C + b % 2 * P : u * C + (b % 2 + 1) * P],
+                        words[:, (2 * b + u) * P : (2 * b + u + 1) * P],
+                        identity[:],
+                    )
 
-        woven2 = bf16_tile("woven2", "g_col", 512)
-        nc.scalar.copy(woven_view(woven2), planar_view(gathered[2]))
+        make_signs(0, "signs0")
+        make_signs(1, "signs1")
+        mask[0] = placed.tile([P, PACK * FIRST], BF16, name="mask0", offset=border, align_bytes=64)
+        clip(0)
+        mask[1] = bf16_tile("mask1", "signs0", 512)
+        clip(1)
+        woven = bf16_tile("woven", "a1", 512)
+        nc.scalar.copy(woven_view(woven), planar_view(gated)[:, :128])
+        woven_rest = bf16_tile("woven_rest", "a0", 256)
+        nc.scalar.copy(woven_view(woven_rest), planar_view(gated)[:, 128:])
+        da0 = bf16_tile("da0", "signs1", 512)
+        nc.gpsimd.tensor_tensor(da0[:], woven[:], mask[0][:, :2048], ALU.mult)
+        make_signs(2, "gd0")
+        mask[2] = bf16_tile("mask2", "a1", 512)
+        clip(2)
+        turn(1, "a2")
+        make_signs(3, "g_col1")
+        mask[3] = bf16_tile("mask3", "gd0", 512)
+        clip(3)
+        turn(2, "a3")
+        turn(3, "turned3")
 
-        dx = keep.tile([P, S], F32, name="dx", tag="gd2", align_bytes=64)
+        dx = keep.tile([P, S], F32, name="dx", tag="g_col3", align_bytes=64)
+        da_rest = bf16_tile("da_rest", "g_col1", 256)
+        all_codes = keep.tile([P, S], U32, name="codes", tag="a0", align_bytes=64)
 
-        def experts(s0, n, da, tag, empty):
-            codes = keep.tile([P, n], U32, name="codes%d" % s0, tag=tag, align_bytes=64)
+        def experts(s0, n, da, empty):
+            codes = all_codes[:, s0 : s0 + n]
             plane = keep.tile([P, n], U8, name="plane%d" % s0, align_bytes=64)
-            nc.vector.quantize_mx(out=codes[:].bitcast(FP8X4), scales=plane[:], in_=da)
+            nc.vector.quantize_mx(out=codes.bitcast(FP8X4), scales=plane[:], in_=da)
             acc = psum.tile([P, 512], F32, name="acc")
             for u0 in range(0, n, C):
                 e = (s0 + u0) // C
@@ -220,31 +229,30 @@ def tile_moe_sdb_relu_kernel(
                 )
             empty(dx[:, s0 : s0 + n], acc[:, :n])
 
-        da0 = bf16_tile("da0", "da0", 768)
-        nc.vector.tensor_tensor(da0[:], woven0[:], mask[0][:], ALU.mult)
-        da1 = [bf16_tile("da1%d" % h, "da1%d" % h, 512) for h in range(2)]
+        da = {j: bf16_tile("da%d" % j, "da%d" % j, PARTS[j][1]) for j in range(1, len(PARTS))}
 
-        def masked_back(j):
-            cols = slice(j % 2 * PACK * C, (j % 2 + 1) * PACK * C)
+        def masked_back(j, v0):
+            cols = slice(PACK * v0, PACK * (v0 + C))
+            bank = back[(PARTS[j][0] + v0 - FIRST) // C]
             nc.vector.tensor_tensor(
-                da1[j // 2][:, cols].rearrange("p (s u e) -> p s u e", u=2, e=2),
-                back[j][:].bitcast(BF16).rearrange("p (u s e) -> p s u e", u=2, e=2),
-                mask[1 + j // 2][:, cols].rearrange("p (s u e) -> p s u e", u=2, e=2),
+                da[j][:, cols].rearrange("p (s u e) -> p s u e", u=2, e=2),
+                bank[:].bitcast(BF16).rearrange("p (u s e) -> p s u e", u=2, e=2),
+                mask[j][:, cols].rearrange("p (s u e) -> p s u e", u=2, e=2),
                 ALU.mult,
             )
 
-        masked_back(0)
-        experts(0, 512, da0[:, :2048], "c0", nc.scalar.copy)
-        experts(512, 256, da0[:, 2048:], "c1", nc.scalar.copy)
-        masked_back(1)
-        masked_back(2)
-        experts(768, 512, da1[0][:], "c2", nc.scalar.copy)
-        masked_back(3)
-        da2 = bf16_tile("da2", "da2", 512)
-        nc.vector.tensor_tensor(da2[:], woven2[:], mask[3][:], ALU.mult)
-        experts(1280, 512, da1[1][:], "g_col", nc.scalar.copy)
-        experts(1792, 256, da2[:, :1024], "c4", nc.scalar.copy)
-        experts(2048, 256, da2[:, 1024:], "c5", nc.vector.tensor_copy)
+        for j in (1, 2):
+            for v0 in range(0, PARTS[j][1], C):
+                masked_back(j, v0)
+        nc.vector.tensor_tensor(da_rest[:], woven_rest[:], mask[0][:, 2048:], ALU.mult)
+        experts(0, 512, da0[:], nc.scalar.copy)
+        experts(768, 512, da[1][:], nc.scalar.copy)
+        experts(512, 256, da_rest[:], nc.scalar.copy)
+        masked_back(3, 0)
+        experts(1280, 512, da[2][:], nc.scalar.copy)
+        masked_back(3, C)
+        experts(1792, 256, da[3][:, :1024], nc.vector.tensor_copy)
+        experts(2048, 256, da[3][:, 1024:], nc.vector.tensor_copy)
 
         for h, t0 in enumerate(range(0, T, TOKEN_HALF)):
             cols = slice(t0 // LIST_ROWS, (t0 + TOKEN_HALF) // LIST_ROWS)

@@ -10,6 +10,8 @@ PACK = 4
 QUADRANTS = 4
 RUN = 4
 LIST_ROWS = 16
+BANK = 512
+BANKS = 8
 FLOPS = 2 * N * H * T + 2 * H * K * S
 
 F32 = mybir.dt.float32
@@ -23,13 +25,14 @@ FP4X4 = mybir.dt.float4_e2m1fn_x4
 ALU = mybir.AluOpType
 ACT = mybir.ActivationFunctionType
 
-PARTS = [(0, 768), (768, 512), (1280, 512), (1792, 512)]
-FIRST = 768
-TURNED = S - FIRST
+GATED = 768
+PARTS = [(0, GATED), (768, 512), (1280, 512), (1792, 512)]
+TURNED = S - GATED
+ON_GPSIMD = 512
 WINDOW = T + 32
 TOKEN_BANKS = [(0, 512), (512, 256)]
-BLOCKS = TURNED // P
-TOKEN_HALF = T // 2
+FIRST_TOKEN_BANKS = [(0, 256), (256, 256), (512, 256)]
+TOKEN_RANGES = [(0, 480), (480, 288)]
 
 
 def tile_moe_sdb_relu_kernel(
@@ -40,13 +43,24 @@ def tile_moe_sdb_relu_kernel(
     with ExitStack() as ctx:
         keep = ctx.enter_context(tc.tile_pool(name="keep", bufs=1))
         placed = ctx.enter_context(tc.tile_pool(name="placed", bufs=1))
-        psum = ctx.enter_context(tc.psum_pool(name="psum", bufs=4))
-        psum_back = ctx.enter_context(tc.psum_pool(name="psum_back", bufs=4))
+        psum = ctx.enter_context(tc.psum_pool(name="psum", bufs=1))
+
+        def bank(i):
+            return psum.tile([P, BANK], F32, name="bank%d" % i, tag="bank%d" % i)
+
+        def bf16_tile(name, tag, slots):
+            return keep.tile([P, PACK * slots], BF16, name=name, tag=tag, align_bytes=64)
+
+        def woven_view(tile):
+            return tile[:].rearrange("p (r i t) -> p r t i", i=RUN, t=PACK)
+
+        def planar_view(tile):
+            return tile[:].rearrange("p (t r i) -> p r t i", i=RUN, t=PACK)
 
         w2_plane_raw = keep.tile([P, H], U8, align_bytes=64)
         dy_plane = keep.tile([P, T], U8, align_bytes=64)
         w1_plane = keep.tile([P, E * K], U8, align_bytes=64)
-        nc.vector.memset(w2_plane_raw[:].bitcast(I32), 0)
+        nc.gpsimd.memset(w2_plane_raw[:].bitcast(I32), 0)
         nc.vector.memset(dy_plane[:].bitcast(I32), 0)
         nc.vector.memset(w1_plane[:].bitcast(I32), 0)
         identity = keep.tile([P, P], F32)
@@ -56,35 +70,36 @@ def tile_moe_sdb_relu_kernel(
             dc.append(keep.tile([P, WINDOW], F32, name="dc%d" % t))
             nc.gpsimd.memset(dc[t][:, T:], 0.0)
 
-        def load_scale_rows(plane_in, scales, q):
-            nc.sync.dma_start(
-                plane_in[32 * q : 32 * q + 4, :].bitcast(I32), scales[0, 4 * q : 4 * q + 4, :].bitcast(I32)
-            )
+        def load_scale_rows(plane, scales, quadrants):
+            for q in quadrants:
+                nc.sync.dma_start(
+                    plane[32 * q : 32 * q + 4, :].bitcast(I32), scales[0, 4 * q : 4 * q + 4, :].bitcast(I32)
+                )
 
         w2_raw = keep.tile([P, 2 * H], U8, align_bytes=64)
+        load_scale_rows(w2_plane_raw, w2t_scales, range(2))
         nc.sync.dma_start(w2_raw[:].bitcast(I32), w2t_words[0].bitcast(I32))
-        for q in range(QUADRANTS):
-            load_scale_rows(w2_plane_raw, w2t_scales, q)
+        load_scale_rows(w2_plane_raw, w2t_scales, range(2, QUADRANTS))
         dy_codes = keep.tile([P, 4 * T], U8, align_bytes=64)
         nc.sync.dma_start(dy_codes[:].bitcast(I32), dy_words[0].rearrange("p t d -> p (t d)").bitcast(I32))
-        for q in range(QUADRANTS):
-            load_scale_rows(dy_plane, dy_scales, q)
+        load_scale_rows(dy_plane, dy_scales, range(QUADRANTS))
         offs_t = keep.tile([P, S // LIST_ROWS], U16)
         nc.sync.dma_start(offs_t[:], offs)
 
-        a_rows = a.rearrange("(p t) s -> p t s", t=PACK)
         border = 4 * PACK * TURNED
-        gate0 = placed.tile([P, FIRST], F32, name="gate0", offset=border - 2 * FIRST, align_bytes=64)
-        g_col = {}
+        gate_rows = placed.tile([P, GATED], F32, name="gate_rows", offset=border - 2 * GATED, align_bytes=64)
+        nc.sync.dma_start(gate_rows[:], gate[:, :GATED])
+        a_rows = a.rearrange("(p t) s -> p t s", t=PACK)
         a_t = []
-        nc.sync.dma_start(gate0[:], gate[:, :FIRST])
         for j, (s0, n) in enumerate(PARTS):
             a_t.append(keep.tile([P, PACK * n], F32, name="a%d" % j, tag="a%d" % j, align_bytes=64))
             nc.sync.dma_start(a_t[j][:].rearrange("p (t s) -> p t s", t=PACK), a_rows[:, :, s0 : s0 + n])
+        gate_cols = {}
         with nc.allow_non_contiguous_dma(reason="one gate a partition"):
-            for j, (s0, n) in list(enumerate(PARTS))[1:]:
-                g_col[j] = keep.tile([P, n // P], F32, name="g_col%d" % j, tag="g_col%d" % j, align_bytes=64)
-                nc.sync.dma_start(g_col[j][:], gate[j, s0 : s0 + n].rearrange("(b p) -> p b", p=P))
+            for j in range(1, len(PARTS)):
+                s0, n = PARTS[j]
+                gate_cols[j] = keep.tile([P, n // P], F32, name="gate_cols%d" % j, tag="cols%d" % j, align_bytes=64)
+                nc.sync.dma_start(gate_cols[j][:], gate[j, s0 : s0 + n].rearrange("(b p) -> p b", p=P))
         w1_codes = keep.tile([P, E, 2 * K], U8, align_bytes=64)
         nc.sync.dma_start(w1_codes[:].bitcast(I32), w1t_words[:, 0].rearrange("e p b -> p e b").bitcast(I32))
         for q in range(QUADRANTS):
@@ -109,45 +124,35 @@ def tile_moe_sdb_relu_kernel(
                 w2_plane_raw[:].rearrange("p (m t) -> p t m", t=PACK)[:, ts, :],
             )
 
-        for t in range(PACK):
-            for t0, n in TOKEN_BANKS:
-                if n == 512:
-                    acc = psum.tile([P, 512], F32, name="acc")
-                else:
-                    acc = psum_back.tile([P, 512], F32, name="back")
-                nc.tensor.matmul_mx(
-                    out=acc[:, :n],
-                    lhsT=w2_codes[:, 2 * P * t : 2 * P * (t + 1)].bitcast(FP4X4),
-                    lhsT_scale=w2_plane[:, P * t : P * (t + 1)],
-                    rhs=dy_codes[:, 4 * t0 : 4 * (t0 + n)].bitcast(FP8X4),
-                    rhs_scale=dy_plane[:, t0 : t0 + n],
-                    start=True,
-                    stop=True,
-                )
-                if t == 0 and t0 > 0:
-                    nc.vector.tensor_copy(dc[t][:, t0 : t0 + n], acc[:, :n])
-                else:
-                    nc.scalar.copy(dc[t][:, t0 : t0 + n], acc[:, :n])
+        products = [(t, t0, n) for t in range(PACK) for t0, n in (FIRST_TOKEN_BANKS if t == 0 else TOKEN_BANKS)]
+        for x, (t, t0, n) in enumerate(products):
+            acc = bank(x % BANKS)
+            nc.tensor.matmul_mx(
+                out=acc[:, :n],
+                lhsT=w2_codes[:, 2 * P * t : 2 * P * (t + 1)].bitcast(FP4X4),
+                lhsT_scale=w2_plane[:, P * t : P * (t + 1)],
+                rhs=dy_codes[:, 4 * t0 : 4 * (t0 + n)].bitcast(FP8X4),
+                rhs_scale=dy_plane[:, t0 : t0 + n],
+                start=True,
+                stop=True,
+            )
+            if t == 0 and (t0 == 0 or t0 + n == T):
+                nc.vector.tensor_copy(dc[t][:, t0 : t0 + n], acc[:, :n])
+            else:
+                nc.scalar.copy(dc[t][:, t0 : t0 + n], acc[:, :n])
 
-        gated = keep.tile([P, PACK * FIRST], F32, name="gated", tag="gd0", align_bytes=64)
+        gated = keep.tile([P, PACK * GATED], F32, name="gated", tag="gated", align_bytes=64)
         plain = placed.tile([P, PACK * TURNED], F32, name="plain", offset=0, align_bytes=64)
         for s0, n in PARTS:
             tokens = offs_t[:, s0 // LIST_ROWS : (s0 + n) // LIST_ROWS]
             for t in range(PACK):
-                if s0 == 0:
-                    nc.vector.tensor_tensor(gated[:, t * n : (t + 1) * n], dc[t][:].indirect(tokens), gate0[:], ALU.mult)
+                if s0 < GATED:
+                    nc.vector.tensor_tensor(
+                        gated[:, t * n : (t + 1) * n], dc[t][:].indirect(tokens), gate_rows[:], ALU.mult
+                    )
                 else:
-                    at = PACK * (s0 - FIRST) + t * n
+                    at = PACK * (s0 - GATED) + t * n
                     nc.vector.tensor_copy(plain[:, at : at + n], dc[t][:].indirect(tokens))
-
-        def woven_view(tile):
-            return tile[:].rearrange("p (u i t) -> p u t i", i=RUN, t=PACK)
-
-        def planar_view(tile):
-            return tile[:].rearrange("p (t u i) -> p u t i", i=RUN, t=PACK)
-
-        def bf16_tile(name, tag, n):
-            return keep.tile([P, PACK * n], BF16, name=name, tag=tag, align_bytes=64)
 
         signs = {}
         mask = {}
@@ -157,7 +162,8 @@ def tile_moe_sdb_relu_kernel(
             signs[j] = bf16_tile("signs%d" % j, tag, PARTS[j][1])
             nc.scalar.activation(woven_view(signs[j]), planar_view(a_t[j]), ACT.Sign)
 
-        def clip(j):
+        def clip(j, tile):
+            mask[j] = tile
             nc.gpsimd.tensor_scalar(mask[j][:], signs[j][:], 1.0, 0.0, ALU.min, ALU.max)
 
         def turn(j, tag):
@@ -165,19 +171,19 @@ def tile_moe_sdb_relu_kernel(
             turned = bf16_tile("turned%d" % j, tag, n)
             words = turned[:].bitcast(F32)
             for b in range(n // P):
-                acc = psum.tile([P, 512], F32, name="acc")
+                acc = bank(b)
                 for t in range(PACK):
-                    at = PACK * (s0 - FIRST) + t * n + b * P
+                    at = PACK * (s0 - GATED) + t * n + b * P
                     nc.tensor.transpose(acc[:, t * P : (t + 1) * P], plain[:, at : at + P], identity[:])
                 nc.scalar.activation(
                     turned[:, b * H : (b + 1) * H].rearrange("s (u p e) -> s u p e", u=2, e=2),
                     acc[:].rearrange("s (u e p) -> s u p e", u=2, e=2),
                     ACT.Copy,
-                    scale=g_col[j][:, b : b + 1],
+                    scale=gate_cols[j][:, b : b + 1],
                 )
             for b in range(n // P):
                 if b % 2 == 0:
-                    back.append(psum_back.tile([P, 512], F32, name="back"))
+                    back.append(bank(4 + len(back) % 4))
                 for u in range(2):
                     nc.tensor.transpose(
                         back[-1][:, u * C + b % 2 * P : u * C + (b % 2 + 1) * P],
@@ -185,81 +191,76 @@ def tile_moe_sdb_relu_kernel(
                         identity[:],
                     )
 
+        rest = GATED - ON_GPSIMD
         make_signs(0, "signs0")
         make_signs(1, "signs1")
-        mask[0] = placed.tile([P, PACK * FIRST], BF16, name="mask0", offset=border, align_bytes=64)
-        clip(0)
-        mask[1] = bf16_tile("mask1", "signs0", 512)
-        clip(1)
-        woven = bf16_tile("woven", "a1", 512)
-        nc.scalar.copy(woven_view(woven), planar_view(gated)[:, :128])
-        woven_rest = bf16_tile("woven_rest", "a0", 256)
-        nc.scalar.copy(woven_view(woven_rest), planar_view(gated)[:, 128:])
-        da0 = bf16_tile("da0", "signs1", 512)
-        nc.gpsimd.tensor_tensor(da0[:], woven[:], mask[0][:, :2048], ALU.mult)
-        make_signs(2, "gd0")
-        mask[2] = bf16_tile("mask2", "a1", 512)
-        clip(2)
+        clip(0, placed.tile([P, PACK * GATED], BF16, name="mask0", offset=border, align_bytes=64))
+        clip(1, bf16_tile("mask1", "signs0", PARTS[1][1]))
+        woven = bf16_tile("woven", "a1", ON_GPSIMD)
+        nc.scalar.copy(woven_view(woven), planar_view(gated)[:, : ON_GPSIMD // RUN])
+        woven_rest = bf16_tile("woven_rest", "a0", rest)
+        nc.scalar.copy(woven_view(woven_rest), planar_view(gated)[:, ON_GPSIMD // RUN :])
+        da_first = bf16_tile("da_first", "signs1", ON_GPSIMD)
+        nc.gpsimd.tensor_tensor(da_first[:], woven[:], mask[0][:, : PACK * ON_GPSIMD], ALU.mult)
+        make_signs(2, "gated")
+        clip(2, bf16_tile("mask2", "a1", PARTS[2][1]))
         turn(1, "a2")
-        make_signs(3, "g_col1")
-        mask[3] = bf16_tile("mask3", "gd0", 512)
-        clip(3)
+        make_signs(3, "cols1")
+        clip(3, bf16_tile("mask3", "gated", PARTS[3][1]))
         turn(2, "a3")
         turn(3, "turned3")
 
-        dx = keep.tile([P, S], F32, name="dx", tag="g_col3", align_bytes=64)
-        da_rest = bf16_tile("da_rest", "g_col1", 256)
-        all_codes = keep.tile([P, S], U32, name="codes", tag="a0", align_bytes=64)
+        dx = keep.tile([P, S], F32, name="dx", tag="cols3", align_bytes=64)
+        da_rest = bf16_tile("da_rest", "cols1", rest)
+        codes = keep.tile([P, S], U32, name="codes", tag="a0", align_bytes=64)
+        da = {j: bf16_tile("da%d" % j, "da%d" % j, PARTS[j][1]) for j in range(1, len(PARTS))}
 
-        def experts(s0, n, da, empty):
-            codes = all_codes[:, s0 : s0 + n]
+        def apply_mask(j, v0):
+            cols = slice(PACK * v0, PACK * (v0 + C))
+            source = back[(PARTS[j][0] + v0 - GATED) // C]
+            nc.vector.tensor_tensor(
+                da[j][:, cols].rearrange("p (s u e) -> p s u e", u=2, e=2),
+                source[:].bitcast(BF16).rearrange("p (u s e) -> p s u e", u=2, e=2),
+                mask[j][:, cols].rearrange("p (s u e) -> p s u e", u=2, e=2),
+                ALU.mult,
+            )
+
+        def experts(s0, n, values, where, empty):
             plane = keep.tile([P, n], U8, name="plane%d" % s0, align_bytes=64)
-            nc.vector.quantize_mx(out=codes.bitcast(FP8X4), scales=plane[:], in_=da)
-            acc = psum.tile([P, 512], F32, name="acc")
-            for u0 in range(0, n, C):
-                e = (s0 + u0) // C
+            nc.vector.quantize_mx(out=codes[:, s0 : s0 + n].bitcast(FP8X4), scales=plane[:], in_=values)
+            acc = bank(where)
+            for v0 in range(0, n, C):
+                e = (s0 + v0) // C
                 nc.tensor.matmul_mx(
-                    out=acc[:, u0 : u0 + C],
+                    out=acc[:, v0 : v0 + C],
                     lhsT=w1_codes[:, e, :].bitcast(FP4X4),
                     lhsT_scale=w1_plane[:, K * e : K * (e + 1)],
-                    rhs=codes[:, u0 : u0 + C].bitcast(FP8X4),
-                    rhs_scale=plane[:, u0 : u0 + C],
+                    rhs=codes[:, s0 + v0 : s0 + v0 + C].bitcast(FP8X4),
+                    rhs_scale=plane[:, v0 : v0 + C],
                     start=True,
                     stop=True,
                 )
             empty(dx[:, s0 : s0 + n], acc[:, :n])
 
-        da = {j: bf16_tile("da%d" % j, "da%d" % j, PARTS[j][1]) for j in range(1, len(PARTS))}
-
-        def masked_back(j, v0):
-            cols = slice(PACK * v0, PACK * (v0 + C))
-            bank = back[(PARTS[j][0] + v0 - FIRST) // C]
-            nc.vector.tensor_tensor(
-                da[j][:, cols].rearrange("p (s u e) -> p s u e", u=2, e=2),
-                bank[:].bitcast(BF16).rearrange("p (u s e) -> p s u e", u=2, e=2),
-                mask[j][:, cols].rearrange("p (s u e) -> p s u e", u=2, e=2),
-                ALU.mult,
-            )
-
         for j in (1, 2):
             for v0 in range(0, PARTS[j][1], C):
-                masked_back(j, v0)
-        nc.vector.tensor_tensor(da_rest[:], woven_rest[:], mask[0][:, 2048:], ALU.mult)
-        experts(0, 512, da0[:], nc.scalar.copy)
-        experts(768, 512, da[1][:], nc.scalar.copy)
-        experts(512, 256, da_rest[:], nc.scalar.copy)
-        masked_back(3, 0)
-        experts(1280, 512, da[2][:], nc.scalar.copy)
-        masked_back(3, C)
-        experts(1792, 256, da[3][:, :1024], nc.vector.tensor_copy)
-        experts(2048, 256, da[3][:, 1024:], nc.vector.tensor_copy)
+                apply_mask(j, v0)
+        nc.vector.tensor_tensor(da_rest[:], woven_rest[:], mask[0][:, PACK * ON_GPSIMD :], ALU.mult)
+        experts(0, ON_GPSIMD, da_first[:], 6, nc.scalar.copy)
+        experts(PARTS[1][0], PARTS[1][1], da[1][:], 7, nc.scalar.copy)
+        experts(ON_GPSIMD, rest, da_rest[:], 0, nc.scalar.copy)
+        apply_mask(3, 0)
+        experts(PARTS[2][0], PARTS[2][1], da[2][:], 1, nc.scalar.copy)
+        apply_mask(3, C)
+        experts(PARTS[3][0], C, da[3][:, : PACK * C], 2, nc.vector.tensor_copy)
+        experts(PARTS[3][0] + C, C, da[3][:, PACK * C :], 3, nc.scalar.copy)
 
-        for h, t0 in enumerate(range(0, T, TOKEN_HALF)):
-            cols = slice(t0 // LIST_ROWS, (t0 + TOKEN_HALF) // LIST_ROWS)
-            first = keep.tile([P, TOKEN_HALF], F32, name="first%d" % h)
+        for h, (t0, n) in enumerate(TOKEN_RANGES):
+            cols = slice(t0 // LIST_ROWS, (t0 + n) // LIST_ROWS)
+            first = keep.tile([P, n], F32, name="first%d" % h)
             nc.vector.tensor_copy(first[:], dx[:].indirect(pos_t[0][:, cols]))
-            second = keep.tile([P, TOKEN_HALF], F32, name="second%d" % h)
+            second = keep.tile([P, n], F32, name="second%d" % h)
             nc.vector.tensor_tensor(second[:], dx[:].indirect(pos_t[1][:, cols]), first[:], ALU.add)
-            third = keep.tile([P, TOKEN_HALF], F32, name="third%d" % h)
+            third = keep.tile([P, n], F32, name="third%d" % h)
             nc.vector.tensor_tensor(third[:], dx[:].indirect(pos_t[2][:, cols]), second[:], ALU.add)
-            nc.sync.dma_start(out[:, t0 : t0 + TOKEN_HALF], third[:])
+            nc.sync.dma_start(out[:, t0 : t0 + n], third[:])

@@ -25,10 +25,10 @@ FP4X4 = mybir.dt.float4_e2m1fn_x4
 ALU = mybir.AluOpType
 ACT = mybir.ActivationFunctionType
 
-GATED = 768
-PARTS = [(0, GATED), (768, 512), (1280, 512), (1792, 512)]
+GATED = 512
+PARTS = [(0, GATED), (512, 768), (1280, 512), (1792, 512)]
 TURNED = S - GATED
-ON_GPSIMD = 512
+RING = 4
 WINDOW = T + 32
 TOKEN_BANKS = [(0, 512), (512, 256)]
 FIRST_TOKEN_BANKS = [(0, 256), (256, 256), (512, 256)]
@@ -171,7 +171,7 @@ def tile_moe_sdb_relu_kernel(
             turned = bf16_tile("turned%d" % j, tag, n)
             words = turned[:].bitcast(F32)
             for b in range(n // P):
-                acc = bank(b)
+                acc = bank(b % RING)
                 for t in range(PACK):
                     at = PACK * (s0 - GATED) + t * n + b * P
                     nc.tensor.transpose(acc[:, t * P : (t + 1) * P], plain[:, at : at + P], identity[:])
@@ -183,45 +183,47 @@ def tile_moe_sdb_relu_kernel(
                 )
             for b in range(n // P):
                 if b % 2 == 0:
-                    back.append(bank(4 + len(back) % 4))
+                    back.append(bank(RING + len(back) % RING))
                 for u in range(2):
                     nc.tensor.transpose(
-                        back[-1][:, u * C + b % 2 * P : u * C + (b % 2 + 1) * P],
+                        back[-1][:, b % 2 * C + u : (b % 2 + 1) * C : 2],
                         words[:, (2 * b + u) * P : (2 * b + u + 1) * P],
                         identity[:],
                     )
 
-        rest = GATED - ON_GPSIMD
         make_signs(0, "signs0")
-        make_signs(1, "signs1")
         clip(0, placed.tile([P, PACK * GATED], BF16, name="mask0", offset=border, align_bytes=64))
-        clip(1, bf16_tile("mask1", "signs0", PARTS[1][1]))
-        woven = bf16_tile("woven", "a1", ON_GPSIMD)
-        nc.scalar.copy(woven_view(woven), planar_view(gated)[:, : ON_GPSIMD // RUN])
-        woven_rest = bf16_tile("woven_rest", "a0", rest)
-        nc.scalar.copy(woven_view(woven_rest), planar_view(gated)[:, ON_GPSIMD // RUN :])
-        da_first = bf16_tile("da_first", "signs1", ON_GPSIMD)
-        nc.gpsimd.tensor_tensor(da_first[:], woven[:], mask[0][:, : PACK * ON_GPSIMD], ALU.mult)
-        make_signs(2, "gated")
-        clip(2, bf16_tile("mask2", "a1", PARTS[2][1]))
+        woven = bf16_tile("woven", "a0", GATED)
+        nc.scalar.copy(woven_view(woven), planar_view(gated))
+        da_first = bf16_tile("da_first", "signs0", GATED)
+        nc.gpsimd.tensor_tensor(da_first[:], woven[:], mask[0][:], ALU.mult)
+        make_signs(1, "gated")
+        clip(1, bf16_tile("mask1", "a0", PARTS[1][1]))
+        make_signs(2, "signs2")
+        clip(2, bf16_tile("mask2", "gated", PARTS[2][1]))
         turn(1, "a2")
+        moved = bf16_tile("moved", "moved", C)
+        nc.scalar.copy(moved[:], back[0][:].bitcast(BF16))
+        da_moved = bf16_tile("da_moved", "signs2", C)
+        nc.gpsimd.tensor_tensor(da_moved[:], moved[:], mask[1][:, : PACK * C], ALU.mult)
         make_signs(3, "cols1")
-        clip(3, bf16_tile("mask3", "gated", PARTS[3][1]))
+        clip(3, bf16_tile("mask3", "moved", PARTS[3][1]))
         turn(2, "a3")
         turn(3, "turned3")
 
         dx = keep.tile([P, S], F32, name="dx", tag="cols3", align_bytes=64)
-        da_rest = bf16_tile("da_rest", "cols1", rest)
-        codes = keep.tile([P, S], U32, name="codes", tag="a0", align_bytes=64)
-        da = {j: bf16_tile("da%d" % j, "da%d" % j, PARTS[j][1]) for j in range(1, len(PARTS))}
+        codes = keep.tile([P, S], U32, name="codes", tag="cols1", align_bytes=64)
+        da = bf16_tile("da", "da", TURNED - C)
+
+        def da_slots(s0, n):
+            return da[:, PACK * (s0 - GATED - C) : PACK * (s0 + n - GATED - C)]
 
         def apply_mask(j, v0):
-            cols = slice(PACK * v0, PACK * (v0 + C))
-            source = back[(PARTS[j][0] + v0 - GATED) // C]
+            s0 = PARTS[j][0] + v0
             nc.vector.tensor_tensor(
-                da[j][:, cols].rearrange("p (s u e) -> p s u e", u=2, e=2),
-                source[:].bitcast(BF16).rearrange("p (u s e) -> p s u e", u=2, e=2),
-                mask[j][:, cols].rearrange("p (s u e) -> p s u e", u=2, e=2),
+                da_slots(s0, C),
+                back[(s0 - GATED) // C][:].bitcast(BF16),
+                mask[j][:, PACK * v0 : PACK * (v0 + C)],
                 ALU.mult,
             )
 
@@ -242,18 +244,16 @@ def tile_moe_sdb_relu_kernel(
                 )
             empty(dx[:, s0 : s0 + n], acc[:, :n])
 
-        for j in (1, 2):
-            for v0 in range(0, PARTS[j][1], C):
-                apply_mask(j, v0)
-        nc.vector.tensor_tensor(da_rest[:], woven_rest[:], mask[0][:, PACK * ON_GPSIMD :], ALU.mult)
-        experts(0, ON_GPSIMD, da_first[:], 6, nc.scalar.copy)
-        experts(PARTS[1][0], PARTS[1][1], da[1][:], 7, nc.scalar.copy)
-        experts(ON_GPSIMD, rest, da_rest[:], 0, nc.scalar.copy)
+        for j, v0 in ((1, C), (1, 2 * C), (2, 0), (2, C)):
+            apply_mask(j, v0)
+        experts(0, GATED, da_first[:], 7, nc.scalar.copy)
+        experts(GATED, C, da_moved[:], 4, nc.scalar.copy)
+        experts(GATED + C, 2 * C, da_slots(GATED + C, 2 * C), 0, nc.scalar.copy)
+        experts(PARTS[2][0], PARTS[2][1], da_slots(*PARTS[2]), 1, nc.scalar.copy)
         apply_mask(3, 0)
-        experts(PARTS[2][0], PARTS[2][1], da[2][:], 1, nc.scalar.copy)
         apply_mask(3, C)
-        experts(PARTS[3][0], C, da[3][:, : PACK * C], 2, nc.vector.tensor_copy)
-        experts(PARTS[3][0] + C, C, da[3][:, PACK * C :], 3, nc.scalar.copy)
+        experts(PARTS[3][0], C, da_slots(PARTS[3][0], C), 2, nc.vector.tensor_copy)
+        experts(PARTS[3][0] + C, C, da_slots(PARTS[3][0] + C, C), 3, nc.scalar.copy)
 
         for h, (t0, n) in enumerate(TOKEN_RANGES):
             cols = slice(t0 // LIST_ROWS, (t0 + n) // LIST_ROWS)

@@ -31,7 +31,7 @@ TURNED = S - GATED
 RING = 4
 WINDOW = T + 32
 TOKEN_BANKS = [(0, 512), (512, 256)]
-FIRST_TOKEN_BANKS = [(0, 256), (256, 256), (512, 256)]
+FIRST_TOKEN_BANKS = [(0, 256), (256, 256), (512, 128), (640, 128)]
 TOKEN_RANGES = [(0, 480), (480, 288)]
 
 
@@ -136,7 +136,7 @@ def tile_moe_sdb_relu_kernel(
                 start=True,
                 stop=True,
             )
-            if t == 0 and (t0 == 0 or t0 + n == T):
+            if t == 0 and x != 1:
                 nc.vector.tensor_copy(dc[t][:, t0 : t0 + n], acc[:, :n])
             else:
                 nc.scalar.copy(dc[t][:, t0 : t0 + n], acc[:, :n])
@@ -231,14 +231,15 @@ def tile_moe_sdb_relu_kernel(
             plane = keep.tile([P, n], U8, name="plane%d" % s0, align_bytes=64)
             nc.vector.quantize_mx(out=codes[:, s0 : s0 + n].bitcast(FP8X4), scales=plane[:], in_=values)
             acc = bank(where)
-            for v0 in range(0, n, C):
+            width = min(n, C)
+            for v0 in range(0, n, width):
                 e = (s0 + v0) // C
                 nc.tensor.matmul_mx(
-                    out=acc[:, v0 : v0 + C],
+                    out=acc[:, v0 : v0 + width],
                     lhsT=w1_codes[:, e, :].bitcast(FP4X4),
                     lhsT_scale=w1_plane[:, K * e : K * (e + 1)],
-                    rhs=codes[:, s0 + v0 : s0 + v0 + C].bitcast(FP8X4),
-                    rhs_scale=plane[:, v0 : v0 + C],
+                    rhs=codes[:, s0 + v0 : s0 + v0 + width].bitcast(FP8X4),
+                    rhs_scale=plane[:, v0 : v0 + width],
                     start=True,
                     stop=True,
                 )
@@ -253,7 +254,8 @@ def tile_moe_sdb_relu_kernel(
         apply_mask(3, 0)
         apply_mask(3, C)
         experts(PARTS[3][0], C, da_slots(PARTS[3][0], C), 2, nc.vector.tensor_copy)
-        experts(PARTS[3][0] + C, C, da_slots(PARTS[3][0] + C, C), 3, nc.scalar.copy)
+        experts(S - C, P, da_slots(S - C, P), 3, nc.scalar.copy)
+        experts(S - P, P, da_slots(S - P, P), 5, nc.vector.tensor_copy)
 
         for h, (t0, n) in enumerate(TOKEN_RANGES):
             cols = slice(t0 // LIST_ROWS, (t0 + n) // LIST_ROWS)

@@ -25,11 +25,15 @@ FP4X4 = mybir.dt.float4_e2m1fn_x4
 ALU = mybir.AluOpType
 ACT = mybir.ActivationFunctionType
 
-GATED = 512
-PARTS = [(0, GATED), (512, 768), (1280, 512), (1792, 512)]
-TURNED = S - GATED
+BLOCKS = S // P
+FUSED = 3
+GATHERS = [(3, 4), (7, 4), (11, 3), (14, 2), (16, 2)]
+LOADS = [(0, 3), (3, 4), (7, 4), (11, 7)]
+MASKS = [(0, 3), (3, 8), (11, 7)]
+PAIRS = [(3, 2), (5, 2), (7, 1), (8, 2), (10, 2), (12, 2), (14, 2), (16, 2)]
+MOVED = 3
+STREAMED = 11
 RING = 4
-WINDOW = T + 32
 TOKEN_BANKS = [(0, 512), (512, 256)]
 FIRST_TOKEN_BANKS = [(0, 256), (256, 256), (512, 128), (640, 128)]
 TOKEN_RANGES = [(0, 480), (480, 288)]
@@ -45,30 +49,31 @@ def tile_moe_sdb_relu_kernel(
         placed = ctx.enter_context(tc.tile_pool(name="placed", bufs=1))
         psum = ctx.enter_context(tc.psum_pool(name="psum", bufs=1))
 
-        def bank(i):
-            return psum.tile([P, BANK], F32, name="bank%d" % i, tag="bank%d" % i)
+        def banks(name, first, count=1):
+            return psum.tile([P, count * BANK], F32, name=name, offset=4 * BANK * first)
 
-        def bf16_tile(name, tag, slots):
-            return keep.tile([P, PACK * slots], BF16, name=name, tag=tag, align_bytes=64)
+        def bf16_tile(name, tag, blocks):
+            return keep.tile([P, blocks * H], BF16, name=name, tag=tag, align_bytes=64)
 
-        def woven_view(tile):
-            return tile[:].rearrange("p (r i t) -> p r t i", i=RUN, t=PACK)
+        def woven_view(ap):
+            return ap.rearrange("p (r i t) -> p r t i", i=RUN, t=PACK)
 
-        def planar_view(tile):
-            return tile[:].rearrange("p (t r i) -> p r t i", i=RUN, t=PACK)
+        def planar_view(ap):
+            return ap.rearrange("p (t r i) -> p r t i", i=RUN, t=PACK)
+
+        def tokens(b0, n):
+            return offs_t[:, b0 * P // LIST_ROWS : (b0 + n) * P // LIST_ROWS]
 
         w2_plane_raw = keep.tile([P, H], U8, align_bytes=64)
         dy_plane = keep.tile([P, T], U8, align_bytes=64)
         w1_plane = keep.tile([P, E * K], U8, align_bytes=64)
+        gate_blocks = keep.tile([P, P], F32)
         nc.gpsimd.memset(w2_plane_raw[:].bitcast(I32), 0)
         nc.vector.memset(dy_plane[:].bitcast(I32), 0)
         nc.vector.memset(w1_plane[:].bitcast(I32), 0)
+        nc.gpsimd.memset(gate_blocks[:], 0.0)
         identity = keep.tile([P, P], F32)
         make_identity(nc, identity[:])
-        dc = []
-        for t in range(PACK):
-            dc.append(keep.tile([P, WINDOW], F32, name="dc%d" % t))
-            nc.gpsimd.memset(dc[t][:, T:], 0.0)
 
         def load_scale_rows(plane, scales, quadrants):
             for q in quadrants:
@@ -86,20 +91,20 @@ def tile_moe_sdb_relu_kernel(
         offs_t = keep.tile([P, S // LIST_ROWS], U16)
         nc.sync.dma_start(offs_t[:], offs)
 
-        border = 4 * PACK * TURNED
-        gate_rows = placed.tile([P, GATED], F32, name="gate_rows", offset=border - 2 * GATED, align_bytes=64)
-        nc.sync.dma_start(gate_rows[:], gate[:, :GATED])
+        plain_bytes = 4 * H * (BLOCKS - FUSED)
+        border = plain_bytes
+        codes_at = border + 2 * H * FUSED
+        gate_rows = placed.tile([P, FUSED * P], F32, name="gate_rows", offset=border - 2 * FUSED * P, align_bytes=64)
+        nc.sync.dma_start(gate_rows[:], gate[:, : FUSED * P])
         a_rows = a.rearrange("(p t) s -> p t s", t=PACK)
         a_t = []
-        for j, (s0, n) in enumerate(PARTS):
-            a_t.append(keep.tile([P, PACK * n], F32, name="a%d" % j, tag="a%d" % j, align_bytes=64))
-            nc.sync.dma_start(a_t[j][:].rearrange("p (t s) -> p t s", t=PACK), a_rows[:, :, s0 : s0 + n])
-        gate_cols = {}
-        with nc.allow_non_contiguous_dma(reason="one gate a partition"):
-            for j in range(1, len(PARTS)):
-                s0, n = PARTS[j]
-                gate_cols[j] = keep.tile([P, n // P], F32, name="gate_cols%d" % j, tag="cols%d" % j, align_bytes=64)
-                nc.sync.dma_start(gate_cols[j][:], gate[j, s0 : s0 + n].rearrange("(b p) -> p b", p=P))
+        for j, (b0, n) in enumerate(LOADS):
+            a_t.append(keep.tile([P, n * H], F32, name="a%d" % j, tag="a%d" % j, align_bytes=64))
+            nc.sync.dma_start(a_t[j][:].rearrange("p (t s) -> p t s", t=PACK), a_rows[:, :, b0 * P : (b0 + n) * P])
+            if j == 1:
+                nc.sync.dma_start(
+                    gate_blocks[: BLOCKS - FUSED, :], gate[0, FUSED * P :].rearrange("(b s) -> b s", s=P)
+                )
         w1_codes = keep.tile([P, E, 2 * K], U8, align_bytes=64)
         nc.sync.dma_start(w1_codes[:].bitcast(I32), w1t_words[:, 0].rearrange("e p b -> p e b").bitcast(I32))
         for q in range(QUADRANTS):
@@ -124,9 +129,10 @@ def tile_moe_sdb_relu_kernel(
                 w2_plane_raw[:].rearrange("p (m t) -> p t m", t=PACK)[:, ts, :],
             )
 
+        dc = [keep.tile([P, T], F32, name="dc%d" % t) for t in range(PACK)]
         products = [(t, t0, n) for t in range(PACK) for t0, n in (FIRST_TOKEN_BANKS if t == 0 else TOKEN_BANKS)]
         for x, (t, t0, n) in enumerate(products):
-            acc = bank(x % BANKS)
+            acc = banks("product%d" % x, x % BANKS)
             nc.tensor.matmul_mx(
                 out=acc[:, :n],
                 lhsT=w2_codes[:, 2 * P * t : 2 * P * (t + 1)].bitcast(FP4X4),
@@ -141,121 +147,150 @@ def tile_moe_sdb_relu_kernel(
             else:
                 nc.scalar.copy(dc[t][:, t0 : t0 + n], acc[:, :n])
 
-        gated = keep.tile([P, PACK * GATED], F32, name="gated", tag="gated", align_bytes=64)
-        plain = placed.tile([P, PACK * TURNED], F32, name="plain", offset=0, align_bytes=64)
-        for s0, n in PARTS:
-            tokens = offs_t[:, s0 // LIST_ROWS : (s0 + n) // LIST_ROWS]
+        gated = keep.tile([P, FUSED * H], F32, name="gated", align_bytes=64)
+        for t in range(PACK):
+            nc.vector.tensor_tensor(
+                gated[:, t * FUSED * P : (t + 1) * FUSED * P], dc[t][:].indirect(tokens(0, FUSED)), gate_rows[:], ALU.mult
+            )
+        plain = placed.tile([P, H * (BLOCKS - FUSED)], F32, name="plain", offset=0, align_bytes=64)
+
+        def plain_at(b0, n, t):
+            at = H * (b0 - FUSED) + t * n * P
+            return plain[:, at : at + n * P]
+
+        for b0, n in GATHERS:
             for t in range(PACK):
-                if s0 < GATED:
-                    nc.vector.tensor_tensor(
-                        gated[:, t * n : (t + 1) * n], dc[t][:].indirect(tokens), gate_rows[:], ALU.mult
-                    )
-                else:
-                    at = PACK * (s0 - GATED) + t * n
-                    nc.vector.tensor_copy(plain[:, at : at + n], dc[t][:].indirect(tokens))
+                nc.vector.tensor_copy(plain_at(b0, n, t), dc[t][:].indirect(tokens(b0, n)))
 
-        signs = {}
+        da = bf16_tile("da", "da", BLOCKS)
+        signs = [bf16_tile("signs%d" % m, "signs%d" % m, n) for m, (b0, n) in enumerate(MASKS)]
         mask = {}
-        back = []
+        back = {}
+        mask_rest = bf16_tile("mask_rest", "mask_rest", BLOCKS - FUSED)
 
-        def make_signs(j, tag):
-            signs[j] = bf16_tile("signs%d" % j, tag, PARTS[j][1])
-            nc.scalar.activation(woven_view(signs[j]), planar_view(a_t[j]), ACT.Sign)
+        def da_blocks(b0, n):
+            return da[:, b0 * H : (b0 + n) * H]
 
-        def clip(j, tile):
-            mask[j] = tile
-            nc.gpsimd.tensor_scalar(mask[j][:], signs[j][:], 1.0, 0.0, ALU.min, ALU.max)
+        def mask_blocks(b0, n):
+            return mask_rest[:, (b0 - FUSED) * H : (b0 - FUSED + n) * H]
+
+        def make_signs(j, m):
+            b0, n = LOADS[j]
+            at = (b0 - MASKS[m][0]) * H
+            nc.scalar.activation(woven_view(signs[m][:, at : at + n * H]), planar_view(a_t[j][:]), ACT.Sign)
+
+        def clip(m, tile):
+            mask[MASKS[m][0]] = tile
+            nc.gpsimd.tensor_scalar(tile, signs[m][:], 1.0, 0.0, ALU.min, ALU.max)
 
         def turn(j, tag):
-            s0, n = PARTS[j]
+            b0, n = GATHERS[j]
+            if b0 < STREAMED:
+                whole = banks("forth%d" % b0, 0, n)
+                forth = [whole[:, b * BANK : (b + 1) * BANK] for b in range(n)]
+                steps = [(b, t) for t in range(PACK) for b in range(n)]
+            else:
+                forth = [banks("forth%d" % b, (b - STREAMED) % RING)[:] for b in range(b0, b0 + n)]
+                steps = [(b, t) for b in range(n) for t in range(PACK)]
+            for b, t in steps:
+                nc.tensor.transpose(
+                    forth[b][:, t * P : (t + 1) * P], plain_at(b0, n, t)[:, b * P : (b + 1) * P], identity[:]
+                )
             turned = bf16_tile("turned%d" % j, tag, n)
             words = turned[:].bitcast(F32)
-            for b in range(n // P):
-                acc = bank(b % RING)
-                for t in range(PACK):
-                    at = PACK * (s0 - GATED) + t * n + b * P
-                    nc.tensor.transpose(acc[:, t * P : (t + 1) * P], plain[:, at : at + P], identity[:])
+            for b in range(n):
                 nc.scalar.activation(
                     turned[:, b * H : (b + 1) * H].rearrange("s (u p e) -> s u p e", u=2, e=2),
-                    acc[:].rearrange("s (u e p) -> s u p e", u=2, e=2),
+                    forth[b].rearrange("s (u e p) -> s u p e", u=2, e=2),
                     ACT.Copy,
-                    scale=gate_cols[j][:, b : b + 1],
+                    scale=gate_cols[:, b0 + b - FUSED : b0 + b - FUSED + 1],
                 )
-            for b in range(n // P):
-                if b % 2 == 0:
-                    back.append(bank(RING + len(back) % RING))
+            for b in range(n):
+                x = max(x for x, (p0, m) in enumerate(PAIRS) if p0 <= b0 + b)
+                place = b0 + b - PAIRS[x][0]
+                if place == 0:
+                    back[x] = banks("back%d" % x, RING + x % RING)
                 for u in range(2):
                     nc.tensor.transpose(
-                        back[-1][:, b % 2 * C + u : (b % 2 + 1) * C : 2],
+                        back[x][:, place * C + u : (place + 1) * C : 2],
                         words[:, (2 * b + u) * P : (2 * b + u + 1) * P],
                         identity[:],
                     )
 
-        make_signs(0, "signs0")
-        clip(0, placed.tile([P, PACK * GATED], BF16, name="mask0", offset=border, align_bytes=64))
-        woven = bf16_tile("woven", "a0", GATED)
-        nc.scalar.copy(woven_view(woven), planar_view(gated))
-        da_first = bf16_tile("da_first", "signs0", GATED)
-        nc.gpsimd.tensor_tensor(da_first[:], woven[:], mask[0][:], ALU.mult)
-        make_signs(1, "gated")
-        clip(1, bf16_tile("mask1", "a0", PARTS[1][1]))
-        make_signs(2, "signs2")
-        clip(2, bf16_tile("mask2", "gated", PARTS[2][1]))
-        turn(1, "a2")
-        moved = bf16_tile("moved", "moved", C)
-        nc.scalar.copy(moved[:], back[0][:].bitcast(BF16))
-        da_moved = bf16_tile("da_moved", "signs2", C)
-        nc.gpsimd.tensor_tensor(da_moved[:], moved[:], mask[1][:, : PACK * C], ALU.mult)
-        make_signs(3, "cols1")
-        clip(3, bf16_tile("mask3", "moved", PARTS[3][1]))
-        turn(2, "a3")
-        turn(3, "turned3")
+        def move(x, tile, at):
+            n = PAIRS[x][1]
+            nc.scalar.copy(tile[:, at * H : (at + n) * H].bitcast(F32), back[x][:, : n * C])
 
-        dx = keep.tile([P, S], F32, name="dx", tag="cols3", align_bytes=64)
-        codes = keep.tile([P, S], U32, name="codes", tag="cols1", align_bytes=64)
-        da = bf16_tile("da", "da", TURNED - C)
+        def mask_moved(b0, n, tile):
+            nc.gpsimd.tensor_tensor(da_blocks(b0, n), tile[:], mask_blocks(b0, n), ALU.mult)
 
-        def da_slots(s0, n):
-            return da[:, PACK * (s0 - GATED - C) : PACK * (s0 + n - GATED - C)]
-
-        def apply_mask(j, v0):
-            s0 = PARTS[j][0] + v0
+        def mask_bank(x):
+            b0, n = PAIRS[x]
             nc.vector.tensor_tensor(
-                da_slots(s0, C),
-                back[(s0 - GATED) // C][:].bitcast(BF16),
-                mask[j][:, PACK * v0 : PACK * (v0 + C)],
-                ALU.mult,
+                da_blocks(b0, n), back[x][:, : n * C].bitcast(BF16), mask_blocks(b0, n), ALU.mult
             )
 
-        def experts(s0, n, values, where, empty):
-            plane = keep.tile([P, n], U8, name="plane%d" % s0, align_bytes=64)
-            nc.vector.quantize_mx(out=codes[:, s0 : s0 + n].bitcast(FP8X4), scales=plane[:], in_=values)
-            acc = bank(where)
-            width = min(n, C)
-            for v0 in range(0, n, width):
-                e = (s0 + v0) // C
+        make_signs(0, 0)
+        clip(0, placed.tile([P, FUSED * H], BF16, name="mask0", offset=border, align_bytes=64)[:])
+        nc.gpsimd.tensor_tensor(
+            da_blocks(0, FUSED).rearrange("p (s t) -> p s t", t=PACK),
+            gated[:].rearrange("p (t s) -> p s t", t=PACK),
+            mask[0].rearrange("p (s t) -> p s t", t=PACK),
+            ALU.mult,
+        )
+        make_signs(1, 1)
+        gates_turned = banks("gates_turned", BANKS - 1)
+        nc.tensor.transpose(gates_turned[:, :P], gate_blocks[:], identity[:])
+        gate_cols = keep.tile([P, BLOCKS - FUSED], F32, name="gate_cols", tag="gate_cols", align_bytes=64)
+        nc.scalar.copy(gate_cols[:], gates_turned[:, : BLOCKS - FUSED])
+        make_signs(2, 1)
+        clip(1, mask_rest[:, : MASKS[1][1] * H])
+        turn(0, "a2")
+        moved_first = bf16_tile("moved_first", "moved_first", 2)
+        move(0, moved_first, 0)
+        mask_moved(3, 2, moved_first)
+        moved_last = placed.tile([P, 3 * H], BF16, name="moved_last", offset=codes_at, align_bytes=64)
+        move(1, moved_last, 0)
+        make_signs(3, 2)
+        clip(2, mask_rest[:, MASKS[1][1] * H :])
+        turn(1, "a3")
+        move(2, moved_last, 2)
+        mask_moved(5, 3, moved_last)
+        turn(2, "turned2")
+        turn(3, "turned3")
+        turn(4, "turned4")
+
+        dx = keep.tile([P, S], F32, name="dx", tag="gate_cols", align_bytes=64)
+        codes = placed.tile([P, S], U32, name="codes", offset=codes_at, align_bytes=64)
+        plane = keep.tile([P, S], U8, name="plane", align_bytes=64)
+
+        def experts(b0, n, where, empty):
+            s0, s1 = b0 * P, (b0 + n) * P
+            nc.vector.quantize_mx(out=codes[:, s0:s1].bitcast(FP8X4), scales=plane[:, s0:s1], in_=da_blocks(b0, n))
+            acc = banks("sums%d" % b0, where)
+            width = min(n * P, C)
+            for v0 in range(s0, s1, width):
+                e = v0 // C
                 nc.tensor.matmul_mx(
-                    out=acc[:, v0 : v0 + width],
+                    out=acc[:, v0 - s0 : v0 - s0 + width],
                     lhsT=w1_codes[:, e, :].bitcast(FP4X4),
                     lhsT_scale=w1_plane[:, K * e : K * (e + 1)],
-                    rhs=codes[:, s0 + v0 : s0 + v0 + width].bitcast(FP8X4),
+                    rhs=codes[:, v0 : v0 + width].bitcast(FP8X4),
                     rhs_scale=plane[:, v0 : v0 + width],
                     start=True,
                     stop=True,
                 )
-            empty(dx[:, s0 : s0 + n], acc[:, :n])
+            empty(dx[:, s0:s1], acc[:, : n * P])
 
-        for j, v0 in ((1, C), (1, 2 * C), (2, 0), (2, C)):
-            apply_mask(j, v0)
-        experts(0, GATED, da_first[:], 7, nc.scalar.copy)
-        experts(GATED, C, da_moved[:], 4, nc.scalar.copy)
-        experts(GATED + C, 2 * C, da_slots(GATED + C, 2 * C), 0, nc.scalar.copy)
-        experts(PARTS[2][0], PARTS[2][1], da_slots(*PARTS[2]), 1, nc.scalar.copy)
-        apply_mask(3, 0)
-        apply_mask(3, C)
-        experts(PARTS[3][0], C, da_slots(PARTS[3][0], C), 2, nc.vector.tensor_copy)
-        experts(S - C, P, da_slots(S - C, P), 3, nc.scalar.copy)
-        experts(S - P, P, da_slots(S - P, P), 5, nc.vector.tensor_copy)
+        for x in range(MOVED, len(PAIRS) - 1):
+            mask_bank(x)
+        experts(0, 4, 4, nc.scalar.copy)
+        experts(4, 4, 5, nc.scalar.copy)
+        mask_bank(len(PAIRS) - 1)
+        experts(8, 4, 3, nc.scalar.copy)
+        experts(12, 4, 0, nc.scalar.copy)
+        experts(16, 1, 6, nc.vector.tensor_copy)
+        experts(17, 1, 1, nc.vector.tensor_copy)
 
         for h, (t0, n) in enumerate(TOKEN_RANGES):
             cols = slice(t0 // LIST_ROWS, (t0 + n) // LIST_ROWS)

@@ -26,17 +26,17 @@ ALU = mybir.AluOpType
 ACT = mybir.ActivationFunctionType
 
 BLOCKS = S // P
-FUSED = 3
-GATHERS = [(3, 4), (7, 4), (11, 3), (14, 2), (16, 2)]
-LOADS = [(0, 3), (3, 4), (7, 4), (11, 7)]
-MASKS = [(0, 3), (3, 8), (11, 7)]
-PAIRS = [(3, 2), (5, 2), (7, 1), (8, 2), (10, 2), (12, 2), (14, 2), (16, 2)]
+FUSED = 4
+GATHERS = [(4, 4), (8, 2), (10, 2), (12, 2), (14, 2), (16, 2)]
+LOADS = [(0, 2), (2, 2), (4, 4), (8, 4), (12, 2), (14, 2), (16, 2)]
+MASKS = [(0, 4), (4, 8), (12, 4), (16, 2)]
+PAIRS = [(4, 2), (6, 2), (8, 2), (10, 2), (12, 2), (14, 2), (16, 2)]
 MOVED = 3
-STREAMED = 11
 RING = 4
 TOKEN_BANKS = [(0, 512), (512, 256)]
 FIRST_TOKEN_BANKS = [(0, 256), (256, 256), (512, 128), (640, 128)]
 TOKEN_RANGES = [(0, 480), (480, 288)]
+STORE_RANGES = [(0, 384), (384, 256), (640, 128)]
 
 
 def tile_moe_sdb_relu_kernel(
@@ -68,7 +68,7 @@ def tile_moe_sdb_relu_kernel(
         dy_plane = keep.tile([P, T], U8, align_bytes=64)
         w1_plane = keep.tile([P, E * K], U8, align_bytes=64)
         gate_blocks = keep.tile([P, P], F32)
-        nc.gpsimd.memset(w2_plane_raw[:].bitcast(I32), 0)
+        nc.gpsimd.memset(w2_plane_raw[P // 2 :, :].bitcast(I32), 0)
         nc.vector.memset(dy_plane[:].bitcast(I32), 0)
         nc.vector.memset(w1_plane[:].bitcast(I32), 0)
         nc.gpsimd.memset(gate_blocks[:], 0.0)
@@ -82,7 +82,11 @@ def tile_moe_sdb_relu_kernel(
                 )
 
         w2_raw = keep.tile([P, 2 * H], U8, align_bytes=64)
-        load_scale_rows(w2_plane_raw, w2t_scales, range(2))
+        for q in range(2):
+            nc.sync.dma_start(
+                w2_plane_raw[32 * q : 32 * (q + 1), :].bitcast(I32),
+                w2t_scales[0, 4 * q : 4 * q + 4, :].bitcast(I32).partition_broadcast(8),
+            )
         nc.sync.dma_start(w2_raw[:].bitcast(I32), w2t_words[0].bitcast(I32))
         load_scale_rows(w2_plane_raw, w2t_scales, range(2, QUADRANTS))
         dy_codes = keep.tile([P, 4 * T], U8, align_bytes=64)
@@ -94,12 +98,15 @@ def tile_moe_sdb_relu_kernel(
         plain_bytes = 4 * H * (BLOCKS - FUSED)
         border = plain_bytes
         codes_at = border + 2 * H * FUSED
-        gate_rows = placed.tile([P, FUSED * P], F32, name="gate_rows", offset=border - 2 * FUSED * P, align_bytes=64)
+        gate_rows = placed.tile([P, FUSED * P], F32, name="gate_rows", offset=border, align_bytes=64)
         nc.sync.dma_start(gate_rows[:], gate[:, : FUSED * P])
         a_rows = a.rearrange("(p t) s -> p t s", t=PACK)
         a_t = []
         for j, (b0, n) in enumerate(LOADS):
-            a_t.append(keep.tile([P, n * H], F32, name="a%d" % j, tag="a%d" % j, align_bytes=64))
+            if j == 0:
+                a_t.append(placed.tile([P, n * H], F32, name="a0", offset=0, align_bytes=64))
+            else:
+                a_t.append(keep.tile([P, n * H], F32, name="a%d" % j, tag="a%d" % j, align_bytes=64))
             nc.sync.dma_start(a_t[j][:].rearrange("p (t s) -> p t s", t=PACK), a_rows[:, :, b0 * P : (b0 + n) * P])
             if j == 1:
                 nc.sync.dma_start(
@@ -162,17 +169,23 @@ def tile_moe_sdb_relu_kernel(
             for t in range(PACK):
                 nc.vector.tensor_copy(plain_at(b0, n, t), dc[t][:].indirect(tokens(b0, n)))
 
-        da = bf16_tile("da", "da", BLOCKS)
+        da_first = bf16_tile("da_first", "da_first", FUSED)
+        da = bf16_tile("da", "da", BLOCKS - FUSED - 2)
+        da_last = bf16_tile("da_last", "da_first", 2)
         signs = [bf16_tile("signs%d" % m, "signs%d" % m, n) for m, (b0, n) in enumerate(MASKS)]
         mask = {}
         back = {}
-        mask_rest = bf16_tile("mask_rest", "mask_rest", BLOCKS - FUSED)
 
         def da_blocks(b0, n):
-            return da[:, b0 * H : (b0 + n) * H]
+            if b0 < FUSED:
+                return da_first[:, b0 * H : (b0 + n) * H]
+            if b0 >= BLOCKS - 2:
+                return da_last[:, (b0 - BLOCKS + 2) * H : (b0 - BLOCKS + 2 + n) * H]
+            return da[:, (b0 - FUSED) * H : (b0 - FUSED + n) * H]
 
         def mask_blocks(b0, n):
-            return mask_rest[:, (b0 - FUSED) * H : (b0 - FUSED + n) * H]
+            m0 = max(m for m in mask if m <= b0)
+            return mask[m0][:, (b0 - m0) * H : (b0 - m0 + n) * H]
 
         def make_signs(j, m):
             b0, n = LOADS[j]
@@ -183,54 +196,56 @@ def tile_moe_sdb_relu_kernel(
             mask[MASKS[m][0]] = tile
             nc.gpsimd.tensor_scalar(tile, signs[m][:], 1.0, 0.0, ALU.min, ALU.max)
 
-        def turn(j, tag):
+        forth = {}
+
+        def turn_forth(j):
             b0, n = GATHERS[j]
-            if b0 < STREAMED:
-                whole = banks("forth%d" % b0, 0, n)
-                forth = [whole[:, b * BANK : (b + 1) * BANK] for b in range(n)]
-                steps = [(b, t) for t in range(PACK) for b in range(n)]
-            else:
-                forth = [banks("forth%d" % b, (b - STREAMED) % RING)[:] for b in range(b0, b0 + n)]
-                steps = [(b, t) for b in range(n) for t in range(PACK)]
-            for b, t in steps:
-                nc.tensor.transpose(
-                    forth[b][:, t * P : (t + 1) * P], plain_at(b0, n, t)[:, b * P : (b + 1) * P], identity[:]
-                )
-            turned = bf16_tile("turned%d" % j, tag, n)
-            words = turned[:].bitcast(F32)
-            for b in range(n):
+            for x in range((b0 - FUSED) // 2, (b0 + n - FUSED) // 2):
+                forth[x] = banks("forth%d" % x, 2 * (x % 2), 2)
+            for t in range(PACK):
+                for b in range(n):
+                    x, place = divmod(b0 + b - FUSED, 2)
+                    at = place * BANK + t * P
+                    nc.tensor.transpose(
+                        forth[x][:, at : at + P], plain_at(b0, n, t)[:, b * P : (b + 1) * P], identity[:]
+                    )
+
+        def gate_pair(x, turned):
+            words = turned.bitcast(F32)
+            back[x] = banks("back%d" % x, RING + x % RING)
+            for place in range(2):
                 nc.scalar.activation(
-                    turned[:, b * H : (b + 1) * H].rearrange("s (u p e) -> s u p e", u=2, e=2),
-                    forth[b].rearrange("s (u e p) -> s u p e", u=2, e=2),
+                    turned[:, place * H : (place + 1) * H].rearrange("s (u p e) -> s u p e", u=2, e=2),
+                    forth[x][:, place * BANK : (place + 1) * BANK].rearrange("s (u e p) -> s u p e", u=2, e=2),
                     ACT.Copy,
-                    scale=gate_cols[:, b0 + b - FUSED : b0 + b - FUSED + 1],
+                    scale=gate_cols[:, 2 * x + place : 2 * x + place + 1],
                 )
-            for b in range(n):
-                x = max(x for x, (p0, m) in enumerate(PAIRS) if p0 <= b0 + b)
-                place = b0 + b - PAIRS[x][0]
-                if place == 0:
-                    back[x] = banks("back%d" % x, RING + x % RING)
+            for place in range(2):
                 for u in range(2):
                     nc.tensor.transpose(
                         back[x][:, place * C + u : (place + 1) * C : 2],
-                        words[:, (2 * b + u) * P : (2 * b + u + 1) * P],
+                        words[:, (2 * place + u) * P : (2 * place + u + 1) * P],
                         identity[:],
                     )
 
-        def move(x, tile, at):
-            n = PAIRS[x][1]
+        def move(x, n, tile, at):
             nc.scalar.copy(tile[:, at * H : (at + n) * H].bitcast(F32), back[x][:, : n * C])
 
         def mask_moved(b0, n, tile):
             nc.gpsimd.tensor_tensor(da_blocks(b0, n), tile[:], mask_blocks(b0, n), ALU.mult)
 
-        def mask_bank(x):
-            b0, n = PAIRS[x]
+        def mask_bank(x, place=0):
+            b0, n = PAIRS[x][0] + place, PAIRS[x][1] - place
             nc.vector.tensor_tensor(
-                da_blocks(b0, n), back[x][:, : n * C].bitcast(BF16), mask_blocks(b0, n), ALU.mult
+                da_blocks(b0, n), back[x][:, place * C : (place + n) * C].bitcast(BF16), mask_blocks(b0, n), ALU.mult
             )
 
+        gates_turned = banks("gates_turned", 2)
+        nc.tensor.transpose(gates_turned[:, :P], gate_blocks[:], identity[:])
+        gate_cols = keep.tile([P, BLOCKS - FUSED], F32, name="gate_cols", tag="gate_cols", align_bytes=64)
+        nc.scalar.copy(gate_cols[:], gates_turned[:, : BLOCKS - FUSED])
         make_signs(0, 0)
+        make_signs(1, 0)
         clip(0, placed.tile([P, FUSED * H], BF16, name="mask0", offset=border, align_bytes=64)[:])
         nc.gpsimd.tensor_tensor(
             da_blocks(0, FUSED).rearrange("p (s t) -> p s t", t=PACK),
@@ -238,35 +253,42 @@ def tile_moe_sdb_relu_kernel(
             mask[0].rearrange("p (s t) -> p s t", t=PACK),
             ALU.mult,
         )
-        make_signs(1, 1)
-        gates_turned = banks("gates_turned", BANKS - 1)
-        nc.tensor.transpose(gates_turned[:, :P], gate_blocks[:], identity[:])
-        gate_cols = keep.tile([P, BLOCKS - FUSED], F32, name="gate_cols", tag="gate_cols", align_bytes=64)
-        nc.scalar.copy(gate_cols[:], gates_turned[:, : BLOCKS - FUSED])
         make_signs(2, 1)
-        clip(1, mask_rest[:, : MASKS[1][1] * H])
-        turn(0, "a2")
-        moved_first = bf16_tile("moved_first", "moved_first", 2)
-        move(0, moved_first, 0)
-        mask_moved(3, 2, moved_first)
-        moved_last = placed.tile([P, 3 * H], BF16, name="moved_last", offset=codes_at, align_bytes=64)
-        move(1, moved_last, 0)
-        make_signs(3, 2)
-        clip(2, mask_rest[:, MASKS[1][1] * H :])
-        turn(1, "a3")
-        move(2, moved_last, 2)
-        mask_moved(5, 3, moved_last)
-        turn(2, "turned2")
-        turn(3, "turned3")
-        turn(4, "turned4")
+        make_signs(3, 1)
+        clip(1, bf16_tile("mask1", "mask1", MASKS[1][1])[:])
+        make_signs(4, 2)
+        turn_forth(0)
+        turned_first = bf16_tile("turned_first", "a3", 4)
+        gate_pair(0, turned_first[:, : 2 * H])
+        gate_pair(1, turned_first[:, 2 * H :])
+        turn_forth(1)
+        gate_pair(2, bf16_tile("turned2", "turned2", 2)[:])
+        make_signs(5, 2)
+        at = codes_at + 2 * MOVED * H
+        clip(2, placed.tile([P, MASKS[2][1] * H], BF16, name="mask2", offset=at, align_bytes=64)[:])
+        turn_forth(2)
+        gate_pair(3, bf16_tile("turned3", "turned3", 2)[:])
+        moved = placed.tile([P, MOVED * H], BF16, name="moved", offset=codes_at, align_bytes=64)
+        move(0, 2, moved, 0)
+        move(1, 1, moved, 2)
+        mask_moved(FUSED, MOVED, moved)
+        turn_forth(3)
+        gate_pair(4, bf16_tile("turned4", "turned4", 2)[:])
+        make_signs(6, 3)
+        turn_forth(4)
+        gate_pair(5, bf16_tile("turned5", "turned5", 2)[:])
+        mask[MASKS[3][0]] = bf16_tile("mask3", "mask3", MASKS[3][1])[:]
+        nc.scalar.activation(mask_blocks(*MASKS[3]), signs[3][:], ACT.Relu)
+        turn_forth(5)
+        gate_pair(6, bf16_tile("turned6", "turned6", 2)[:])
 
         dx = keep.tile([P, S], F32, name="dx", tag="gate_cols", align_bytes=64)
         codes = placed.tile([P, S], U32, name="codes", offset=codes_at, align_bytes=64)
-        plane = keep.tile([P, S], U8, name="plane", align_bytes=64)
 
         def experts(b0, n, where, empty):
             s0, s1 = b0 * P, (b0 + n) * P
-            nc.vector.quantize_mx(out=codes[:, s0:s1].bitcast(FP8X4), scales=plane[:, s0:s1], in_=da_blocks(b0, n))
+            plane = keep.tile([P, n * P], U8, name="plane%d" % b0, align_bytes=64)
+            nc.vector.quantize_mx(out=codes[:, s0:s1].bitcast(FP8X4), scales=plane[:], in_=da_blocks(b0, n))
             acc = banks("sums%d" % b0, where)
             width = min(n * P, C)
             for v0 in range(s0, s1, width):
@@ -276,28 +298,31 @@ def tile_moe_sdb_relu_kernel(
                     lhsT=w1_codes[:, e, :].bitcast(FP4X4),
                     lhsT_scale=w1_plane[:, K * e : K * (e + 1)],
                     rhs=codes[:, v0 : v0 + width].bitcast(FP8X4),
-                    rhs_scale=plane[:, v0 : v0 + width],
+                    rhs_scale=plane[:, v0 - s0 : v0 - s0 + width],
                     start=True,
                     stop=True,
                 )
             empty(dx[:, s0:s1], acc[:, : n * P])
 
-        for x in range(MOVED, len(PAIRS) - 1):
+        mask_bank(1, 1)
+        for x in range(2, len(PAIRS) - 1):
             mask_bank(x)
-        experts(0, 4, 4, nc.scalar.copy)
-        experts(4, 4, 5, nc.scalar.copy)
+        experts(0, 4, 5, nc.scalar.copy)
+        experts(4, 4, 4, nc.scalar.copy)
         mask_bank(len(PAIRS) - 1)
-        experts(8, 4, 3, nc.scalar.copy)
-        experts(12, 4, 0, nc.scalar.copy)
-        experts(16, 1, 6, nc.vector.tensor_copy)
-        experts(17, 1, 1, nc.vector.tensor_copy)
+        experts(8, 4, 7, nc.scalar.copy)
+        experts(12, 4, 2, nc.scalar.copy)
+        experts(16, 1, 3, nc.vector.tensor_copy)
+        experts(17, 1, 0, nc.vector.tensor_copy)
 
+        second = keep.tile([P, T], F32, name="second")
         for h, (t0, n) in enumerate(TOKEN_RANGES):
             cols = slice(t0 // LIST_ROWS, (t0 + n) // LIST_ROWS)
             first = keep.tile([P, n], F32, name="first%d" % h)
             nc.vector.tensor_copy(first[:], dx[:].indirect(pos_t[0][:, cols]))
-            second = keep.tile([P, n], F32, name="second%d" % h)
-            nc.vector.tensor_tensor(second[:], dx[:].indirect(pos_t[1][:, cols]), first[:], ALU.add)
+            nc.vector.tensor_tensor(second[:, t0 : t0 + n], dx[:].indirect(pos_t[1][:, cols]), first[:], ALU.add)
+        for h, (t0, n) in enumerate(STORE_RANGES):
+            cols = slice(t0 // LIST_ROWS, (t0 + n) // LIST_ROWS)
             third = keep.tile([P, n], F32, name="third%d" % h)
-            nc.vector.tensor_tensor(third[:], dx[:].indirect(pos_t[2][:, cols]), second[:], ALU.add)
+            nc.vector.tensor_tensor(third[:], dx[:].indirect(pos_t[2][:, cols]), second[:, t0 : t0 + n], ALU.add)
             nc.sync.dma_start(out[:, t0 : t0 + n], third[:])

@@ -27,7 +27,7 @@ ACT = mybir.ActivationFunctionType
 
 BLOCKS = S // P
 FUSED = 4
-GATHERS = [(4, 4), (8, 2), (10, 2), (12, 2), (14, 2), (16, 2)]
+GATHERS = [(4, 4), (8, 4), (12, 2), (14, 2), (16, 2)]
 LOADS = [(0, 2), (2, 2), (4, 4), (8, 4), (12, 2), (14, 2), (16, 2)]
 MASKS = [(0, 4), (4, 8), (12, 4), (16, 2)]
 PAIRS = [(4, 2), (6, 2), (8, 2), (10, 2), (12, 2), (14, 2), (16, 2)]
@@ -170,17 +170,19 @@ def tile_moe_sdb_relu_kernel(
                 nc.vector.tensor_copy(plain_at(b0, n, t), dc[t][:].indirect(tokens(b0, n)))
 
         da_first = bf16_tile("da_first", "da_first", FUSED)
-        da = bf16_tile("da", "da", BLOCKS - FUSED - 2)
-        da_last = bf16_tile("da_last", "da_first", 2)
-        signs = [bf16_tile("signs%d" % m, "signs%d" % m, n) for m, (b0, n) in enumerate(MASKS)]
+        da = bf16_tile("da", "da", BLOCKS - 2 * FUSED)
+        da_last = bf16_tile("da_last", "da_first", FUSED)
+        signs = [bf16_tile("signs%d" % m, "signs%d" % m, n) for m, (b0, n) in enumerate(MASKS[:-1])]
+        at = codes_at + 2 * (MOVED + 2) * H
+        signs.append(placed.tile([P, MASKS[-1][1] * H], BF16, name="signs3", offset=at, align_bytes=64))
         mask = {}
         back = {}
 
         def da_blocks(b0, n):
             if b0 < FUSED:
                 return da_first[:, b0 * H : (b0 + n) * H]
-            if b0 >= BLOCKS - 2:
-                return da_last[:, (b0 - BLOCKS + 2) * H : (b0 - BLOCKS + 2 + n) * H]
+            if b0 >= BLOCKS - FUSED:
+                return da_last[:, (b0 - BLOCKS + FUSED) * H : (b0 - BLOCKS + FUSED + n) * H]
             return da[:, (b0 - FUSED) * H : (b0 - FUSED + n) * H]
 
         def mask_blocks(b0, n):
@@ -200,8 +202,12 @@ def tile_moe_sdb_relu_kernel(
 
         def turn_forth(j):
             b0, n = GATHERS[j]
-            for x in range((b0 - FUSED) // 2, (b0 + n - FUSED) // 2):
-                forth[x] = banks("forth%d" % x, 2 * (x % 2), 2)
+            if j == 0:
+                whole = banks("forth", 0, RING)
+                forth[0], forth[1] = whole[:, : 2 * BANK], whole[:, 2 * BANK :]
+            else:
+                for x in range((b0 - FUSED) // 2, (b0 + n - FUSED) // 2):
+                    forth[x] = banks("forth%d" % x, 2 * (x % 2), 2)[:]
             for t in range(PACK):
                 for b in range(n):
                     x, place = divmod(b0 + b - FUSED, 2)
@@ -261,34 +267,37 @@ def tile_moe_sdb_relu_kernel(
         turned_first = bf16_tile("turned_first", "a3", 4)
         gate_pair(0, turned_first[:, : 2 * H])
         gate_pair(1, turned_first[:, 2 * H :])
-        turn_forth(1)
-        gate_pair(2, bf16_tile("turned2", "turned2", 2)[:])
         make_signs(5, 2)
-        at = codes_at + 2 * MOVED * H
-        clip(2, placed.tile([P, MASKS[2][1] * H], BF16, name="mask2", offset=at, align_bytes=64)[:])
-        turn_forth(2)
-        gate_pair(3, bf16_tile("turned3", "turned3", 2)[:])
+        clip(2, bf16_tile("mask2", "mask2", MASKS[2][1])[:])
         moved = placed.tile([P, MOVED * H], BF16, name="moved", offset=codes_at, align_bytes=64)
         move(0, 2, moved, 0)
         move(1, 1, moved, 2)
         mask_moved(FUSED, MOVED, moved)
-        turn_forth(3)
+        turn_forth(1)
+        gate_pair(2, bf16_tile("turned2", "turned2", 2)[:])
+        gate_pair(3, bf16_tile("turned3", "turned3", 2)[:])
+        turn_forth(2)
         gate_pair(4, bf16_tile("turned4", "turned4", 2)[:])
         make_signs(6, 3)
-        turn_forth(4)
-        gate_pair(5, bf16_tile("turned5", "turned5", 2)[:])
+        turn_forth(3)
+        at = codes_at + 2 * MOVED * H
+        gate_pair(5, placed.tile([P, 2 * H], BF16, name="turned5", offset=at, align_bytes=64)[:])
         mask[MASKS[3][0]] = bf16_tile("mask3", "mask3", MASKS[3][1])[:]
         nc.scalar.activation(mask_blocks(*MASKS[3]), signs[3][:], ACT.Relu)
-        turn_forth(5)
+        turn_forth(4)
         gate_pair(6, bf16_tile("turned6", "turned6", 2)[:])
 
         dx = keep.tile([P, S], F32, name="dx", tag="gate_cols", align_bytes=64)
         codes = placed.tile([P, S], U32, name="codes", offset=codes_at, align_bytes=64)
 
+        plane = keep.tile([P, S], U8, name="plane", align_bytes=64)
+
+        def quantise(b0, n):
+            s0, s1 = b0 * P, (b0 + n) * P
+            nc.vector.quantize_mx(out=codes[:, s0:s1].bitcast(FP8X4), scales=plane[:, s0:s1], in_=da_blocks(b0, n))
+
         def experts(b0, n, where, empty):
             s0, s1 = b0 * P, (b0 + n) * P
-            plane = keep.tile([P, n * P], U8, name="plane%d" % b0, align_bytes=64)
-            nc.vector.quantize_mx(out=codes[:, s0:s1].bitcast(FP8X4), scales=plane[:], in_=da_blocks(b0, n))
             acc = banks("sums%d" % b0, where)
             width = min(n * P, C)
             for v0 in range(s0, s1, width):
@@ -298,22 +307,31 @@ def tile_moe_sdb_relu_kernel(
                     lhsT=w1_codes[:, e, :].bitcast(FP4X4),
                     lhsT_scale=w1_plane[:, K * e : K * (e + 1)],
                     rhs=codes[:, v0 : v0 + width].bitcast(FP8X4),
-                    rhs_scale=plane[:, v0 - s0 : v0 - s0 + width],
+                    rhs_scale=plane[:, v0 : v0 + width],
                     start=True,
                     stop=True,
                 )
             empty(dx[:, s0:s1], acc[:, : n * P])
 
         mask_bank(1, 1)
-        for x in range(2, len(PAIRS) - 1):
+        for x in (2, 3, 4):
             mask_bank(x)
-        experts(0, 4, 5, nc.scalar.copy)
-        experts(4, 4, 4, nc.scalar.copy)
-        mask_bank(len(PAIRS) - 1)
-        experts(8, 4, 7, nc.scalar.copy)
-        experts(12, 4, 2, nc.scalar.copy)
-        experts(16, 1, 3, nc.vector.tensor_copy)
-        experts(17, 1, 0, nc.vector.tensor_copy)
+        quantise(0, 4)
+        experts(0, 4, 0, nc.scalar.copy)
+        quantise(4, 4)
+        experts(4, 4, 1, nc.scalar.copy)
+        mask_bank(5)
+        quantise(8, 4)
+        experts(8, 4, 2, nc.scalar.copy)
+        quantise(12, 2)
+        experts(12, 2, 3, nc.scalar.copy)
+        mask_bank(6)
+        quantise(14, 2)
+        experts(14, 2, 6, nc.scalar.copy)
+        quantise(16, 1)
+        experts(16, 1, 4, nc.vector.tensor_copy)
+        quantise(17, 1)
+        experts(17, 1, 5, nc.vector.tensor_copy)
 
         second = keep.tile([P, T], F32, name="second")
         for h, (t0, n) in enumerate(TOKEN_RANGES):

@@ -149,7 +149,7 @@ def tile_moe_sdb_relu_kernel(
                 start=True,
                 stop=True,
             )
-            if t == 0 and x != 1:
+            if t == 0 and x % 2 == 0:
                 nc.vector.tensor_copy(dc[t][:, t0 : t0 + n], acc[:, :n])
             else:
                 nc.scalar.copy(dc[t][:, t0 : t0 + n], acc[:, :n])
@@ -331,7 +331,7 @@ def tile_moe_sdb_relu_kernel(
         quantise(16, 1)
         experts(16, 1, 4, nc.vector.tensor_copy)
         quantise(17, 1)
-        experts(17, 1, 5, nc.vector.tensor_copy)
+        experts(17, 1, 5, nc.scalar.copy)
 
         second = keep.tile([P, T], F32, name="second")
         for h, (t0, n) in enumerate(TOKEN_RANGES):

@@ -27,12 +27,16 @@ ACT = mybir.ActivationFunctionType
 
 BLOCKS = S // P
 FUSED = 4
-GATHERS = [(4, 4), (8, 4), (12, 2), (14, 2), (16, 2)]
-LOADS = [(0, 2), (2, 2), (4, 4), (8, 4), (12, 2), (14, 2), (16, 2)]
-MASKS = [(0, 4), (4, 8), (12, 4), (16, 2)]
+GATHERS = [(4, 6), (10, 4), (14, 4)]
+LOADS = [(0, 2), (2, 2), (4, 4), (8, 2), (10, 2), (12, 2), (14, 2), (16, 2)]
+MASKS = [(0, 4), (4, 8), (12, 6)]
+CLIPPED = 4
 PAIRS = [(4, 2), (6, 2), (8, 2), (10, 2), (12, 2), (14, 2), (16, 2)]
-MOVED = 3
-RING = 4
+MOVED = 2
+RING = 3
+WINDOW = 800
+BACK = [3, 4, 5, 6, 7, 3, 2]
+SUMS = [1, 0, 4, 5, 6, 7, 3]
 TOKEN_BANKS = [(0, 512), (512, 256)]
 FIRST_TOKEN_BANKS = [(0, 256), (256, 256), (512, 128), (640, 128)]
 TOKEN_RANGES = [(0, 480), (480, 288)]
@@ -136,7 +140,9 @@ def tile_moe_sdb_relu_kernel(
                 w2_plane_raw[:].rearrange("p (m t) -> p t m", t=PACK)[:, ts, :],
             )
 
-        dc = [keep.tile([P, T], F32, name="dc%d" % t) for t in range(PACK)]
+        dc = [keep.tile([P, WINDOW], F32, name="dc%d" % t) for t in range(PACK)]
+        for t in range(PACK):
+            nc.vector.memset(dc[t][:, T:], 0.0)
         products = [(t, t0, n) for t in range(PACK) for t0, n in (FIRST_TOKEN_BANKS if t == 0 else TOKEN_BANKS)]
         for x, (t, t0, n) in enumerate(products):
             acc = banks("product%d" % x, x % BANKS)
@@ -170,122 +176,113 @@ def tile_moe_sdb_relu_kernel(
                 nc.vector.tensor_copy(plain_at(b0, n, t), dc[t][:].indirect(tokens(b0, n)))
 
         da_first = bf16_tile("da_first", "da_first", FUSED)
-        da = bf16_tile("da", "da", BLOCKS - 2 * FUSED)
-        da_last = bf16_tile("da_last", "da_first", FUSED)
-        signs = [bf16_tile("signs%d" % m, "signs%d" % m, n) for m, (b0, n) in enumerate(MASKS[:-1])]
-        at = codes_at + 2 * (MOVED + 2) * H
-        signs.append(placed.tile([P, MASKS[-1][1] * H], BF16, name="signs3", offset=at, align_bytes=64))
+        da_middle = bf16_tile("da_middle", "da_middle", 8)
+        da_late = bf16_tile("da_late", "da_first", 4)
+        da_last = bf16_tile("da_last", "da_last", 2)
+        da = {0: da_first, 4: da_middle, 12: da_late, 16: da_last}
+        signs = {b0: bf16_tile("signs%d" % b0, "signs%d" % b0, n) for b0, n in MASKS[:2]}
+        at = codes_at + 2 * MOVED * H + 2 * 2 * C
+        signs[12] = placed.tile([P, 4 * H], BF16, name="signs12", offset=at, align_bytes=64)
+        signs[16] = bf16_tile("signs16", "signs16", 2)
         mask = {}
         back = {}
-
-        def da_blocks(b0, n):
-            if b0 < FUSED:
-                return da_first[:, b0 * H : (b0 + n) * H]
-            if b0 >= BLOCKS - FUSED:
-                return da_last[:, (b0 - BLOCKS + FUSED) * H : (b0 - BLOCKS + FUSED + n) * H]
-            return da[:, (b0 - FUSED) * H : (b0 - FUSED + n) * H]
-
-        def mask_blocks(b0, n):
-            m0 = max(m for m in mask if m <= b0)
-            return mask[m0][:, (b0 - m0) * H : (b0 - m0 + n) * H]
-
-        def make_signs(j, m):
-            b0, n = LOADS[j]
-            at = (b0 - MASKS[m][0]) * H
-            nc.scalar.activation(woven_view(signs[m][:, at : at + n * H]), planar_view(a_t[j][:]), ACT.Sign)
-
-        def clip(m, tile):
-            mask[MASKS[m][0]] = tile
-            nc.gpsimd.tensor_scalar(tile, signs[m][:], 1.0, 0.0, ALU.min, ALU.max)
-
         forth = {}
 
-        def turn_forth(j):
-            b0, n = GATHERS[j]
-            if j == 0:
-                whole = banks("forth", 0, RING)
-                forth[0], forth[1] = whole[:, : 2 * BANK], whole[:, 2 * BANK :]
-            else:
-                for x in range((b0 - FUSED) // 2, (b0 + n - FUSED) // 2):
-                    forth[x] = banks("forth%d" % x, 2 * (x % 2), 2)[:]
-            for t in range(PACK):
-                for b in range(n):
-                    x, place = divmod(b0 + b - FUSED, 2)
-                    at = place * BANK + t * P
-                    nc.tensor.transpose(
-                        forth[x][:, at : at + P], plain_at(b0, n, t)[:, b * P : (b + 1) * P], identity[:]
-                    )
+        def blocks_of(tiles, b0, n):
+            first = max(b for b in tiles if b <= b0)
+            return tiles[first][:, (b0 - first) * H : (b0 - first + n) * H]
 
-        def gate_pair(x, turned):
-            words = turned.bitcast(F32)
-            back[x] = banks("back%d" % x, RING + x % RING)
+        def make_signs(j):
+            nc.scalar.activation(woven_view(blocks_of(signs, *LOADS[j])), planar_view(a_t[j][:]), ACT.Sign)
+
+        def clip(b0, n):
+            nc.gpsimd.tensor_scalar(blocks_of(mask, b0, n), blocks_of(signs, b0, n), 1.0, 0.0, ALU.min, ALU.max)
+
+        steps = [(b0, n, u, b) for b0, n in GATHERS for u in range(2) for b in range(b0, b0 + n, 2)]
+
+        def turn_plane(k, e):
+            b0, n, u, b = steps[k]
+            if k not in forth:
+                forth[k] = banks("forth%d" % k, k % RING)
+            for place in range(2):
+                at = (2 * place + e) * P
+                source = plain_at(b0, n, 2 * u + e)[:, (b + place - b0) * P : (b + place - b0 + 1) * P]
+                nc.tensor.transpose(forth[k][:, at : at + P], source, identity[:])
+
+        def gate_step(k, turned=None):
+            b0, n, u, b = steps[k]
+            x = (b - FUSED) // 2
+            if turned is None:
+                turned = keep.tile([P, 2 * C], BF16, name="turned%d" % k, tag="turned%d" % k, align_bytes=64)
             for place in range(2):
                 nc.scalar.activation(
-                    turned[:, place * H : (place + 1) * H].rearrange("s (u p e) -> s u p e", u=2, e=2),
-                    forth[x][:, place * BANK : (place + 1) * BANK].rearrange("s (u e p) -> s u p e", u=2, e=2),
+                    turned[:, place * C : (place + 1) * C].rearrange("s (p e) -> s p e", e=2),
+                    forth[k][:, place * C : (place + 1) * C].rearrange("s (e p) -> s p e", e=2),
                     ACT.Copy,
                     scale=gate_cols[:, 2 * x + place : 2 * x + place + 1],
                 )
+            if x not in back:
+                back[x] = banks("back%d" % x, BACK[x])
             for place in range(2):
-                for u in range(2):
-                    nc.tensor.transpose(
-                        back[x][:, place * C + u : (place + 1) * C : 2],
-                        words[:, (2 * place + u) * P : (2 * place + u + 1) * P],
-                        identity[:],
-                    )
+                nc.tensor.transpose(
+                    back[x][:, place * C + u : (place + 1) * C : 2],
+                    turned[:, : 2 * C].bitcast(F32)[:, place * P : (place + 1) * P],
+                    identity[:],
+                )
+            if k + RING < len(steps):
+                turn_plane(k + RING, 0)
+                turn_plane(k + RING, 1)
 
-        def move(x, n, tile, at):
-            nc.scalar.copy(tile[:, at * H : (at + n) * H].bitcast(F32), back[x][:, : n * C])
-
-        def mask_moved(b0, n, tile):
-            nc.gpsimd.tensor_tensor(da_blocks(b0, n), tile[:], mask_blocks(b0, n), ALU.mult)
-
-        def mask_bank(x, place=0):
-            b0, n = PAIRS[x][0] + place, PAIRS[x][1] - place
-            nc.vector.tensor_tensor(
-                da_blocks(b0, n), back[x][:, place * C : (place + n) * C].bitcast(BF16), mask_blocks(b0, n), ALU.mult
-            )
+        def mask_bank(x):
+            b0, n = PAIRS[x]
+            nc.vector.tensor_tensor(blocks_of(da, b0, n), back[x][:].bitcast(BF16), blocks_of(mask, b0, n), ALU.mult)
 
         gates_turned = banks("gates_turned", 2)
         nc.tensor.transpose(gates_turned[:, :P], gate_blocks[:], identity[:])
         gate_cols = keep.tile([P, BLOCKS - FUSED], F32, name="gate_cols", tag="gate_cols", align_bytes=64)
+        make_signs(0)
+        make_signs(1)
         nc.scalar.copy(gate_cols[:], gates_turned[:, : BLOCKS - FUSED])
-        make_signs(0, 0)
-        make_signs(1, 0)
-        clip(0, placed.tile([P, FUSED * H], BF16, name="mask0", offset=border, align_bytes=64)[:])
+        mask[0] = placed.tile([P, FUSED * H], BF16, name="mask0", offset=border, align_bytes=64)
+        clip(0, FUSED)
         nc.gpsimd.tensor_tensor(
-            da_blocks(0, FUSED).rearrange("p (s t) -> p s t", t=PACK),
+            da_first[:].rearrange("p (s t) -> p s t", t=PACK),
             gated[:].rearrange("p (t s) -> p s t", t=PACK),
-            mask[0].rearrange("p (s t) -> p s t", t=PACK),
+            mask[0][:].rearrange("p (s t) -> p s t", t=PACK),
             ALU.mult,
         )
-        make_signs(2, 1)
-        make_signs(3, 1)
-        clip(1, bf16_tile("mask1", "mask1", MASKS[1][1])[:])
-        make_signs(4, 2)
-        turn_forth(0)
-        turned_first = bf16_tile("turned_first", "a3", 4)
-        gate_pair(0, turned_first[:, : 2 * H])
-        gate_pair(1, turned_first[:, 2 * H :])
-        make_signs(5, 2)
-        clip(2, bf16_tile("mask2", "mask2", MASKS[2][1])[:])
+        make_signs(2)
+        make_signs(3)
+        for e in range(2):
+            for k in range(RING):
+                turn_plane(k, e)
+        gate_step(0, keep.tile([P, 4 * C], BF16, name="turned_first", tag="a3", align_bytes=64))
+        gate_step(1)
+        gate_step(2)
+        make_signs(4)
+        mask[4] = bf16_tile("mask4", "mask4", 8)
+        clip(4, 8)
+        gate_step(3)
+        make_signs(5)
+        gate_step(4)
+        gate_step(5)
         moved = placed.tile([P, MOVED * H], BF16, name="moved", offset=codes_at, align_bytes=64)
-        move(0, 2, moved, 0)
-        move(1, 1, moved, 2)
-        mask_moved(FUSED, MOVED, moved)
-        turn_forth(1)
-        gate_pair(2, bf16_tile("turned2", "turned2", 2)[:])
-        gate_pair(3, bf16_tile("turned3", "turned3", 2)[:])
-        turn_forth(2)
-        gate_pair(4, bf16_tile("turned4", "turned4", 2)[:])
-        make_signs(6, 3)
-        turn_forth(3)
+        nc.scalar.copy(moved[:].bitcast(F32), back[0][:])
+        nc.gpsimd.tensor_tensor(blocks_of(da, FUSED, MOVED), moved[:], blocks_of(mask, FUSED, MOVED), ALU.mult)
+        gate_step(6)
+        gate_step(7)
+        make_signs(6)
+        mask[12] = bf16_tile("mask12", "mask12", 6)
+        clip(12, CLIPPED)
+        gate_step(8)
+        gate_step(9)
+        gate_step(10)
+        make_signs(7)
         at = codes_at + 2 * MOVED * H
-        gate_pair(5, placed.tile([P, 2 * H], BF16, name="turned5", offset=at, align_bytes=64)[:])
-        mask[MASKS[3][0]] = bf16_tile("mask3", "mask3", MASKS[3][1])[:]
-        nc.scalar.activation(mask_blocks(*MASKS[3]), signs[3][:], ACT.Relu)
-        turn_forth(4)
-        gate_pair(6, bf16_tile("turned6", "turned6", 2)[:])
+        gate_step(11, placed.tile([P, 2 * C], BF16, name="turned_late", offset=at, align_bytes=64))
+        gate_step(12)
+        gate_step(13)
+        nc.scalar.activation(blocks_of(mask, 12 + CLIPPED, 6 - CLIPPED), blocks_of(signs, 16, 2), ACT.Relu)
 
         dx = keep.tile([P, S], F32, name="dx", tag="gate_cols", align_bytes=64)
         codes = placed.tile([P, S], U32, name="codes", offset=codes_at, align_bytes=64)
@@ -294,7 +291,7 @@ def tile_moe_sdb_relu_kernel(
 
         def quantise(b0, n):
             s0, s1 = b0 * P, (b0 + n) * P
-            nc.vector.quantize_mx(out=codes[:, s0:s1].bitcast(FP8X4), scales=plane[:, s0:s1], in_=da_blocks(b0, n))
+            nc.vector.quantize_mx(out=codes[:, s0:s1].bitcast(FP8X4), scales=plane[:, s0:s1], in_=blocks_of(da, b0, n))
 
         def experts(b0, n, where, empty):
             s0, s1 = b0 * P, (b0 + n) * P
@@ -313,25 +310,25 @@ def tile_moe_sdb_relu_kernel(
                 )
             empty(dx[:, s0:s1], acc[:, : n * P])
 
-        mask_bank(1, 1)
-        for x in (2, 3, 4):
+        for x in (1, 2, 3):
             mask_bank(x)
         quantise(0, 4)
-        experts(0, 4, 0, nc.scalar.copy)
+        experts(0, 4, SUMS[0], nc.scalar.copy)
+        mask_bank(4)
         quantise(4, 4)
-        experts(4, 4, 1, nc.scalar.copy)
+        experts(4, 4, SUMS[1], nc.scalar.copy)
         mask_bank(5)
         quantise(8, 4)
-        experts(8, 4, 2, nc.scalar.copy)
-        quantise(12, 2)
-        experts(12, 2, 3, nc.scalar.copy)
+        experts(8, 4, SUMS[2], nc.scalar.copy)
         mask_bank(6)
+        quantise(12, 2)
+        experts(12, 2, SUMS[3], nc.scalar.copy)
         quantise(14, 2)
-        experts(14, 2, 6, nc.scalar.copy)
+        experts(14, 2, SUMS[4], nc.scalar.copy)
         quantise(16, 1)
-        experts(16, 1, 4, nc.vector.tensor_copy)
+        experts(16, 1, SUMS[5], nc.vector.tensor_copy)
         quantise(17, 1)
-        experts(17, 1, 5, nc.scalar.copy)
+        experts(17, 1, SUMS[6], nc.scalar.copy)
 
         second = keep.tile([P, T], F32, name="second")
         for h, (t0, n) in enumerate(TOKEN_RANGES):

@@ -26,21 +26,17 @@ ALU = mybir.AluOpType
 ACT = mybir.ActivationFunctionType
 
 BLOCKS = S // P
-FUSED = 4
-GATHERS = [(4, 6), (10, 4), (14, 4)]
-LOADS = [(0, 2), (2, 2), (4, 4), (8, 2), (10, 2), (12, 2), (14, 2), (16, 2)]
-MASKS = [(0, 4), (4, 8), (12, 6)]
-CLIPPED = 4
-PAIRS = [(4, 2), (6, 2), (8, 2), (10, 2), (12, 2), (14, 2), (16, 2)]
-MOVED = 2
-RING = 3
+TURNED = 10
+SCALAR_GATHERS = [(0, 4), (4, 4), (8, 2)]
+VECTOR_GATHERS = [(10, 4), (14, 4)]
+LOADS = [(0, 4), (10, 2), (12, 2), (4, 4), (8, 2), (14, 2), (16, 2)]
 WINDOW = 800
-BACK = [3, 4, 5, 6, 7, 3, 2]
-SUMS = [1, 0, 4, 5, 6, 7, 3]
+FORTH = [0, 1, 2, 3]
+BACK = [4, 5, 6]
 TOKEN_BANKS = [(0, 512), (512, 256)]
 FIRST_TOKEN_BANKS = [(0, 256), (256, 256), (512, 128), (640, 128)]
-TOKEN_RANGES = [(0, 480), (480, 288)]
-STORE_RANGES = [(0, 384), (384, 256), (640, 128)]
+ALONE = (0, 160)
+SHARED = [(160, 256), (416, 224), (640, 128)]
 
 
 def tile_moe_sdb_relu_kernel(
@@ -50,20 +46,11 @@ def tile_moe_sdb_relu_kernel(
 
     with ExitStack() as ctx:
         keep = ctx.enter_context(tc.tile_pool(name="keep", bufs=1))
-        placed = ctx.enter_context(tc.tile_pool(name="placed", bufs=1))
+        ring = ctx.enter_context(tc.tile_pool(name="ring", bufs=2))
         psum = ctx.enter_context(tc.psum_pool(name="psum", bufs=1))
 
-        def banks(name, first, count=1):
-            return psum.tile([P, count * BANK], F32, name=name, offset=4 * BANK * first)
-
-        def bf16_tile(name, tag, blocks):
-            return keep.tile([P, blocks * H], BF16, name=name, tag=tag, align_bytes=64)
-
-        def woven_view(ap):
-            return ap.rearrange("p (r i t) -> p r t i", i=RUN, t=PACK)
-
-        def planar_view(ap):
-            return ap.rearrange("p (t r i) -> p r t i", i=RUN, t=PACK)
+        def bank(name, which):
+            return psum.tile([P, BANK], F32, name=name, offset=4 * BANK * which)
 
         def tokens(b0, n):
             return offs_t[:, b0 * P // LIST_ROWS : (b0 + n) * P // LIST_ROWS]
@@ -99,23 +86,16 @@ def tile_moe_sdb_relu_kernel(
         offs_t = keep.tile([P, S // LIST_ROWS], U16)
         nc.sync.dma_start(offs_t[:], offs)
 
-        plain_bytes = 4 * H * (BLOCKS - FUSED)
-        border = plain_bytes
-        codes_at = border + 2 * H * FUSED
-        gate_rows = placed.tile([P, FUSED * P], F32, name="gate_rows", offset=border, align_bytes=64)
-        nc.sync.dma_start(gate_rows[:], gate[:, : FUSED * P])
+        gate_rows = {}
+        for b0, n in VECTOR_GATHERS:
+            gate_rows[b0] = keep.tile([P, n * P], F32, name="gate_rows%d" % b0, align_bytes=64)
+            nc.sync.dma_start(gate_rows[b0][:], gate[:, b0 * P : (b0 + n) * P])
+        nc.sync.dma_start(gate_blocks[:TURNED, :], gate[0, : TURNED * P].rearrange("(b s) -> b s", s=P))
         a_rows = a.rearrange("(p t) s -> p t s", t=PACK)
-        a_t = []
-        for j, (b0, n) in enumerate(LOADS):
-            if j == 0:
-                a_t.append(placed.tile([P, n * H], F32, name="a0", offset=0, align_bytes=64))
-            else:
-                a_t.append(keep.tile([P, n * H], F32, name="a%d" % j, tag="a%d" % j, align_bytes=64))
-            nc.sync.dma_start(a_t[j][:].rearrange("p (t s) -> p t s", t=PACK), a_rows[:, :, b0 * P : (b0 + n) * P])
-            if j == 1:
-                nc.sync.dma_start(
-                    gate_blocks[: BLOCKS - FUSED, :], gate[0, FUSED * P :].rearrange("(b s) -> b s", s=P)
-                )
+        a_t = {}
+        for b0, n in LOADS:
+            a_t[b0] = keep.tile([P, n * H], F32, name="a%d" % b0, align_bytes=64)
+            nc.sync.dma_start(a_t[b0][:].rearrange("p (t s) -> p t s", t=PACK), a_rows[:, :, b0 * P : (b0 + n) * P])
         w1_codes = keep.tile([P, E, 2 * K], U8, align_bytes=64)
         nc.sync.dma_start(w1_codes[:].bitcast(I32), w1t_words[:, 0].rearrange("e p b -> p e b").bitcast(I32))
         for q in range(QUADRANTS):
@@ -145,7 +125,7 @@ def tile_moe_sdb_relu_kernel(
             nc.vector.memset(dc[t][:, T:], 0.0)
         products = [(t, t0, n) for t in range(PACK) for t0, n in (FIRST_TOKEN_BANKS if t == 0 else TOKEN_BANKS)]
         for x, (t, t0, n) in enumerate(products):
-            acc = banks("product%d" % x, x % BANKS)
+            acc = bank("product%d" % x, x % BANKS)
             nc.tensor.matmul_mx(
                 out=acc[:, :n],
                 lhsT=w2_codes[:, 2 * P * t : 2 * P * (t + 1)].bitcast(FP4X4),
@@ -160,133 +140,90 @@ def tile_moe_sdb_relu_kernel(
             else:
                 nc.scalar.copy(dc[t][:, t0 : t0 + n], acc[:, :n])
 
-        gated = keep.tile([P, FUSED * H], F32, name="gated", align_bytes=64)
+        gates_turned = bank("gates_turned", 7)
+        nc.tensor.transpose(gates_turned[:, :P], gate_blocks[:], identity[:])
+        gate_cols = keep.tile([P, TURNED], F32, name="gate_cols", align_bytes=64)
+        nc.scalar.copy(gate_cols[:], gates_turned[:, :TURNED])
+
+        gated = {b0: keep.tile([P, n * H], F32, name="gated%d" % b0, align_bytes=64) for b0, n in VECTOR_GATHERS}
         for t in range(PACK):
-            nc.vector.tensor_tensor(
-                gated[:, t * FUSED * P : (t + 1) * FUSED * P], dc[t][:].indirect(tokens(0, FUSED)), gate_rows[:], ALU.mult
-            )
-        plain = placed.tile([P, H * (BLOCKS - FUSED)], F32, name="plain", offset=0, align_bytes=64)
+            for b0, n in VECTOR_GATHERS:
+                nc.vector.tensor_tensor(
+                    gated[b0][:, t * n * P : (t + 1) * n * P], dc[t][:].indirect(tokens(b0, n)), gate_rows[b0][:], ALU.mult
+                )
 
-        def plain_at(b0, n, t):
-            at = H * (b0 - FUSED) + t * n * P
-            return plain[:, at : at + n * P]
-
-        for b0, n in GATHERS:
-            for t in range(PACK):
-                nc.vector.tensor_copy(plain_at(b0, n, t), dc[t][:].indirect(tokens(b0, n)))
-
-        da_first = bf16_tile("da_first", "da_first", FUSED)
-        da_middle = bf16_tile("da_middle", "da_middle", 8)
-        da_late = bf16_tile("da_late", "da_first", 4)
-        da_last = bf16_tile("da_last", "da_last", 2)
-        da = {0: da_first, 4: da_middle, 12: da_late, 16: da_last}
-        signs = {b0: bf16_tile("signs%d" % b0, "signs%d" % b0, n) for b0, n in MASKS[:2]}
-        at = codes_at + 2 * MOVED * H + 2 * 2 * C
-        signs[12] = placed.tile([P, 4 * H], BF16, name="signs12", offset=at, align_bytes=64)
-        signs[16] = bf16_tile("signs16", "signs16", 2)
-        mask = {}
-        back = {}
+        halves = [(b0, n, u) for b0, n in SCALAR_GATHERS for u in range(2)]
+        plain = {}
         forth = {}
+        back = {}
+
+        def gather_half(k):
+            b0, n, u = halves[k]
+            for e in range(2):
+                plain[k, e] = ring.tile([P, n * P], F32, name="plain", tag="plain%d" % e)
+                nc.scalar.activation(plain[k, e][:], dc[2 * u + e][:].indirect(tokens(b0, n)), ACT.Copy)
+            for e in range(2):
+                for b in range(b0, b0 + n, 2):
+                    if (b, u) not in forth:
+                        forth[b, u] = bank("forth", FORTH[len(forth) % len(FORTH)])
+                    for place in range(2):
+                        at = (2 * place + e) * P
+                        source = plain[k, e][:, (b + place - b0) * P : (b + place - b0 + 1) * P]
+                        nc.tensor.transpose(forth[b, u][:, at : at + P], source, identity[:])
+
+        def gate_half(k):
+            b0, n, u = halves[k]
+            for b in range(b0, b0 + n, 2):
+                turned = keep.tile([P, 2 * C], BF16, name="turned%d_%d" % (b, u), align_bytes=64)
+                for place in range(2):
+                    nc.scalar.activation(
+                        turned[:, place * C : (place + 1) * C].rearrange("s (p e) -> s p e", e=2),
+                        forth[b, u][:, place * C : (place + 1) * C].rearrange("s (e p) -> s p e", e=2),
+                        ACT.Copy,
+                        scale=gate_cols[:, b + place : b + place + 1],
+                    )
+                if b not in back:
+                    back[b] = bank("back", BACK[len(back) % len(BACK)])
+                for place in range(2):
+                    nc.tensor.transpose(
+                        back[b][:, place * C + u : (place + 1) * C : 2],
+                        turned[:].bitcast(F32)[:, place * P : (place + 1) * P],
+                        identity[:],
+                    )
+
+        da = {}
+        mask = {}
 
         def blocks_of(tiles, b0, n):
             first = max(b for b in tiles if b <= b0)
             return tiles[first][:, (b0 - first) * H : (b0 - first + n) * H]
 
-        def make_signs(j):
-            nc.scalar.activation(woven_view(blocks_of(signs, *LOADS[j])), planar_view(a_t[j][:]), ACT.Sign)
+        def make_mask(b0, n):
+            mask[b0] = keep.tile([P, n * H], BF16, name="mask%d" % b0, align_bytes=64)
+            nc.vector.tensor_scalar(
+                mask[b0][:].rearrange("p (r i t) -> p r t i", i=RUN, t=PACK),
+                a_t[b0][:].rearrange("p (t r i) -> p r t i", i=RUN, t=PACK),
+                0.0,
+                None,
+                ALU.is_gt,
+            )
 
-        def clip(b0, n):
-            nc.gpsimd.tensor_scalar(blocks_of(mask, b0, n), blocks_of(signs, b0, n), 1.0, 0.0, ALU.min, ALU.max)
+        def mask_bank(b):
+            nc.vector.tensor_tensor(blocks_of(da, b, 2), back[b][:].bitcast(BF16), blocks_of(mask, b, 2), ALU.mult)
 
-        steps = [(b0, n, u, b) for b0, n in GATHERS for u in range(2) for b in range(b0, b0 + n, 2)]
+        def mask_gated(b):
+            first = max(x for x in gated if x <= b)
+            nc.vector.scalar_tensor_tensor(
+                blocks_of(da, b, 2).rearrange("p (s t) -> p s t", t=PACK),
+                a_t[b][:].rearrange("p (t s) -> p s t", t=PACK),
+                0.0,
+                gated[first][:].rearrange("p (t s) -> p s t", t=PACK)[:, (b - first) * P : (b - first + 2) * P, :],
+                ALU.is_gt,
+                ALU.mult,
+            )
 
-        def turn_plane(k, e):
-            b0, n, u, b = steps[k]
-            if k not in forth:
-                forth[k] = banks("forth%d" % k, k % RING)
-            for place in range(2):
-                at = (2 * place + e) * P
-                source = plain_at(b0, n, 2 * u + e)[:, (b + place - b0) * P : (b + place - b0 + 1) * P]
-                nc.tensor.transpose(forth[k][:, at : at + P], source, identity[:])
-
-        def gate_step(k, turned=None):
-            b0, n, u, b = steps[k]
-            x = (b - FUSED) // 2
-            if turned is None:
-                turned = keep.tile([P, 2 * C], BF16, name="turned%d" % k, tag="turned%d" % k, align_bytes=64)
-            for place in range(2):
-                nc.scalar.activation(
-                    turned[:, place * C : (place + 1) * C].rearrange("s (p e) -> s p e", e=2),
-                    forth[k][:, place * C : (place + 1) * C].rearrange("s (e p) -> s p e", e=2),
-                    ACT.Copy,
-                    scale=gate_cols[:, 2 * x + place : 2 * x + place + 1],
-                )
-            if x not in back:
-                back[x] = banks("back%d" % x, BACK[x])
-            for place in range(2):
-                nc.tensor.transpose(
-                    back[x][:, place * C + u : (place + 1) * C : 2],
-                    turned[:, : 2 * C].bitcast(F32)[:, place * P : (place + 1) * P],
-                    identity[:],
-                )
-            if k + RING < len(steps):
-                turn_plane(k + RING, 0)
-                turn_plane(k + RING, 1)
-
-        def mask_bank(x):
-            b0, n = PAIRS[x]
-            nc.vector.tensor_tensor(blocks_of(da, b0, n), back[x][:].bitcast(BF16), blocks_of(mask, b0, n), ALU.mult)
-
-        gates_turned = banks("gates_turned", 2)
-        nc.tensor.transpose(gates_turned[:, :P], gate_blocks[:], identity[:])
-        gate_cols = keep.tile([P, BLOCKS - FUSED], F32, name="gate_cols", tag="gate_cols", align_bytes=64)
-        make_signs(0)
-        make_signs(1)
-        nc.scalar.copy(gate_cols[:], gates_turned[:, : BLOCKS - FUSED])
-        mask[0] = placed.tile([P, FUSED * H], BF16, name="mask0", offset=border, align_bytes=64)
-        clip(0, FUSED)
-        nc.gpsimd.tensor_tensor(
-            da_first[:].rearrange("p (s t) -> p s t", t=PACK),
-            gated[:].rearrange("p (t s) -> p s t", t=PACK),
-            mask[0][:].rearrange("p (s t) -> p s t", t=PACK),
-            ALU.mult,
-        )
-        make_signs(2)
-        make_signs(3)
-        for e in range(2):
-            for k in range(RING):
-                turn_plane(k, e)
-        gate_step(0, keep.tile([P, 4 * C], BF16, name="turned_first", tag="a3", align_bytes=64))
-        gate_step(1)
-        gate_step(2)
-        make_signs(4)
-        mask[4] = bf16_tile("mask4", "mask4", 8)
-        clip(4, 8)
-        gate_step(3)
-        make_signs(5)
-        gate_step(4)
-        gate_step(5)
-        moved = placed.tile([P, MOVED * H], BF16, name="moved", offset=codes_at, align_bytes=64)
-        nc.scalar.copy(moved[:].bitcast(F32), back[0][:])
-        nc.gpsimd.tensor_tensor(blocks_of(da, FUSED, MOVED), moved[:], blocks_of(mask, FUSED, MOVED), ALU.mult)
-        gate_step(6)
-        gate_step(7)
-        make_signs(6)
-        mask[12] = bf16_tile("mask12", "mask12", 6)
-        clip(12, CLIPPED)
-        gate_step(8)
-        gate_step(9)
-        gate_step(10)
-        make_signs(7)
-        at = codes_at + 2 * MOVED * H
-        gate_step(11, placed.tile([P, 2 * C], BF16, name="turned_late", offset=at, align_bytes=64))
-        gate_step(12)
-        gate_step(13)
-        nc.scalar.activation(blocks_of(mask, 12 + CLIPPED, 6 - CLIPPED), blocks_of(signs, 16, 2), ACT.Relu)
-
-        dx = keep.tile([P, S], F32, name="dx", tag="gate_cols", align_bytes=64)
-        codes = placed.tile([P, S], U32, name="codes", offset=codes_at, align_bytes=64)
-
+        dx = keep.tile([P, S], F32, name="dx", align_bytes=64)
+        codes = keep.tile([P, S], U32, name="codes", align_bytes=64)
         plane = keep.tile([P, S], U8, name="plane", align_bytes=64)
 
         def quantise(b0, n):
@@ -295,7 +232,7 @@ def tile_moe_sdb_relu_kernel(
 
         def experts(b0, n, where, empty):
             s0, s1 = b0 * P, (b0 + n) * P
-            acc = banks("sums%d" % b0, where)
+            acc = bank("sums%d" % b0, where)
             width = min(n * P, C)
             for v0 in range(s0, s1, width):
                 e = v0 // C
@@ -310,34 +247,65 @@ def tile_moe_sdb_relu_kernel(
                 )
             empty(dx[:, s0:s1], acc[:, : n * P])
 
-        for x in (1, 2, 3):
-            mask_bank(x)
-        quantise(0, 4)
-        experts(0, 4, SUMS[0], nc.scalar.copy)
-        mask_bank(4)
-        quantise(4, 4)
-        experts(4, 4, SUMS[1], nc.scalar.copy)
-        mask_bank(5)
-        quantise(8, 4)
-        experts(8, 4, SUMS[2], nc.scalar.copy)
-        mask_bank(6)
-        quantise(12, 2)
-        experts(12, 2, SUMS[3], nc.scalar.copy)
-        quantise(14, 2)
-        experts(14, 2, SUMS[4], nc.scalar.copy)
-        quantise(16, 1)
-        experts(16, 1, SUMS[5], nc.vector.tensor_copy)
-        quantise(17, 1)
-        experts(17, 1, SUMS[6], nc.scalar.copy)
+        for b0, n in SCALAR_GATHERS + VECTOR_GATHERS:
+            da[b0] = keep.tile([P, n * H], BF16, name="da%d" % b0, align_bytes=64)
 
-        second = keep.tile([P, T], F32, name="second")
-        for h, (t0, n) in enumerate(TOKEN_RANGES):
-            cols = slice(t0 // LIST_ROWS, (t0 + n) // LIST_ROWS)
-            first = keep.tile([P, n], F32, name="first%d" % h)
-            nc.vector.tensor_copy(first[:], dx[:].indirect(pos_t[0][:, cols]))
-            nc.vector.tensor_tensor(second[:, t0 : t0 + n], dx[:].indirect(pos_t[1][:, cols]), first[:], ALU.add)
-        for h, (t0, n) in enumerate(STORE_RANGES):
-            cols = slice(t0 // LIST_ROWS, (t0 + n) // LIST_ROWS)
-            third = keep.tile([P, n], F32, name="third%d" % h)
-            nc.vector.tensor_tensor(third[:], dx[:].indirect(pos_t[2][:, cols]), second[:, t0 : t0 + n], ALU.add)
-            nc.sync.dma_start(out[:, t0 : t0 + n], third[:])
+        gather_half(0)
+        gather_half(1)
+        gate_half(0)
+        gather_half(2)
+        gate_half(1)
+        make_mask(0, 4)
+        mask_gated(10)
+        mask_bank(0)
+        mask_bank(2)
+        mask_gated(12)
+        quantise(0, 4)
+        quantise(10, 4)
+        gather_half(3)
+        gate_half(2)
+        gather_half(4)
+        gate_half(3)
+        make_mask(4, 4)
+        make_mask(8, 2)
+        mask_gated(14)
+        mask_bank(4)
+        mask_bank(6)
+        gather_half(5)
+        gate_half(4)
+        gate_half(5)
+        mask_gated(16)
+        quantise(4, 4)
+        mask_bank(8)
+        quantise(14, 4)
+        quantise(8, 1)
+        quantise(9, 1)
+        experts(0, 4, 2, nc.scalar.copy)
+        experts(10, 4, 3, nc.scalar.copy)
+        experts(4, 4, 0, nc.scalar.copy)
+        experts(14, 4, 1, nc.scalar.copy)
+        experts(8, 1, 7, nc.vector.tensor_copy)
+        experts(9, 1, 6, nc.scalar.copy)
+
+        def columns(t0, n):
+            return slice(t0 // LIST_ROWS, (t0 + n) // LIST_ROWS)
+
+        fetched = {}
+        for t0, n in SHARED:
+            for r in range(2):
+                fetched[t0, r] = keep.tile([P, n], F32, name="fetched%d_%d" % (t0, r))
+                nc.scalar.activation(fetched[t0, r][:], dx[:].indirect(pos_t[r][:, columns(t0, n)]), ACT.Copy)
+        t0, n = ALONE
+        one = keep.tile([P, n], F32)
+        two = keep.tile([P, n], F32)
+        three = keep.tile([P, n], F32)
+        nc.vector.tensor_copy(one[:], dx[:].indirect(pos_t[0][:, columns(t0, n)]))
+        nc.vector.tensor_tensor(two[:], dx[:].indirect(pos_t[1][:, columns(t0, n)]), one[:], ALU.add)
+        nc.vector.tensor_tensor(three[:], dx[:].indirect(pos_t[2][:, columns(t0, n)]), two[:], ALU.add)
+        nc.sync.dma_start(out[:, t0 : t0 + n], three[:])
+        for t0, n in SHARED:
+            part = keep.tile([P, n], F32, name="part%d" % t0)
+            whole = keep.tile([P, n], F32, name="whole%d" % t0)
+            nc.vector.tensor_tensor(part[:], dx[:].indirect(pos_t[2][:, columns(t0, n)]), fetched[t0, 0][:], ALU.add)
+            nc.vector.tensor_tensor(whole[:], part[:], fetched[t0, 1][:], ALU.add)
+            nc.sync.dma_start(out[:, t0 : t0 + n], whole[:])

@@ -8,7 +8,6 @@ S = E * C
 P = 128
 PACK = 4
 QUADRANTS = 4
-RUN = 4
 LIST_ROWS = 16
 BANK = 512
 BANKS = 8
@@ -26,17 +25,18 @@ ALU = mybir.AluOpType
 ACT = mybir.ActivationFunctionType
 
 BLOCKS = S // P
-TURNED = 10
-SCALAR_GATHERS = [(0, 4), (4, 4), (8, 2)]
-VECTOR_GATHERS = [(10, 4), (14, 4)]
-LOADS = [(0, 4), (10, 2), (12, 2), (4, 4), (8, 2), (14, 2), (16, 2)]
-WINDOW = 800
-FORTH = [0, 1, 2, 3]
-BACK = [4, 5, 6]
+PAIR = 4
+WOVEN = 10
+FIRST = 2
+TURNED_GATHERS = [(10, 4), (14, 2), (16, 2)]
+FORTH = [2, 3, 4, 5, 2, 3, 5, 2]
+BACK = {10: 6, 12: 7, 14: 4, 16: 3}
+GATE_BANKS = [(2, 1), (6, 0)]
 TOKEN_BANKS = [(0, 512), (512, 256)]
 FIRST_TOKEN_BANKS = [(0, 256), (256, 256), (512, 128), (640, 128)]
 ALONE = (0, 160)
 SHARED = [(160, 256), (416, 224), (640, 128)]
+KB = 1024
 
 
 def tile_moe_sdb_relu_kernel(
@@ -46,17 +46,20 @@ def tile_moe_sdb_relu_kernel(
 
     with ExitStack() as ctx:
         keep = ctx.enter_context(tc.tile_pool(name="keep", bufs=1))
-        ring = ctx.enter_context(tc.tile_pool(name="ring", bufs=2))
+        placed = ctx.enter_context(tc.tile_pool(name="placed", bufs=1))
         psum = ctx.enter_context(tc.psum_pool(name="psum", bufs=1))
 
         def bank(name, which):
             return psum.tile([P, BANK], F32, name=name, offset=4 * BANK * which)
 
+        def place(name, columns, dtype, kb):
+            return placed.tile([P, columns], dtype, name=name, offset=kb * KB, align_bytes=64)
+
         def tokens(b0, n):
             return offs_t[:, b0 * P // LIST_ROWS : (b0 + n) * P // LIST_ROWS]
 
         w2_plane_raw = keep.tile([P, H], U8, align_bytes=64)
-        dy_plane = keep.tile([P, T], U8, align_bytes=64)
+        dy_plane = place("dy_plane", T, U8, 36)
         w1_plane = keep.tile([P, E * K], U8, align_bytes=64)
         gate_blocks = keep.tile([P, P], F32)
         nc.gpsimd.memset(w2_plane_raw[P // 2 :, :].bitcast(I32), 0)
@@ -80,22 +83,24 @@ def tile_moe_sdb_relu_kernel(
             )
         nc.sync.dma_start(w2_raw[:].bitcast(I32), w2t_words[0].bitcast(I32))
         load_scale_rows(w2_plane_raw, w2t_scales, range(2, QUADRANTS))
-        dy_codes = keep.tile([P, 4 * T], U8, align_bytes=64)
+        dy_codes = place("dy_codes", 4 * T, U8, 31)
         nc.sync.dma_start(dy_codes[:].bitcast(I32), dy_words[0].rearrange("p t d -> p (t d)").bitcast(I32))
         load_scale_rows(dy_plane, dy_scales, range(QUADRANTS))
         offs_t = keep.tile([P, S // LIST_ROWS], U16)
         nc.sync.dma_start(offs_t[:], offs)
 
-        gate_rows = {}
-        for b0, n in VECTOR_GATHERS:
-            gate_rows[b0] = keep.tile([P, n * P], F32, name="gate_rows%d" % b0, align_bytes=64)
-            nc.sync.dma_start(gate_rows[b0][:], gate[:, b0 * P : (b0 + n) * P])
-        nc.sync.dma_start(gate_blocks[:TURNED, :], gate[0, : TURNED * P].rearrange("(b s) -> b s", s=P))
+        gate_rows = place("gate_rows", FIRST * P, F32, 40)
+        nc.sync.dma_start(gate_rows[:], gate[:, : FIRST * P])
         a_rows = a.rearrange("(p t) s -> p t s", t=PACK)
         a_t = {}
-        for b0, n in LOADS:
-            a_t[b0] = keep.tile([P, n * H], F32, name="a%d" % b0, align_bytes=64)
-            nc.sync.dma_start(a_t[b0][:].rearrange("p (t s) -> p t s", t=PACK), a_rows[:, :, b0 * P : (b0 + n) * P])
+        for b in range(0, BLOCKS, 2):
+            if b < WOVEN:
+                a_t[b] = place("a%d" % b, 2 * H, F32, 2 * b)
+            else:
+                a_t[b] = keep.tile([P, 2 * H], F32, name="a%d" % b, align_bytes=64)
+            nc.sync.dma_start(a_t[b][:].rearrange("p (t s) -> p t s", t=PACK), a_rows[:, :, b * P : (b + 2) * P])
+            if b == 0:
+                nc.sync.dma_start(gate_blocks[: BLOCKS - FIRST, :], gate[0, FIRST * P :].rearrange("(b s) -> b s", s=P))
         w1_codes = keep.tile([P, E, 2 * K], U8, align_bytes=64)
         nc.sync.dma_start(w1_codes[:].bitcast(I32), w1t_words[:, 0].rearrange("e p b -> p e b").bitcast(I32))
         for q in range(QUADRANTS):
@@ -108,7 +113,7 @@ def tile_moe_sdb_relu_kernel(
             pos_t.append(keep.tile([P, T // LIST_ROWS], U16, name="pos%d" % r))
             nc.sync.dma_start(pos_t[r][:], pos)
 
-        w2_codes = keep.tile([P, 2 * H], U8, align_bytes=64)
+        w2_codes = place("w2_codes", 2 * H, U8, 34)
         w2_plane = keep.tile([P, H], U8, align_bytes=64)
         for ts in (slice(0, 1), slice(1, PACK)):
             nc.vector.tensor_copy(
@@ -120,10 +125,10 @@ def tile_moe_sdb_relu_kernel(
                 w2_plane_raw[:].rearrange("p (m t) -> p t m", t=PACK)[:, ts, :],
             )
 
-        dc = [keep.tile([P, WINDOW], F32, name="dc%d" % t) for t in range(PACK)]
-        for t in range(PACK):
-            nc.vector.memset(dc[t][:, T:], 0.0)
+        dc = [keep.tile([P, T], F32, name="dc%d" % t) for t in range(PACK - 1)]
         products = [(t, t0, n) for t in range(PACK) for t0, n in (FIRST_TOKEN_BANKS if t == 0 else TOKEN_BANKS)]
+        gate_cols = keep.tile([P, BLOCKS - FIRST], F32, name="gate_cols", align_bytes=64)
+        factor = {0: keep.tile([P, 2 * H], F32, name="factor0", align_bytes=64)}
         for x, (t, t0, n) in enumerate(products):
             acc = bank("product%d" % x, x % BANKS)
             nc.tensor.matmul_mx(
@@ -135,24 +140,85 @@ def tile_moe_sdb_relu_kernel(
                 start=True,
                 stop=True,
             )
+            if t == len(dc):
+                nc.vector.scalar_tensor_tensor(
+                    factor[0][:].rearrange("p (t s) -> p t s", t=PACK),
+                    a_t[0][:].rearrange("p (t s) -> p t s", t=PACK),
+                    0.0,
+                    gate_rows[:].unsqueeze(1).to_broadcast([P, PACK, C]),
+                    ALU.is_gt,
+                    ALU.mult,
+                )
+                dc.append(place("dc3", T, F32, 40))
             if t == 0 and x % 2 == 0:
                 nc.vector.tensor_copy(dc[t][:, t0 : t0 + n], acc[:, :n])
             else:
                 nc.scalar.copy(dc[t][:, t0 : t0 + n], acc[:, :n])
 
-        gates_turned = bank("gates_turned", 7)
+        gates_turned = bank("gates_turned", 2)
         nc.tensor.transpose(gates_turned[:, :P], gate_blocks[:], identity[:])
-        gate_cols = keep.tile([P, TURNED], F32, name="gate_cols", align_bytes=64)
-        nc.scalar.copy(gate_cols[:], gates_turned[:, :TURNED])
+        nc.scalar.copy(gate_cols[:], gates_turned[:, : BLOCKS - FIRST])
 
-        gated = {b0: keep.tile([P, n * H], F32, name="gated%d" % b0, align_bytes=64) for b0, n in VECTOR_GATHERS}
-        for t in range(PACK):
-            for b0, n in VECTOR_GATHERS:
-                nc.vector.tensor_tensor(
-                    gated[b0][:, t * n * P : (t + 1) * n * P], dc[t][:].indirect(tokens(b0, n)), gate_rows[b0][:], ALU.mult
+        def gate_col(b):
+            return gate_cols[:, b - FIRST : b - FIRST + 1]
+
+        gate_bank = {}
+        for b0, where in GATE_BANKS:
+            gate_bank[b0] = bank("gate%d" % b0, where)
+            for j in range(4):
+                nc.tensor.transpose(
+                    gate_bank[b0][:, j * P : (j + 1) * P], gate_col(b0 + j).to_broadcast([P, P]), identity[:]
                 )
 
-        halves = [(b0, n, u) for b0, n in SCALAR_GATHERS for u in range(2)]
+        da = {0: place("da0", 8 * H, BF16, 20)}
+        plain_pair = {}
+
+        def blocks_of(tiles, b0, n):
+            first = max(b for b in tiles if b <= b0)
+            return tiles[first][:, (b0 - first) * H : (b0 - first + n) * H]
+
+        def gather_pair(b, engine_copy, tile):
+            plain_pair[b] = tile
+            for t in range(PACK):
+                engine_copy(tile[:, t * C : (t + 1) * C], dc[t][:].indirect(tokens(b, 2)))
+
+        def scalar_gather(dst, src):
+            nc.scalar.activation(dst, src, ACT.Copy)
+
+        def make_factor(b):
+            factor[b] = keep.tile([P, 2 * H], F32, name="factor%d" % b, align_bytes=64)
+            first = max(x for x in gate_bank if x <= b)
+            rows = gate_bank[first][:, (b - first) * P : (b - first + 2) * P]
+            nc.vector.scalar_tensor_tensor(
+                factor[b][:].rearrange("p (t s) -> p t s", t=PACK),
+                a_t[b][:].rearrange("p (t s) -> p t s", t=PACK),
+                0.0,
+                rows.unsqueeze(1).to_broadcast([P, PACK, C]),
+                ALU.is_gt,
+                ALU.mult,
+            )
+
+        def weave(b):
+            nc.gpsimd.tensor_tensor(
+                blocks_of(da, b, 2).rearrange("p (r i t) -> p r t i", i=PAIR, t=PACK),
+                plain_pair[b][:].rearrange("p (t r i) -> p r t i", i=PAIR, t=PACK),
+                factor[b][:].rearrange("p (t r i) -> p r t i", i=PAIR, t=PACK),
+                ALU.mult,
+            )
+
+        gather_pair(0, nc.vector.tensor_copy, keep.tile([P, 2 * H], F32, name="plain0", align_bytes=64))
+        weave(0)
+        gather_pair(2, scalar_gather, place("plain2", 2 * H, F32, 28))
+        make_factor(2)
+        weave(2)
+        for b in range(4, WOVEN, 2):
+            gather_pair(b, nc.vector.tensor_copy, place("plain%d" % b, 2 * H, F32, 2 * (b - 2)))
+            make_factor(b)
+            if b < 8:
+                weave(b)
+
+        halves = [(b0, n, u) for b0, n in TURNED_GATHERS for u in range(2)]
+        plain_at = [32, 36, 32, 36, 24, 26]
         plain = {}
         forth = {}
         back = {}
@@ -160,132 +226,125 @@ def tile_moe_sdb_relu_kernel(
         def gather_half(k):
             b0, n, u = halves[k]
             for e in range(2):
-                plain[k, e] = ring.tile([P, n * P], F32, name="plain", tag="plain%d" % e)
+                step = 2 if k < 4 else 1
+                plain[k, e] = place("plain%d_%d" % (k, e), n * P, F32, plain_at[k] + step * e)
                 nc.scalar.activation(plain[k, e][:], dc[2 * u + e][:].indirect(tokens(b0, n)), ACT.Copy)
             for e in range(2):
                 for b in range(b0, b0 + n, 2):
                     if (b, u) not in forth:
-                        forth[b, u] = bank("forth", FORTH[len(forth) % len(FORTH)])
-                    for place in range(2):
-                        at = (2 * place + e) * P
-                        source = plain[k, e][:, (b + place - b0) * P : (b + place - b0 + 1) * P]
+                        forth[b, u] = bank("forth", FORTH[len(forth)])
+                    for side in range(2):
+                        at = (2 * side + e) * P
+                        source = plain[k, e][:, (b + side - b0) * P : (b + side - b0 + 1) * P]
                         nc.tensor.transpose(forth[b, u][:, at : at + P], source, identity[:])
 
         def gate_half(k):
             b0, n, u = halves[k]
             for b in range(b0, b0 + n, 2):
                 turned = keep.tile([P, 2 * C], BF16, name="turned%d_%d" % (b, u), align_bytes=64)
-                for place in range(2):
+                for side in range(2):
                     nc.scalar.activation(
-                        turned[:, place * C : (place + 1) * C].rearrange("s (p e) -> s p e", e=2),
-                        forth[b, u][:, place * C : (place + 1) * C].rearrange("s (e p) -> s p e", e=2),
+                        turned[:, side * C : (side + 1) * C].rearrange("s (p e) -> s p e", e=2),
+                        forth[b, u][:, side * C : (side + 1) * C].rearrange("s (e p) -> s p e", e=2),
                         ACT.Copy,
-                        scale=gate_cols[:, b + place : b + place + 1],
+                        scale=gate_col(b + side),
                     )
                 if b not in back:
-                    back[b] = bank("back", BACK[len(back) % len(BACK)])
-                for place in range(2):
+                    back[b] = bank("back", BACK[b])
+                for side in range(2):
                     nc.tensor.transpose(
-                        back[b][:, place * C + u : (place + 1) * C : 2],
-                        turned[:].bitcast(F32)[:, place * P : (place + 1) * P],
+                        back[b][:, side * C + u : (side + 1) * C : 2],
+                        turned[:].bitcast(F32)[:, side * P : (side + 1) * P],
                         identity[:],
                     )
 
-        da = {}
-        mask = {}
-
-        def blocks_of(tiles, b0, n):
-            first = max(b for b in tiles if b <= b0)
-            return tiles[first][:, (b0 - first) * H : (b0 - first + n) * H]
-
-        def make_mask(b0, n):
-            mask[b0] = keep.tile([P, n * H], BF16, name="mask%d" % b0, align_bytes=64)
-            nc.vector.tensor_scalar(
-                mask[b0][:].rearrange("p (r i t) -> p r t i", i=RUN, t=PACK),
-                a_t[b0][:].rearrange("p (t r i) -> p r t i", i=RUN, t=PACK),
-                0.0,
-                None,
-                ALU.is_gt,
-            )
-
-        def mask_bank(b):
-            nc.vector.tensor_tensor(blocks_of(da, b, 2), back[b][:].bitcast(BF16), blocks_of(mask, b, 2), ALU.mult)
-
-        def mask_gated(b):
-            first = max(x for x in gated if x <= b)
+        def mask_bank(b, n):
+            first = b - b % 2
             nc.vector.scalar_tensor_tensor(
-                blocks_of(da, b, 2).rearrange("p (s t) -> p s t", t=PACK),
-                a_t[b][:].rearrange("p (t s) -> p s t", t=PACK),
+                blocks_of(da, b, n).rearrange("p (s t) -> p s t", t=PACK),
+                a_t[first][:].rearrange("p (t s) -> p s t", t=PACK)[:, (b - first) * P : (b - first + n) * P, :],
                 0.0,
-                gated[first][:].rearrange("p (t s) -> p s t", t=PACK)[:, (b - first) * P : (b - first + 2) * P, :],
+                back[first][:, (b - first) * C : (b - first + n) * C].bitcast(BF16).rearrange("p (s t) -> p s t", t=PACK),
                 ALU.is_gt,
                 ALU.mult,
             )
 
         dx = keep.tile([P, S], F32, name="dx", align_bytes=64)
-        codes = keep.tile([P, S], U32, name="codes", align_bytes=64)
+        codes = {0: keep.tile([P, WOVEN * P], U32, name="codes0", align_bytes=64)}
         plane = keep.tile([P, S], U8, name="plane", align_bytes=64)
+
+        def codes_of(s0, s1):
+            first = P * max(b for b in codes if b * P <= s0)
+            return codes[first // P][:, s0 - first : s1 - first].bitcast(FP8X4)
 
         def quantise(b0, n):
             s0, s1 = b0 * P, (b0 + n) * P
-            nc.vector.quantize_mx(out=codes[:, s0:s1].bitcast(FP8X4), scales=plane[:, s0:s1], in_=blocks_of(da, b0, n))
+            nc.vector.quantize_mx(out=codes_of(s0, s1), scales=plane[:, s0:s1], in_=blocks_of(da, b0, n))
 
-        def experts(b0, n, where, empty):
+        sums = {}
+
+        def experts(b0, n, where):
             s0, s1 = b0 * P, (b0 + n) * P
-            acc = bank("sums%d" % b0, where)
+            sums[b0] = bank("sums%d" % b0, where)
             width = min(n * P, C)
             for v0 in range(s0, s1, width):
                 e = v0 // C
                 nc.tensor.matmul_mx(
-                    out=acc[:, v0 - s0 : v0 - s0 + width],
+                    out=sums[b0][:, v0 - s0 : v0 - s0 + width],
                     lhsT=w1_codes[:, e, :].bitcast(FP4X4),
                     lhsT_scale=w1_plane[:, K * e : K * (e + 1)],
-                    rhs=codes[:, v0 : v0 + width].bitcast(FP8X4),
+                    rhs=codes_of(v0, v0 + width),
                     rhs_scale=plane[:, v0 : v0 + width],
                     start=True,
                     stop=True,
                 )
-            empty(dx[:, s0:s1], acc[:, : n * P])
 
-        for b0, n in SCALAR_GATHERS + VECTOR_GATHERS:
-            da[b0] = keep.tile([P, n * H], BF16, name="da%d" % b0, align_bytes=64)
+        def empty(b0, n, copy):
+            copy(dx[:, b0 * P : (b0 + n) * P], sums[b0][:, : n * P])
 
         gather_half(0)
         gather_half(1)
         gate_half(0)
         gather_half(2)
         gate_half(1)
-        make_mask(0, 4)
-        mask_gated(10)
-        mask_bank(0)
-        mask_bank(2)
-        mask_gated(12)
-        quantise(0, 4)
-        quantise(10, 4)
         gather_half(3)
         gate_half(2)
-        gather_half(4)
         gate_half(3)
-        make_mask(4, 4)
-        make_mask(8, 2)
-        mask_gated(14)
-        mask_bank(4)
-        mask_bank(6)
+        quantise(0, 8)
+        experts(0, 4, 1)
+        experts(4, 4, 0)
+        da[8] = place("da8", 2 * H, BF16, 20)
+        weave(8)
+        da[10] = place("da10", 4 * H, BF16, 8)
+        da[14] = place("da14", 2 * H, BF16, 22)
+        mask_bank(10, 2)
+        mask_bank(12, 2)
+        mask_bank(14, 2)
+        gather_half(4)
         gather_half(5)
         gate_half(4)
         gate_half(5)
-        mask_gated(16)
-        quantise(4, 4)
-        mask_bank(8)
-        quantise(14, 4)
-        quantise(8, 1)
-        quantise(9, 1)
-        experts(0, 4, 2, nc.scalar.copy)
-        experts(10, 4, 3, nc.scalar.copy)
-        experts(4, 4, 0, nc.scalar.copy)
-        experts(14, 4, 1, nc.scalar.copy)
-        experts(8, 1, 7, nc.vector.tensor_copy)
-        experts(9, 1, 6, nc.scalar.copy)
+        codes[10] = place("codes10", 8 * P, U32, 12)
+        quantise(8, 2)
+        quantise(10, 4)
+        quantise(14, 2)
+        da[16] = place("da16", 2 * H, BF16, 20)
+        mask_bank(16, 1)
+        mask_bank(17, 1)
+        quantise(16, 1)
+        quantise(17, 1)
+        experts(8, 2, 6)
+        experts(10, 4, 7)
+        experts(14, 2, 4)
+        experts(16, 1, 5)
+        experts(17, 1, 2)
+        empty(0, 4, nc.scalar.copy)
+        empty(4, 4, nc.scalar.copy)
+        empty(8, 2, nc.scalar.copy)
+        empty(10, 4, nc.scalar.copy)
+        empty(14, 2, nc.scalar.copy)
+        empty(16, 1, nc.vector.tensor_copy)
+        empty(17, 1, nc.scalar.copy)
 
         def columns(t0, n):
             return slice(t0 // LIST_ROWS, (t0 + n) // LIST_ROWS)

@@ -26,16 +26,14 @@ ACT = mybir.ActivationFunctionType
 
 BLOCKS = S // P
 PAIR = 4
-WOVEN = 10
+POOLED = 8
 FIRST = 2
-TURNED_GATHERS = [(10, 4), (14, 2), (16, 2)]
-FORTH = [2, 3, 4, 5, 2, 3, 5, 2]
-BACK = {10: 6, 12: 7, 14: 4, 16: 3}
-GATE_BANKS = [(2, 1), (6, 0)]
+GATE_BANKS = [((2, 3, 4, 5), 1), ((6, 7, 16, 17), 0), ((8, 9, 10, 11), 3), ((12, 13, 14, 15), 4)]
 TOKEN_BANKS = [(0, 512), (512, 256)]
 FIRST_TOKEN_BANKS = [(0, 256), (256, 256), (512, 128), (640, 128)]
+VECTOR_PRODUCTS = (0, 2, 5)
 ALONE = (0, 160)
-SHARED = [(160, 256), (416, 224), (640, 128)]
+SHARED = [(160, 128), (288, 352), (640, 128)]
 KB = 1024
 
 
@@ -53,16 +51,16 @@ def tile_moe_sdb_relu_kernel(
             return psum.tile([P, BANK], F32, name=name, offset=4 * BANK * which)
 
         def place(name, columns, dtype, kb):
-            return placed.tile([P, columns], dtype, name=name, offset=kb * KB, align_bytes=64)
+            return placed.tile([P, columns], dtype, name=name, offset=int(kb * KB), align_bytes=64)
 
         def tokens(b0, n):
             return offs_t[:, b0 * P // LIST_ROWS : (b0 + n) * P // LIST_ROWS]
 
-        w2_plane_raw = keep.tile([P, H], U8, align_bytes=64)
-        dy_plane = place("dy_plane", T, U8, 36)
+        w2_plane_raw = keep.tile([P, 2 * H], U8, align_bytes=64)
+        dy_plane = keep.tile([P, T], U8, align_bytes=64)
         w1_plane = keep.tile([P, E * K], U8, align_bytes=64)
         gate_blocks = keep.tile([P, P], F32)
-        nc.gpsimd.memset(w2_plane_raw[P // 2 :, :].bitcast(I32), 0)
+        nc.gpsimd.memset(w2_plane_raw[: P // 2, :].bitcast(I32), 0)
         nc.vector.memset(dy_plane[:].bitcast(I32), 0)
         nc.vector.memset(w1_plane[:].bitcast(I32), 0)
         nc.gpsimd.memset(gate_blocks[:], 0.0)
@@ -78,29 +76,32 @@ def tile_moe_sdb_relu_kernel(
         w2_raw = keep.tile([P, 2 * H], U8, align_bytes=64)
         for q in range(2):
             nc.sync.dma_start(
-                w2_plane_raw[32 * q : 32 * (q + 1), :].bitcast(I32),
-                w2t_scales[0, 4 * q : 4 * q + 4, :].bitcast(I32).partition_broadcast(8),
+                w2_plane_raw[32 * q : 32 * q + 4, :].bitcast(I32).rearrange("r (h c) -> r h c", h=2),
+                w2t_scales[0].bitcast(I32).rearrange("(h q r) c -> q r h c", h=2, q=2)[q],
             )
         nc.sync.dma_start(w2_raw[:].bitcast(I32), w2t_words[0].bitcast(I32))
-        load_scale_rows(w2_plane_raw, w2t_scales, range(2, QUADRANTS))
-        dy_codes = place("dy_codes", 4 * T, U8, 31)
+        dy_codes = place("dy_codes", 4 * T, U8, 19)
         nc.sync.dma_start(dy_codes[:].bitcast(I32), dy_words[0].rearrange("p t d -> p (t d)").bitcast(I32))
         load_scale_rows(dy_plane, dy_scales, range(QUADRANTS))
         offs_t = keep.tile([P, S // LIST_ROWS], U16)
         nc.sync.dma_start(offs_t[:], offs)
 
-        gate_rows = place("gate_rows", FIRST * P, F32, 40)
+        gate_rows = keep.tile([P, FIRST * P], F32, align_bytes=64)
         nc.sync.dma_start(gate_rows[:], gate[:, : FIRST * P])
         a_rows = a.rearrange("(p t) s -> p t s", t=PACK)
         a_t = {}
-        for b in range(0, BLOCKS, 2):
-            if b < WOVEN:
-                a_t[b] = place("a%d" % b, 2 * H, F32, 2 * b)
+        a_at = {0: 12, 4: 30, 16: 8}
+
+        def load_a(b, n=2):
+            if b in a_at:
+                a_t[b] = place("a%d" % b, n * H, F32, a_at[b])
             else:
-                a_t[b] = keep.tile([P, 2 * H], F32, name="a%d" % b, align_bytes=64)
-            nc.sync.dma_start(a_t[b][:].rearrange("p (t s) -> p t s", t=PACK), a_rows[:, :, b * P : (b + 2) * P])
-            if b == 0:
-                nc.sync.dma_start(gate_blocks[: BLOCKS - FIRST, :], gate[0, FIRST * P :].rearrange("(b s) -> b s", s=P))
+                a_t[b] = keep.tile([P, n * H], F32, name="a%d" % b, align_bytes=64)
+            nc.sync.dma_start(a_t[b][:].rearrange("p (t s) -> p t s", t=PACK), a_rows[:, :, b * P : (b + n) * P])
+
+        load_a(0)
+        nc.sync.dma_start(gate_blocks[: BLOCKS - FIRST, :], gate[0, FIRST * P :].rearrange("(b s) -> b s", s=P))
+        load_a(2)
         w1_codes = keep.tile([P, E, 2 * K], U8, align_bytes=64)
         nc.sync.dma_start(w1_codes[:].bitcast(I32), w1t_words[:, 0].rearrange("e p b -> p e b").bitcast(I32))
         for q in range(QUADRANTS):
@@ -108,13 +109,16 @@ def tile_moe_sdb_relu_kernel(
                 w1_plane[32 * q : 32 * q + 4, :].rearrange("r (e k) -> r e k", e=E).bitcast(I32),
                 w1t_scales[:, 0, 4 * q : 4 * q + 4, :].rearrange("e r k -> r e k").bitcast(I32),
             )
+        for b, n in ((4, 2), (6, 2), (8, 4), (12, 4), (16, 2)):
+            load_a(b, n)
         pos_t = []
         for r, pos in enumerate((pos1, pos2, pos3)):
             pos_t.append(keep.tile([P, T // LIST_ROWS], U16, name="pos%d" % r))
             nc.sync.dma_start(pos_t[r][:], pos)
 
-        w2_codes = place("w2_codes", 2 * H, U8, 34)
+        w2_codes = keep.tile([P, 2 * H], U8, align_bytes=64)
         w2_plane = keep.tile([P, H], U8, align_bytes=64)
+        nc.vector.tensor_copy(w2_plane_raw[P // 2 :, :H].bitcast(I32), w2_plane_raw[: P // 2, H:].bitcast(I32))
         for ts in (slice(0, 1), slice(1, PACK)):
             nc.vector.tensor_copy(
                 w2_codes[:].bitcast(U16).rearrange("p (t m) -> p t m", t=PACK)[:, ts, :],
@@ -122,13 +126,11 @@ def tile_moe_sdb_relu_kernel(
             )
             nc.vector.tensor_copy(
                 w2_plane[:].rearrange("p (t m) -> p t m", t=PACK)[:, ts, :],
-                w2_plane_raw[:].rearrange("p (m t) -> p t m", t=PACK)[:, ts, :],
+                w2_plane_raw[:, :H].rearrange("p (m t) -> p t m", t=PACK)[:, ts, :],
             )
 
-        dc = [keep.tile([P, T], F32, name="dc%d" % t) for t in range(PACK - 1)]
+        dc = [keep.tile([P, T], F32, name="dc%d" % t) for t in range(PACK)]
         products = [(t, t0, n) for t in range(PACK) for t0, n in (FIRST_TOKEN_BANKS if t == 0 else TOKEN_BANKS)]
-        gate_cols = keep.tile([P, BLOCKS - FIRST], F32, name="gate_cols", align_bytes=64)
-        factor = {0: keep.tile([P, 2 * H], F32, name="factor0", align_bytes=64)}
         for x, (t, t0, n) in enumerate(products):
             acc = bank("product%d" % x, x % BANKS)
             nc.tensor.matmul_mx(
@@ -140,21 +142,12 @@ def tile_moe_sdb_relu_kernel(
                 start=True,
                 stop=True,
             )
-            if t == len(dc):
-                nc.vector.scalar_tensor_tensor(
-                    factor[0][:].rearrange("p (t s) -> p t s", t=PACK),
-                    a_t[0][:].rearrange("p (t s) -> p t s", t=PACK),
-                    0.0,
-                    gate_rows[:].unsqueeze(1).to_broadcast([P, PACK, C]),
-                    ALU.is_gt,
-                    ALU.mult,
-                )
-                dc.append(place("dc3", T, F32, 40))
-            if t == 0 and x % 2 == 0:
+            if x in VECTOR_PRODUCTS:
                 nc.vector.tensor_copy(dc[t][:, t0 : t0 + n], acc[:, :n])
             else:
                 nc.scalar.copy(dc[t][:, t0 : t0 + n], acc[:, :n])
 
+        gate_cols = keep.tile([P, BLOCKS - FIRST], F32, name="gate_cols", align_bytes=64)
         gates_turned = bank("gates_turned", 2)
         nc.tensor.transpose(gates_turned[:, :P], gate_blocks[:], identity[:])
         nc.scalar.copy(gate_cols[:], gates_turned[:, : BLOCKS - FIRST])
@@ -162,120 +155,70 @@ def tile_moe_sdb_relu_kernel(
         def gate_col(b):
             return gate_cols[:, b - FIRST : b - FIRST + 1]
 
-        gate_bank = {}
-        for b0, where in GATE_BANKS:
-            gate_bank[b0] = bank("gate%d" % b0, where)
-            for j in range(4):
-                nc.tensor.transpose(
-                    gate_bank[b0][:, j * P : (j + 1) * P], gate_col(b0 + j).to_broadcast([P, P]), identity[:]
-                )
+        gate_spread = {}
+        for blocks, where in GATE_BANKS:
+            rows = bank("gate%d" % blocks[0], where)
+            for j, b in enumerate(blocks):
+                gate_spread[b] = (rows, j)
+                nc.tensor.transpose(rows[:, j * P : (j + 1) * P], gate_col(b).to_broadcast([P, P]), identity[:])
 
-        da = {0: place("da0", 8 * H, BF16, 20)}
-        plain_pair = {}
+        da = {0: place("da0", POOLED * H, BF16, 40)}
+        plain = {}
+        factor = {}
 
         def blocks_of(tiles, b0, n):
             first = max(b for b in tiles if b <= b0)
             return tiles[first][:, (b0 - first) * H : (b0 - first + n) * H]
 
-        def gather_pair(b, engine_copy, tile):
-            plain_pair[b] = tile
-            for t in range(PACK):
-                engine_copy(tile[:, t * C : (t + 1) * C], dc[t][:].indirect(tokens(b, 2)))
-
         def scalar_gather(dst, src):
             nc.scalar.activation(dst, src, ACT.Copy)
 
-        def make_factor(b):
-            factor[b] = keep.tile([P, 2 * H], F32, name="factor%d" % b, align_bytes=64)
-            first = max(x for x in gate_bank if x <= b)
-            rows = gate_bank[first][:, (b - first) * P : (b - first + 2) * P]
-            nc.vector.scalar_tensor_tensor(
-                factor[b][:].rearrange("p (t s) -> p t s", t=PACK),
-                a_t[b][:].rearrange("p (t s) -> p t s", t=PACK),
-                0.0,
-                rows.unsqueeze(1).to_broadcast([P, PACK, C]),
-                ALU.is_gt,
+        def gather(b0, n, planes, copy):
+            for t in planes:
+                copy(plain[b0][:, t * n * P : (t + 1) * n * P], dc[t][:].indirect(tokens(b0, n)))
+
+        def planes_of(b, n):
+            first = max(x for x in plain if x <= b)
+            return plain[first][:].rearrange("p (t s) -> p t s", t=PACK)[:, :, (b - first) * P : (b - first + n) * P]
+
+        def make_factor(b, n, tile=None):
+            factor[b] = tile or keep.tile([P, n * H], F32, name="factor%d" % b, align_bytes=64)
+            if b < FIRST:
+                rows = gate_rows[:]
+            else:
+                spread, j = gate_spread[b]
+                rows = spread[:, j * P : (j + n) * P]
+            if b < POOLED:
+                made = factor[b][:].rearrange("p (t s) -> p t s", t=PACK)
+                values = a_t[b][:].rearrange("p (t s) -> p t s", t=PACK)
+                gates = rows.unsqueeze(1).to_broadcast([P, PACK, n * P])
+            else:
+                made = factor[b][:].rearrange("p (s t) -> p s t", t=PACK)
+                values = a_t[b][:].rearrange("p (t s) -> p s t", t=PACK)
+                gates = rows.unsqueeze(2).to_broadcast([P, n * P, PACK])
+            nc.vector.scalar_tensor_tensor(made, values, 0.0, gates, ALU.is_gt, ALU.mult)
+
+        def multiply(b, n):
+            nc.vector.tensor_tensor(
+                blocks_of(da, b, n).rearrange("p (s t) -> p s t", t=PACK),
+                planes_of(b, n).rearrange("p t s -> p s t"),
+                blocks_of(factor, b, n).rearrange("p (s t) -> p s t", t=PACK),
                 ALU.mult,
             )
 
         def weave(b):
             nc.gpsimd.tensor_tensor(
                 blocks_of(da, b, 2).rearrange("p (r i t) -> p r t i", i=PAIR, t=PACK),
-                plain_pair[b][:].rearrange("p (t r i) -> p r t i", i=PAIR, t=PACK),
+                planes_of(b, 2).rearrange("p t (r i) -> p r t i", i=PAIR),
                 factor[b][:].rearrange("p (t r i) -> p r t i", i=PAIR, t=PACK),
                 ALU.mult,
             )
 
-        gather_pair(0, nc.vector.tensor_copy, keep.tile([P, 2 * H], F32, name="plain0", align_bytes=64))
-        weave(0)
-        gather_pair(2, scalar_gather, place("plain2", 2 * H, F32, 28))
-        make_factor(2)
-        weave(2)
-        for b in range(4, WOVEN, 2):
-            gather_pair(b, nc.vector.tensor_copy, place("plain%d" % b, 2 * H, F32, 2 * (b - 2)))
-            make_factor(b)
-            if b < 8:
-                weave(b)
-
-        halves = [(b0, n, u) for b0, n in TURNED_GATHERS for u in range(2)]
-        plain_at = [32, 36, 32, 36, 24, 26]
-        plain = {}
-        forth = {}
-        back = {}
-
-        def gather_half(k):
-            b0, n, u = halves[k]
-            for e in range(2):
-                step = 2 if k < 4 else 1
-                plain[k, e] = place("plain%d_%d" % (k, e), n * P, F32, plain_at[k] + step * e)
-                nc.scalar.activation(plain[k, e][:], dc[2 * u + e][:].indirect(tokens(b0, n)), ACT.Copy)
-            for e in range(2):
-                for b in range(b0, b0 + n, 2):
-                    if (b, u) not in forth:
-                        forth[b, u] = bank("forth", FORTH[len(forth)])
-                    for side in range(2):
-                        at = (2 * side + e) * P
-                        source = plain[k, e][:, (b + side - b0) * P : (b + side - b0 + 1) * P]
-                        nc.tensor.transpose(forth[b, u][:, at : at + P], source, identity[:])
-
-        def gate_half(k):
-            b0, n, u = halves[k]
-            for b in range(b0, b0 + n, 2):
-                turned = keep.tile([P, 2 * C], BF16, name="turned%d_%d" % (b, u), align_bytes=64)
-                for side in range(2):
-                    nc.scalar.activation(
-                        turned[:, side * C : (side + 1) * C].rearrange("s (p e) -> s p e", e=2),
-                        forth[b, u][:, side * C : (side + 1) * C].rearrange("s (e p) -> s p e", e=2),
-                        ACT.Copy,
-                        scale=gate_col(b + side),
-                    )
-                if b not in back:
-                    back[b] = bank("back", BACK[b])
-                for side in range(2):
-                    nc.tensor.transpose(
-                        back[b][:, side * C + u : (side + 1) * C : 2],
-                        turned[:].bitcast(F32)[:, side * P : (side + 1) * P],
-                        identity[:],
-                    )
-
-        def mask_bank(b, n):
-            first = b - b % 2
-            nc.vector.scalar_tensor_tensor(
-                blocks_of(da, b, n).rearrange("p (s t) -> p s t", t=PACK),
-                a_t[first][:].rearrange("p (t s) -> p s t", t=PACK)[:, (b - first) * P : (b - first + n) * P, :],
-                0.0,
-                back[first][:, (b - first) * C : (b - first + n) * C].bitcast(BF16).rearrange("p (s t) -> p s t", t=PACK),
-                ALU.is_gt,
-                ALU.mult,
-            )
-
         dx = keep.tile([P, S], F32, name="dx", align_bytes=64)
-        codes = {0: keep.tile([P, WOVEN * P], U32, name="codes0", align_bytes=64)}
         plane = keep.tile([P, S], U8, name="plane", align_bytes=64)
 
         def codes_of(s0, s1):
-            first = P * max(b for b in codes if b * P <= s0)
-            return codes[first // P][:, s0 - first : s1 - first].bitcast(FP8X4)
+            return codes[:, s0:s1].bitcast(FP8X4)
 
         def quantise(b0, n):
             s0, s1 = b0 * P, (b0 + n) * P
@@ -283,14 +226,16 @@ def tile_moe_sdb_relu_kernel(
 
         sums = {}
 
-        def experts(b0, n, where):
-            s0, s1 = b0 * P, (b0 + n) * P
-            sums[b0] = bank("sums%d" % b0, where)
+        def experts(b0, n, where=None):
+            if where is not None:
+                sums[b0] = bank("sums%d" % b0, where)
+            first = max(x for x in sums if x <= b0)
+            s0 = first * P
             width = min(n * P, C)
-            for v0 in range(s0, s1, width):
+            for v0 in range(b0 * P, (b0 + n) * P, width):
                 e = v0 // C
                 nc.tensor.matmul_mx(
-                    out=sums[b0][:, v0 - s0 : v0 - s0 + width],
+                    out=sums[first][:, v0 - s0 : v0 - s0 + width],
                     lhsT=w1_codes[:, e, :].bitcast(FP4X4),
                     lhsT_scale=w1_plane[:, K * e : K * (e + 1)],
                     rhs=codes_of(v0, v0 + width),
@@ -302,47 +247,58 @@ def tile_moe_sdb_relu_kernel(
         def empty(b0, n, copy):
             copy(dx[:, b0 * P : (b0 + n) * P], sums[b0][:, : n * P])
 
-        gather_half(0)
-        gather_half(1)
-        gate_half(0)
-        gather_half(2)
-        gate_half(1)
-        gather_half(3)
-        gate_half(2)
-        gate_half(3)
+        plain[0] = keep.tile([P, 2 * H], F32, name="plain0", align_bytes=64)
+        gather(0, 2, range(2), nc.vector.tensor_copy)
+        gather(0, 2, range(2, PACK), scalar_gather)
+        make_factor(0, 2)
+        weave(0)
+        plain[2] = place("plain2", 2 * H, F32, 20)
+        gather(2, 2, range(PACK), scalar_gather)
+        plain[4] = place("plain4", 4 * H, F32, 12)
+        gather(4, 4, range(2), nc.vector.tensor_copy)
+        gather(4, 4, range(2, PACK), scalar_gather)
+        make_factor(2, 2)
+        weave(2)
+        make_factor(4, 2)
+        weave(4)
+        make_factor(6, 2, place("factor6", 2 * H, F32, 48))
+        weave(6)
+        plain[8] = place("plain8", 4 * H, F32, 24)
+        gather(8, 4, range(PACK), scalar_gather)
+        plain[12] = place("plain12", 4 * H, F32, 32)
+        gather(12, 4, range(PACK), scalar_gather)
+        make_factor(8, 4)
+        make_factor(12, 4)
+        make_factor(16, 2)
+        codes = place("codes", S, U32, 1)
         quantise(0, 8)
-        experts(0, 4, 1)
-        experts(4, 4, 0)
-        da[8] = place("da8", 2 * H, BF16, 20)
-        weave(8)
-        da[10] = place("da10", 4 * H, BF16, 8)
-        da[14] = place("da14", 2 * H, BF16, 22)
-        mask_bank(10, 2)
-        mask_bank(12, 2)
-        mask_bank(14, 2)
-        gather_half(4)
-        gather_half(5)
-        gate_half(4)
-        gate_half(5)
-        codes[10] = place("codes10", 8 * P, U32, 12)
-        quantise(8, 2)
-        quantise(10, 4)
+        experts(0, 4, 5)
+        experts(4, 4, 6)
+        da[8] = place("da8", 4 * H, BF16, 10)
+        da[12] = place("da12", 4 * H, BF16, 44)
+        da[16] = place("da16", 2 * H, BF16, 48)
+        multiply(8, 4)
+        plain[16] = place("plain16", 2 * H, F32, 40)
+        gather(16, 2, range(1), nc.vector.tensor_copy)
+        gather(16, 2, range(1, PACK), scalar_gather)
+        quantise(8, 4)
+        experts(8, 4, 7)
+        multiply(12, 2)
+        multiply(14, 2)
+        quantise(12, 2)
+        experts(12, 2, 2)
+        multiply(16, 1)
         quantise(14, 2)
-        da[16] = place("da16", 2 * H, BF16, 20)
-        mask_bank(16, 1)
-        mask_bank(17, 1)
+        experts(14, 2)
+        multiply(17, 1)
         quantise(16, 1)
         quantise(17, 1)
-        experts(8, 2, 6)
-        experts(10, 4, 7)
-        experts(14, 2, 4)
-        experts(16, 1, 5)
-        experts(17, 1, 2)
+        experts(16, 1, 1)
+        experts(17, 1, 3)
         empty(0, 4, nc.scalar.copy)
         empty(4, 4, nc.scalar.copy)
-        empty(8, 2, nc.scalar.copy)
-        empty(10, 4, nc.scalar.copy)
-        empty(14, 2, nc.scalar.copy)
+        empty(8, 4, nc.scalar.copy)
+        empty(12, 4, nc.scalar.copy)
         empty(16, 1, nc.vector.tensor_copy)
         empty(17, 1, nc.scalar.copy)
 
@@ -354,17 +310,28 @@ def tile_moe_sdb_relu_kernel(
             for r in range(2):
                 fetched[t0, r] = keep.tile([P, n], F32, name="fetched%d_%d" % (t0, r))
                 nc.scalar.activation(fetched[t0, r][:], dx[:].indirect(pos_t[r][:, columns(t0, n)]), ACT.Copy)
+        def fetch_third(t0, n):
+            fetched[t0, 2] = keep.tile([P, n], F32, name="part%d" % t0)
+            nc.vector.tensor_tensor(
+                fetched[t0, 2][:], dx[:].indirect(pos_t[2][:, columns(t0, n)]), fetched[t0, 0][:], ALU.add
+            )
+
+        def finish(t0, n):
+            whole = keep.tile([P, n], F32, name="whole%d" % t0)
+            nc.vector.tensor_tensor(whole[:], fetched[t0, 2][:], fetched[t0, 1][:], ALU.add)
+            nc.sync.dma_start(out[:, t0 : t0 + n], whole[:])
+
         t0, n = ALONE
         one = keep.tile([P, n], F32)
         two = keep.tile([P, n], F32)
         three = keep.tile([P, n], F32)
         nc.vector.tensor_copy(one[:], dx[:].indirect(pos_t[0][:, columns(t0, n)]))
+        fetch_third(*SHARED[0])
         nc.vector.tensor_tensor(two[:], dx[:].indirect(pos_t[1][:, columns(t0, n)]), one[:], ALU.add)
+        finish(*SHARED[0])
         nc.vector.tensor_tensor(three[:], dx[:].indirect(pos_t[2][:, columns(t0, n)]), two[:], ALU.add)
         nc.sync.dma_start(out[:, t0 : t0 + n], three[:])
-        for t0, n in SHARED:
-            part = keep.tile([P, n], F32, name="part%d" % t0)
-            whole = keep.tile([P, n], F32, name="whole%d" % t0)
-            nc.vector.tensor_tensor(part[:], dx[:].indirect(pos_t[2][:, columns(t0, n)]), fetched[t0, 0][:], ALU.add)
-            nc.vector.tensor_tensor(whole[:], part[:], fetched[t0, 1][:], ALU.add)
-            nc.sync.dma_start(out[:, t0 : t0 + n], whole[:])
+        fetch_third(*SHARED[1])
+        fetch_third(*SHARED[2])
+        finish(*SHARED[1])
+        finish(*SHARED[2])

@@ -26,14 +26,14 @@ ACT = mybir.ActivationFunctionType
 
 BLOCKS = S // P
 PAIR = 4
-POOLED = 8
+POOLED = 7
 FIRST = 2
 GATE_BANKS = [((2, 3, 4, 5), 1), ((6, 7, 16, 17), 0), ((8, 9, 10, 11), 3), ((12, 13, 14, 15), 4)]
 TOKEN_BANKS = [(0, 512), (512, 256)]
 FIRST_TOKEN_BANKS = [(0, 256), (256, 256), (512, 128), (640, 128)]
 VECTOR_PRODUCTS = (0, 2, 5)
 ALONE = (0, 160)
-SHARED = [(160, 128), (288, 352), (640, 128)]
+SHARED = [(160, 192), (352, 256), (608, 160)]
 KB = 1024
 
 
@@ -56,11 +56,11 @@ def tile_moe_sdb_relu_kernel(
         def tokens(b0, n):
             return offs_t[:, b0 * P // LIST_ROWS : (b0 + n) * P // LIST_ROWS]
 
-        w2_plane_raw = keep.tile([P, 2 * H], U8, align_bytes=64)
+        w2_plane_raw = keep.tile([P, H], U8, align_bytes=64)
         dy_plane = keep.tile([P, T], U8, align_bytes=64)
         w1_plane = keep.tile([P, E * K], U8, align_bytes=64)
         gate_blocks = keep.tile([P, P], F32)
-        nc.gpsimd.memset(w2_plane_raw[: P // 2, :].bitcast(I32), 0)
+        nc.gpsimd.memset(w2_plane_raw[P // 2 :, :].bitcast(I32), 0)
         nc.vector.memset(dy_plane[:].bitcast(I32), 0)
         nc.vector.memset(w1_plane[:].bitcast(I32), 0)
         nc.gpsimd.memset(gate_blocks[:], 0.0)
@@ -76,11 +76,12 @@ def tile_moe_sdb_relu_kernel(
         w2_raw = keep.tile([P, 2 * H], U8, align_bytes=64)
         for q in range(2):
             nc.sync.dma_start(
-                w2_plane_raw[32 * q : 32 * q + 4, :].bitcast(I32).rearrange("r (h c) -> r h c", h=2),
-                w2t_scales[0].bitcast(I32).rearrange("(h q r) c -> q r h c", h=2, q=2)[q],
+                w2_plane_raw[32 * q : 32 * (q + 1), :].bitcast(I32),
+                w2t_scales[0, 4 * q : 4 * q + 4, :].bitcast(I32).partition_broadcast(8),
             )
         nc.sync.dma_start(w2_raw[:].bitcast(I32), w2t_words[0].bitcast(I32))
-        dy_codes = place("dy_codes", 4 * T, U8, 19)
+        load_scale_rows(w2_plane_raw, w2t_scales, range(2, QUADRANTS))
+        dy_codes = place("dy_codes", 4 * T, U8, 20)
         nc.sync.dma_start(dy_codes[:].bitcast(I32), dy_words[0].rearrange("p t d -> p (t d)").bitcast(I32))
         load_scale_rows(dy_plane, dy_scales, range(QUADRANTS))
         offs_t = keep.tile([P, S // LIST_ROWS], U16)
@@ -90,7 +91,7 @@ def tile_moe_sdb_relu_kernel(
         nc.sync.dma_start(gate_rows[:], gate[:, : FIRST * P])
         a_rows = a.rearrange("(p t) s -> p t s", t=PACK)
         a_t = {}
-        a_at = {0: 12, 4: 30, 16: 8}
+        a_at = {0: 13, 4: 31, 6: 52, 16: 9}
 
         def load_a(b, n=2):
             if b in a_at:
@@ -118,7 +119,6 @@ def tile_moe_sdb_relu_kernel(
 
         w2_codes = keep.tile([P, 2 * H], U8, align_bytes=64)
         w2_plane = keep.tile([P, H], U8, align_bytes=64)
-        nc.vector.tensor_copy(w2_plane_raw[P // 2 :, :H].bitcast(I32), w2_plane_raw[: P // 2, H:].bitcast(I32))
         for ts in (slice(0, 1), slice(1, PACK)):
             nc.vector.tensor_copy(
                 w2_codes[:].bitcast(U16).rearrange("p (t m) -> p t m", t=PACK)[:, ts, :],
@@ -126,7 +126,7 @@ def tile_moe_sdb_relu_kernel(
             )
             nc.vector.tensor_copy(
                 w2_plane[:].rearrange("p (t m) -> p t m", t=PACK)[:, ts, :],
-                w2_plane_raw[:, :H].rearrange("p (m t) -> p t m", t=PACK)[:, ts, :],
+                w2_plane_raw[:].rearrange("p (m t) -> p t m", t=PACK)[:, ts, :],
             )
 
         dc = [keep.tile([P, T], F32, name="dc%d" % t) for t in range(PACK)]
@@ -150,7 +150,7 @@ def tile_moe_sdb_relu_kernel(
         gate_cols = keep.tile([P, BLOCKS - FIRST], F32, name="gate_cols", align_bytes=64)
         gates_turned = bank("gates_turned", 2)
         nc.tensor.transpose(gates_turned[:, :P], gate_blocks[:], identity[:])
-        nc.scalar.copy(gate_cols[:], gates_turned[:, : BLOCKS - FIRST])
+        nc.vector.tensor_copy(gate_cols[:], gates_turned[:, : BLOCKS - FIRST])
 
         def gate_col(b):
             return gate_cols[:, b - FIRST : b - FIRST + 1]
@@ -162,7 +162,7 @@ def tile_moe_sdb_relu_kernel(
                 gate_spread[b] = (rows, j)
                 nc.tensor.transpose(rows[:, j * P : (j + 1) * P], gate_col(b).to_broadcast([P, P]), identity[:])
 
-        da = {0: place("da0", POOLED * H, BF16, 40)}
+        da = {0: place("da0", POOLED * H, BF16, 44.5)}
         plain = {}
         factor = {}
 
@@ -188,28 +188,26 @@ def tile_moe_sdb_relu_kernel(
             else:
                 spread, j = gate_spread[b]
                 rows = spread[:, j * P : (j + n) * P]
-            if b < POOLED:
-                made = factor[b][:].rearrange("p (t s) -> p t s", t=PACK)
-                values = a_t[b][:].rearrange("p (t s) -> p t s", t=PACK)
-                gates = rows.unsqueeze(1).to_broadcast([P, PACK, n * P])
-            else:
-                made = factor[b][:].rearrange("p (s t) -> p s t", t=PACK)
-                values = a_t[b][:].rearrange("p (t s) -> p s t", t=PACK)
-                gates = rows.unsqueeze(2).to_broadcast([P, n * P, PACK])
+            made = factor[b][:].rearrange("p (t s) -> p t s", t=PACK)
+            first = max(x for x in a_t if x <= b)
+            values = a_t[first][:].rearrange("p (t s) -> p t s", t=PACK)[:, :, (b - first) * P : (b - first + n) * P]
+            gates = rows.unsqueeze(1).to_broadcast([P, PACK, n * P])
             nc.vector.scalar_tensor_tensor(made, values, 0.0, gates, ALU.is_gt, ALU.mult)
 
         def multiply(b, n):
+            first = max(x for x in factor if x <= b)
+            factors = factor[first][:].rearrange("p (t s) -> p t s", t=PACK)[:, :, (b - first) * P : (b - first + n) * P]
             nc.vector.tensor_tensor(
-                blocks_of(da, b, n).rearrange("p (s t) -> p s t", t=PACK),
-                planes_of(b, n).rearrange("p t s -> p s t"),
-                blocks_of(factor, b, n).rearrange("p (s t) -> p s t", t=PACK),
+                blocks_of(da, b, n).rearrange("p (r i t) -> p r t i", i=2, t=PACK),
+                planes_of(b, n).rearrange("p t (r i) -> p r t i", i=2),
+                factors.rearrange("p t (r i) -> p r t i", i=2),
                 ALU.mult,
             )
 
-        def weave(b):
+        def weave(b, n=2):
             nc.gpsimd.tensor_tensor(
-                blocks_of(da, b, 2).rearrange("p (r i t) -> p r t i", i=PAIR, t=PACK),
-                planes_of(b, 2).rearrange("p t (r i) -> p r t i", i=PAIR),
+                blocks_of(da, b, n).rearrange("p (r i t) -> p r t i", i=PAIR, t=PACK),
+                planes_of(b, n).rearrange("p t (r i) -> p r t i", i=PAIR),
                 factor[b][:].rearrange("p (t r i) -> p r t i", i=PAIR, t=PACK),
                 ALU.mult,
             )
@@ -252,36 +250,39 @@ def tile_moe_sdb_relu_kernel(
         gather(0, 2, range(2, PACK), scalar_gather)
         make_factor(0, 2)
         weave(0)
-        plain[2] = place("plain2", 2 * H, F32, 20)
+        plain[2] = place("plain2", 2 * H, F32, 21)
         gather(2, 2, range(PACK), scalar_gather)
-        plain[4] = place("plain4", 4 * H, F32, 12)
+        plain[4] = place("plain4", 4 * H, F32, 13)
         gather(4, 4, range(2), nc.vector.tensor_copy)
         gather(4, 4, range(2, PACK), scalar_gather)
         make_factor(2, 2)
         weave(2)
         make_factor(4, 2)
         weave(4)
-        make_factor(6, 2, place("factor6", 2 * H, F32, 48))
-        weave(6)
-        plain[8] = place("plain8", 4 * H, F32, 24)
+        make_factor(6, 1, place("factor6", H, F32, 7))
+        weave(6, 1)
+        make_factor(7, 1)
+        plain[8] = place("plain8", 4 * H, F32, 25)
         gather(8, 4, range(PACK), scalar_gather)
-        plain[12] = place("plain12", 4 * H, F32, 32)
+        plain[12] = place("plain12", 4 * H, F32, 33)
         gather(12, 4, range(PACK), scalar_gather)
+        plain[16] = place("plain16", 2 * H, F32, 52)
+        gather(16, 2, range(PACK), scalar_gather)
         make_factor(8, 4)
         make_factor(12, 4)
         make_factor(16, 2)
         codes = place("codes", S, U32, 1)
-        quantise(0, 8)
+        quantise(0, 4)
+        quantise(4, 3)
         experts(0, 4, 5)
-        experts(4, 4, 6)
-        da[8] = place("da8", 4 * H, BF16, 10)
-        da[12] = place("da12", 4 * H, BF16, 44)
-        da[16] = place("da16", 2 * H, BF16, 48)
+        da[7] = place("da7", 5 * H, BF16, 45)
+        da[12] = place("da12", 4 * H, BF16, 41)
+        da[16] = place("da16", 2 * H, BF16, 50)
+        multiply(7, 1)
         multiply(8, 4)
-        plain[16] = place("plain16", 2 * H, F32, 40)
-        gather(16, 2, range(1), nc.vector.tensor_copy)
-        gather(16, 2, range(1, PACK), scalar_gather)
+        quantise(7, 1)
         quantise(8, 4)
+        experts(4, 4, 6)
         experts(8, 4, 7)
         multiply(12, 2)
         multiply(14, 2)

@@ -26,12 +26,12 @@ ACT = mybir.ActivationFunctionType
 
 BLOCKS = S // P
 PAIR = 4
-POOLED = 7
+POOLED = 8
 FIRST = 2
-GATE_BANKS = [((2, 3, 4, 5), 1), ((6, 7, 16, 17), 0), ((8, 9, 10, 11), 3), ((12, 13, 14, 15), 4)]
+GATE_BANKS = [((2, 3, 16, 17), 1), ((4, 5, 6, 7), 0), ((8, 9, 10, 11), 3), ((12, 13, 14, 15), 4)]
 TOKEN_BANKS = [(0, 512), (512, 256)]
 FIRST_TOKEN_BANKS = [(0, 256), (256, 256), (512, 128), (640, 128)]
-VECTOR_PRODUCTS = (0, 2, 5)
+VECTOR_PRODUCTS = (0, 2, 5, 7)
 ALONE = (0, 160)
 SHARED = [(160, 192), (352, 256), (608, 160)]
 KB = 1024
@@ -56,11 +56,11 @@ def tile_moe_sdb_relu_kernel(
         def tokens(b0, n):
             return offs_t[:, b0 * P // LIST_ROWS : (b0 + n) * P // LIST_ROWS]
 
-        w2_plane_raw = keep.tile([P, H], U8, align_bytes=64)
+        w2_plane_raw = keep.tile([P, 2 * H], U8, align_bytes=64)
         dy_plane = keep.tile([P, T], U8, align_bytes=64)
         w1_plane = keep.tile([P, E * K], U8, align_bytes=64)
         gate_blocks = keep.tile([P, P], F32)
-        nc.gpsimd.memset(w2_plane_raw[P // 2 :, :].bitcast(I32), 0)
+        nc.gpsimd.memset(w2_plane_raw[: P // 2, :].bitcast(I32), 0)
         nc.vector.memset(dy_plane[:].bitcast(I32), 0)
         nc.vector.memset(w1_plane[:].bitcast(I32), 0)
         nc.gpsimd.memset(gate_blocks[:], 0.0)
@@ -76,12 +76,11 @@ def tile_moe_sdb_relu_kernel(
         w2_raw = keep.tile([P, 2 * H], U8, align_bytes=64)
         for q in range(2):
             nc.sync.dma_start(
-                w2_plane_raw[32 * q : 32 * (q + 1), :].bitcast(I32),
-                w2t_scales[0, 4 * q : 4 * q + 4, :].bitcast(I32).partition_broadcast(8),
+                w2_plane_raw[32 * q : 32 * q + 4, :].bitcast(I32).rearrange("r (h c) -> r h c", h=2),
+                w2t_scales[0].bitcast(I32).rearrange("(h q r) c -> q r h c", h=2, q=2)[q],
             )
         nc.sync.dma_start(w2_raw[:].bitcast(I32), w2t_words[0].bitcast(I32))
-        load_scale_rows(w2_plane_raw, w2t_scales, range(2, QUADRANTS))
-        dy_codes = place("dy_codes", 4 * T, U8, 20)
+        dy_codes = place("dy_codes", 4 * T, U8, 19)
         nc.sync.dma_start(dy_codes[:].bitcast(I32), dy_words[0].rearrange("p t d -> p (t d)").bitcast(I32))
         load_scale_rows(dy_plane, dy_scales, range(QUADRANTS))
         offs_t = keep.tile([P, S // LIST_ROWS], U16)
@@ -91,7 +90,7 @@ def tile_moe_sdb_relu_kernel(
         nc.sync.dma_start(gate_rows[:], gate[:, : FIRST * P])
         a_rows = a.rearrange("(p t) s -> p t s", t=PACK)
         a_t = {}
-        a_at = {0: 13, 4: 31, 6: 52, 16: 9}
+        a_at = {0: 12, 4: 28, 8: 56, 16: 8}
 
         def load_a(b, n=2):
             if b in a_at:
@@ -110,7 +109,7 @@ def tile_moe_sdb_relu_kernel(
                 w1_plane[32 * q : 32 * q + 4, :].rearrange("r (e k) -> r e k", e=E).bitcast(I32),
                 w1t_scales[:, 0, 4 * q : 4 * q + 4, :].rearrange("e r k -> r e k").bitcast(I32),
             )
-        for b, n in ((4, 2), (6, 2), (8, 4), (12, 4), (16, 2)):
+        for b, n in ((4, 4), (8, 4), (12, 4), (16, 2)):
             load_a(b, n)
         pos_t = []
         for r, pos in enumerate((pos1, pos2, pos3)):
@@ -119,6 +118,7 @@ def tile_moe_sdb_relu_kernel(
 
         w2_codes = keep.tile([P, 2 * H], U8, align_bytes=64)
         w2_plane = keep.tile([P, H], U8, align_bytes=64)
+        nc.vector.tensor_copy(w2_plane_raw[P // 2 :, :H].bitcast(I32), w2_plane_raw[: P // 2, H:].bitcast(I32))
         for ts in (slice(0, 1), slice(1, PACK)):
             nc.vector.tensor_copy(
                 w2_codes[:].bitcast(U16).rearrange("p (t m) -> p t m", t=PACK)[:, ts, :],
@@ -126,7 +126,7 @@ def tile_moe_sdb_relu_kernel(
             )
             nc.vector.tensor_copy(
                 w2_plane[:].rearrange("p (t m) -> p t m", t=PACK)[:, ts, :],
-                w2_plane_raw[:].rearrange("p (m t) -> p t m", t=PACK)[:, ts, :],
+                w2_plane_raw[:, :H].rearrange("p (m t) -> p t m", t=PACK)[:, ts, :],
             )
 
         dc = [keep.tile([P, T], F32, name="dc%d" % t) for t in range(PACK)]
@@ -162,7 +162,7 @@ def tile_moe_sdb_relu_kernel(
                 gate_spread[b] = (rows, j)
                 nc.tensor.transpose(rows[:, j * P : (j + 1) * P], gate_col(b).to_broadcast([P, P]), identity[:])
 
-        da = {0: place("da0", POOLED * H, BF16, 44.5)}
+        da = {0: place("da0", POOLED * H, BF16, 40)}
         plain = {}
         factor = {}
 
@@ -172,6 +172,9 @@ def tile_moe_sdb_relu_kernel(
 
         def scalar_gather(dst, src):
             nc.scalar.activation(dst, src, ACT.Copy)
+
+        def gated_gather(dst, src):
+            nc.vector.tensor_tensor(dst, src, gate_rows[:], ALU.mult)
 
         def gather(b0, n, planes, copy):
             for t in planes:
@@ -183,11 +186,8 @@ def tile_moe_sdb_relu_kernel(
 
         def make_factor(b, n, tile=None):
             factor[b] = tile or keep.tile([P, n * H], F32, name="factor%d" % b, align_bytes=64)
-            if b < FIRST:
-                rows = gate_rows[:]
-            else:
-                spread, j = gate_spread[b]
-                rows = spread[:, j * P : (j + n) * P]
+            spread, j = gate_spread[b]
+            rows = spread[:, j * P : (j + n) * P]
             made = factor[b][:].rearrange("p (t s) -> p t s", t=PACK)
             first = max(x for x in a_t if x <= b)
             values = a_t[first][:].rearrange("p (t s) -> p t s", t=PACK)[:, :, (b - first) * P : (b - first + n) * P]
@@ -246,43 +246,47 @@ def tile_moe_sdb_relu_kernel(
             copy(dx[:, b0 * P : (b0 + n) * P], sums[b0][:, : n * P])
 
         plain[0] = keep.tile([P, 2 * H], F32, name="plain0", align_bytes=64)
-        gather(0, 2, range(2), nc.vector.tensor_copy)
+        gather(0, 2, range(2), gated_gather)
         gather(0, 2, range(2, PACK), scalar_gather)
-        make_factor(0, 2)
+        factor[0] = keep.tile([P, 2 * H], F32, name="factor0", align_bytes=64)
+        nc.vector.tensor_scalar(factor[0][:, :H], a_t[0][:, :H], 0.0, None, ALU.is_gt)
+        nc.vector.scalar_tensor_tensor(
+            factor[0][:, H:].rearrange("p (t s) -> p t s", t=2),
+            a_t[0][:, H:].rearrange("p (t s) -> p t s", t=2),
+            0.0,
+            gate_rows[:].unsqueeze(1).to_broadcast([P, 2, C]),
+            ALU.is_gt,
+            ALU.mult,
+        )
         weave(0)
-        plain[2] = place("plain2", 2 * H, F32, 21)
+        plain[2] = place("plain2", 2 * H, F32, 20)
         gather(2, 2, range(PACK), scalar_gather)
-        plain[4] = place("plain4", 4 * H, F32, 13)
+        plain[4] = place("plain4", 4 * H, F32, 12)
         gather(4, 4, range(2), nc.vector.tensor_copy)
         gather(4, 4, range(2, PACK), scalar_gather)
         make_factor(2, 2)
         weave(2)
-        make_factor(4, 2)
-        weave(4)
-        make_factor(6, 1, place("factor6", H, F32, 7))
-        weave(6, 1)
-        make_factor(7, 1)
-        plain[8] = place("plain8", 4 * H, F32, 25)
-        gather(8, 4, range(PACK), scalar_gather)
-        plain[12] = place("plain12", 4 * H, F32, 33)
+        make_factor(4, 4, place("factor4", 4 * H, F32, 48))
+        weave(4, 4)
+        plain[8] = place("plain8", 4 * H, F32, 24)
+        gather(8, 4, range(1), nc.vector.tensor_copy)
+        gather(8, 4, range(1, PACK), scalar_gather)
+        plain[12] = place("plain12", 4 * H, F32, 32)
         gather(12, 4, range(PACK), scalar_gather)
-        plain[16] = place("plain16", 2 * H, F32, 52)
-        gather(16, 2, range(PACK), scalar_gather)
         make_factor(8, 4)
+        plain[16] = place("plain16", 2 * H, F32, 56)
+        gather(16, 2, range(PACK), scalar_gather)
         make_factor(12, 4)
         make_factor(16, 2)
         codes = place("codes", S, U32, 1)
-        quantise(0, 4)
-        quantise(4, 3)
+        quantise(0, 8)
         experts(0, 4, 5)
-        da[7] = place("da7", 5 * H, BF16, 45)
-        da[12] = place("da12", 4 * H, BF16, 41)
-        da[16] = place("da16", 2 * H, BF16, 50)
-        multiply(7, 1)
-        multiply(8, 4)
-        quantise(7, 1)
-        quantise(8, 4)
         experts(4, 4, 6)
+        da[8] = place("da8", 4 * H, BF16, 10)
+        da[12] = place("da12", 4 * H, BF16, 44)
+        da[16] = place("da16", 2 * H, BF16, 48)
+        multiply(8, 4)
+        quantise(8, 4)
         experts(8, 4, 7)
         multiply(12, 2)
         multiply(14, 2)

@@ -25,13 +25,13 @@ ALU = mybir.AluOpType
 ACT = mybir.ActivationFunctionType
 
 BLOCKS = S // P
-PAIR = 4
+PAIR = 2
 POOLED = 8
 FIRST = 2
 GATE_BANKS = [((2, 3, 16, 17), 1), ((4, 5, 6, 7), 0), ((8, 9, 10, 11), 3), ((12, 13, 14, 15), 4)]
 TOKEN_BANKS = [(0, 512), (512, 256)]
 FIRST_TOKEN_BANKS = [(0, 256), (256, 256), (512, 128), (640, 128)]
-VECTOR_PRODUCTS = (0, 2, 5, 7)
+VECTOR_PRODUCTS = (0, 2, 5)
 ALONE = (0, 160)
 SHARED = [(160, 192), (352, 256), (608, 160)]
 KB = 1024
@@ -56,11 +56,11 @@ def tile_moe_sdb_relu_kernel(
         def tokens(b0, n):
             return offs_t[:, b0 * P // LIST_ROWS : (b0 + n) * P // LIST_ROWS]
 
-        w2_plane_raw = keep.tile([P, 2 * H], U8, align_bytes=64)
+        w2_plane_raw = keep.tile([P, H], U8, align_bytes=64)
         dy_plane = keep.tile([P, T], U8, align_bytes=64)
         w1_plane = keep.tile([P, E * K], U8, align_bytes=64)
         gate_blocks = keep.tile([P, P], F32)
-        nc.gpsimd.memset(w2_plane_raw[: P // 2, :].bitcast(I32), 0)
+        nc.gpsimd.memset(w2_plane_raw[P // 2 :, :].bitcast(I32), 0)
         nc.vector.memset(dy_plane[:].bitcast(I32), 0)
         nc.vector.memset(w1_plane[:].bitcast(I32), 0)
         nc.gpsimd.memset(gate_blocks[:], 0.0)
@@ -76,10 +76,11 @@ def tile_moe_sdb_relu_kernel(
         w2_raw = keep.tile([P, 2 * H], U8, align_bytes=64)
         for q in range(2):
             nc.sync.dma_start(
-                w2_plane_raw[32 * q : 32 * q + 4, :].bitcast(I32).rearrange("r (h c) -> r h c", h=2),
-                w2t_scales[0].bitcast(I32).rearrange("(h q r) c -> q r h c", h=2, q=2)[q],
+                w2_plane_raw[32 * q : 32 * (q + 1), :].bitcast(I32),
+                w2t_scales[0, 4 * q : 4 * q + 4, :].bitcast(I32).partition_broadcast(8),
             )
         nc.sync.dma_start(w2_raw[:].bitcast(I32), w2t_words[0].bitcast(I32))
+        load_scale_rows(w2_plane_raw, w2t_scales, range(2, QUADRANTS))
         dy_codes = place("dy_codes", 4 * T, U8, 19)
         nc.sync.dma_start(dy_codes[:].bitcast(I32), dy_words[0].rearrange("p t d -> p (t d)").bitcast(I32))
         load_scale_rows(dy_plane, dy_scales, range(QUADRANTS))
@@ -118,7 +119,6 @@ def tile_moe_sdb_relu_kernel(
 
         w2_codes = keep.tile([P, 2 * H], U8, align_bytes=64)
         w2_plane = keep.tile([P, H], U8, align_bytes=64)
-        nc.vector.tensor_copy(w2_plane_raw[P // 2 :, :H].bitcast(I32), w2_plane_raw[: P // 2, H:].bitcast(I32))
         for ts in (slice(0, 1), slice(1, PACK)):
             nc.vector.tensor_copy(
                 w2_codes[:].bitcast(U16).rearrange("p (t m) -> p t m", t=PACK)[:, ts, :],
@@ -126,7 +126,7 @@ def tile_moe_sdb_relu_kernel(
             )
             nc.vector.tensor_copy(
                 w2_plane[:].rearrange("p (t m) -> p t m", t=PACK)[:, ts, :],
-                w2_plane_raw[:, :H].rearrange("p (m t) -> p t m", t=PACK)[:, ts, :],
+                w2_plane_raw[:].rearrange("p (m t) -> p t m", t=PACK)[:, ts, :],
             )
 
         dc = [keep.tile([P, T], F32, name="dc%d" % t) for t in range(PACK)]
@@ -269,8 +269,7 @@ def tile_moe_sdb_relu_kernel(
         make_factor(4, 4, place("factor4", 4 * H, F32, 48))
         weave(4, 4)
         plain[8] = place("plain8", 4 * H, F32, 24)
-        gather(8, 4, range(1), nc.vector.tensor_copy)
-        gather(8, 4, range(1, PACK), scalar_gather)
+        gather(8, 4, range(PACK), scalar_gather)
         plain[12] = place("plain12", 4 * H, F32, 32)
         gather(12, 4, range(PACK), scalar_gather)
         make_factor(8, 4)

@@ -31,7 +31,7 @@ FIRST = 2
 GATE_BANKS = [((2, 3, 16, 17), 1), ((4, 5, 6, 7), 0), ((8, 9, 10, 11), 3), ((12, 13, 14, 15), 4)]
 TOKEN_BANKS = [(0, 512), (512, 256)]
 FIRST_TOKEN_BANKS = [(0, 256), (256, 256), (512, 128), (640, 128)]
-VECTOR_PRODUCTS = (0, 2, 5)
+VECTOR_PRODUCTS = (0, 2, 5, 7)
 ALONE = (0, 160)
 SHARED = [(160, 192), (352, 256), (608, 160)]
 KB = 1024
@@ -57,33 +57,29 @@ def tile_moe_sdb_relu_kernel(
             return offs_t[:, b0 * P // LIST_ROWS : (b0 + n) * P // LIST_ROWS]
 
         w2_plane_raw = keep.tile([P, H], U8, align_bytes=64)
-        dy_plane = keep.tile([P, T], U8, align_bytes=64)
         w1_plane = keep.tile([P, E * K], U8, align_bytes=64)
         gate_blocks = keep.tile([P, P], F32)
-        nc.gpsimd.memset(w2_plane_raw[P // 2 :, :].bitcast(I32), 0)
-        nc.vector.memset(dy_plane[:].bitcast(I32), 0)
+        nc.gpsimd.memset(w2_plane_raw[:].bitcast(I32), 0)
         nc.vector.memset(w1_plane[:].bitcast(I32), 0)
         nc.gpsimd.memset(gate_blocks[:], 0.0)
         identity = keep.tile([P, P], F32)
         make_identity(nc, identity[:])
 
-        def load_scale_rows(plane, scales, quadrants):
-            for q in quadrants:
-                nc.sync.dma_start(
-                    plane[32 * q : 32 * q + 4, :].bitcast(I32), scales[0, 4 * q : 4 * q + 4, :].bitcast(I32)
-                )
-
-        w2_raw = keep.tile([P, 2 * H], U8, align_bytes=64)
-        for q in range(2):
+        w2_rows = keep.tile([4, QUADRANTS * H], U8, align_bytes=64)
+        nc.sync.dma_start(
+            w2_rows[:].bitcast(I32).rearrange("r (q c) -> r q c", q=QUADRANTS),
+            w2t_scales[0].bitcast(I32).rearrange("(q r) c -> r q c", q=QUADRANTS),
+        )
+        dy_plane = keep.tile([P, T], U8, align_bytes=64)
+        for q in range(QUADRANTS):
             nc.sync.dma_start(
-                w2_plane_raw[32 * q : 32 * (q + 1), :].bitcast(I32),
-                w2t_scales[0, 4 * q : 4 * q + 4, :].bitcast(I32).partition_broadcast(8),
+                dy_plane[32 * q : 32 * (q + 1), :].bitcast(I32),
+                dy_scales[0, 4 * q : 4 * q + 4, :].bitcast(I32).partition_broadcast(8),
             )
+        w2_raw = keep.tile([P, 2 * H], U8, align_bytes=64)
         nc.sync.dma_start(w2_raw[:].bitcast(I32), w2t_words[0].bitcast(I32))
-        load_scale_rows(w2_plane_raw, w2t_scales, range(2, QUADRANTS))
         dy_codes = place("dy_codes", 4 * T, U8, 19)
         nc.sync.dma_start(dy_codes[:].bitcast(I32), dy_words[0].rearrange("p t d -> p (t d)").bitcast(I32))
-        load_scale_rows(dy_plane, dy_scales, range(QUADRANTS))
         offs_t = keep.tile([P, S // LIST_ROWS], U16)
         nc.sync.dma_start(offs_t[:], offs)
 
@@ -119,6 +115,10 @@ def tile_moe_sdb_relu_kernel(
 
         w2_codes = keep.tile([P, 2 * H], U8, align_bytes=64)
         w2_plane = keep.tile([P, H], U8, align_bytes=64)
+        for q in range(QUADRANTS):
+            nc.vector.tensor_copy(
+                w2_plane_raw[32 * q : 32 * q + 4, :].bitcast(I32), w2_rows[:, q * H : (q + 1) * H].bitcast(I32)
+            )
         for ts in (slice(0, 1), slice(1, PACK)):
             nc.vector.tensor_copy(
                 w2_codes[:].bitcast(U16).rearrange("p (t m) -> p t m", t=PACK)[:, ts, :],
@@ -284,8 +284,10 @@ def tile_moe_sdb_relu_kernel(
         da[8] = place("da8", 4 * H, BF16, 10)
         da[12] = place("da12", 4 * H, BF16, 44)
         da[16] = place("da16", 2 * H, BF16, 48)
-        multiply(8, 4)
-        quantise(8, 4)
+        multiply(8, 2)
+        multiply(10, 2)
+        quantise(8, 2)
+        quantise(10, 2)
         experts(8, 4, 7)
         multiply(12, 2)
         multiply(14, 2)

from contextlib import ExitStack

import concourse.mybir as mybir
from concourse.masks import make_identity

K, T, E, C, H, N = 128, 768, 9, 256, 512, 512
S = E * C
P = 128
PACK = 4
QUADRANTS = 4
LIST_ROWS = 16
BANK = 512
BANKS = 8
FLOPS = 2 * N * H * T + 2 * H * K * S

F32 = mybir.dt.float32
BF16 = mybir.dt.bfloat16
I32 = mybir.dt.int32
U32 = mybir.dt.uint32
U16 = mybir.dt.uint16
U8 = mybir.dt.uint8
FP8X4 = mybir.dt.float8_e4m3fn_x4
FP4X4 = mybir.dt.float4_e2m1fn_x4
ALU = mybir.AluOpType
ACT = mybir.ActivationFunctionType

BLOCKS = S // P
PAIR = 2
POOLED = 8
FIRST = 2
GATE_BANKS = [((2, 3, 16, 17), 1), ((4, 5, 6, 7), 0), ((8, 9, 10, 11), 3), ((12, 13, 14, 15), 4)]
TOKEN_BANKS = [(0, 512), (512, 256)]
FIRST_TOKEN_BANKS = [(0, 256), (256, 256), (512, 128), (640, 128)]
VECTOR_PRODUCTS = (0, 2, 5, 7)
ALONE = (0, 160)
SHARED = [(160, 192), (352, 256), (608, 160)]
KB = 1024


def tile_moe_sdb_relu_kernel(
    tc, dy_words, dy_scales, w2t_words, w2t_scales, w1t_words, w1t_scales, a, gate, offs, pos1, pos2, pos3, out
):
    nc = tc.nc

    with ExitStack() as ctx:
        keep = ctx.enter_context(tc.tile_pool(name="keep", bufs=1))
        placed = ctx.enter_context(tc.tile_pool(name="placed", bufs=1))
        psum = ctx.enter_context(tc.psum_pool(name="psum", bufs=1))

        def bank(name, which):
            return psum.tile([P, BANK], F32, name=name, offset=4 * BANK * which)

        def place(name, columns, dtype, kb):
            return placed.tile([P, columns], dtype, name=name, offset=int(kb * KB), align_bytes=64)

        def tokens(b0, n):
            return offs_t[:, b0 * P // LIST_ROWS : (b0 + n) * P // LIST_ROWS]

        w2_plane_raw = keep.tile([P, H], U8, align_bytes=64)
        w1_plane = keep.tile([P, E * K], U8, align_bytes=64)
        gate_blocks = keep.tile([P, P], F32)
        nc.gpsimd.memset(w2_plane_raw[:].bitcast(I32), 0)
        nc.vector.memset(w1_plane[:].bitcast(I32), 0)
        nc.gpsimd.memset(gate_blocks[:], 0.0)
        identity = keep.tile([P, P], F32)
        make_identity(nc, identity[:])

        w2_rows = keep.tile([4, QUADRANTS * H], U8, align_bytes=64)
        nc.sync.dma_start(
            w2_rows[:].bitcast(I32).rearrange("r (q c) -> r q c", q=QUADRANTS),
            w2t_scales[0].bitcast(I32).rearrange("(q r) c -> r q c", q=QUADRANTS),
        )
        dy_plane = keep.tile([P, T], U8, align_bytes=64)
        for q in range(QUADRANTS):
            nc.sync.dma_start(
                dy_plane[32 * q : 32 * (q + 1), :].bitcast(I32),
                dy_scales[0, 4 * q : 4 * q + 4, :].bitcast(I32).partition_broadcast(8),
            )
        w2_raw = keep.tile([P, 2 * H], U8, align_bytes=64)
        nc.sync.dma_start(w2_raw[:].bitcast(I32), w2t_words[0].bitcast(I32))
        dy_codes = place("dy_codes", 4 * T, U8, 19)
        nc.sync.dma_start(dy_codes[:].bitcast(I32), dy_words[0].rearrange("p t d -> p (t d)").bitcast(I32))
        offs_t = keep.tile([P, S // LIST_ROWS], U16)
        nc.sync.dma_start(offs_t[:], offs)

        gate_rows = keep.tile([P, FIRST * P], F32, align_bytes=64)
        nc.sync.dma_start(gate_rows[:], gate[:, : FIRST * P])
        a_rows = a.rearrange("(p t) s -> p t s", t=PACK)
        a_t = {}
        a_at = {0: 12, 4: 28, 8: 56, 16: 8}

        def load_a(b, n=2):
            if b in a_at:
                a_t[b] = place("a%d" % b, n * H, F32, a_at[b])
            else:
                a_t[b] = keep.tile([P, n * H], F32, name="a%d" % b, align_bytes=64)
            nc.sync.dma_start(a_t[b][:].rearrange("p (t s) -> p t s", t=PACK), a_rows[:, :, b * P : (b + n) * P])

        load_a(0)
        nc.sync.dma_start(gate_blocks[: BLOCKS - FIRST, :], gate[0, FIRST * P :].rearrange("(b s) -> b s", s=P))
        load_a(2)
        w1_codes = keep.tile([P, E, 2 * K], U8, align_bytes=64)
        nc.sync.dma_start(w1_codes[:].bitcast(I32), w1t_words[:, 0].rearrange("e p b -> p e b").bitcast(I32))
        for q in range(QUADRANTS):
            nc.sync.dma_start(
                w1_plane[32 * q : 32 * q + 4, :].rearrange("r (e k) -> r e k", e=E).bitcast(I32),
                w1t_scales[:, 0, 4 * q : 4 * q + 4, :].rearrange("e r k -> r e k").bitcast(I32),
            )
        for b, n in ((4, 4), (8, 4), (12, 4), (16, 2)):
            load_a(b, n)
        pos_t = []
        for r, pos in enumerate((pos1, pos2, pos3)):
            pos_t.append(keep.tile([P, T // LIST_ROWS], U16, name="pos%d" % r))
            nc.sync.dma_start(pos_t[r][:], pos)

        w2_codes = keep.tile([P, 2 * H], U8, align_bytes=64)
        w2_plane = keep.tile([P, H], U8, align_bytes=64)
        for q in range(QUADRANTS):
            nc.vector.tensor_copy(
                w2_plane_raw[32 * q : 32 * q + 4, :].bitcast(I32), w2_rows[:, q * H : (q + 1) * H].bitcast(I32)
            )
        for ts in (slice(0, 1), slice(1, PACK)):
            nc.vector.tensor_copy(
                w2_codes[:].bitcast(U16).rearrange("p (t m) -> p t m", t=PACK)[:, ts, :],
                w2_raw[:].bitcast(U16).rearrange("p (m t) -> p t m", t=PACK)[:, ts, :],
            )
            nc.vector.tensor_copy(
                w2_plane[:].rearrange("p (t m) -> p t m", t=PACK)[:, ts, :],
                w2_plane_raw[:].rearrange("p (m t) -> p t m", t=PACK)[:, ts, :],
            )

        dc = [keep.tile([P, T], F32, name="dc%d" % t) for t in range(PACK)]
        products = [(t, t0, n) for t in range(PACK) for t0, n in (FIRST_TOKEN_BANKS if t == 0 else TOKEN_BANKS)]
        for x, (t, t0, n) in enumerate(products):
            acc = bank("product%d" % x, x % BANKS)
            nc.tensor.matmul_mx(
                out=acc[:, :n],
                lhsT=w2_codes[:, 2 * P * t : 2 * P * (t + 1)].bitcast(FP4X4),
                lhsT_scale=w2_plane[:, P * t : P * (t + 1)],
                rhs=dy_codes[:, 4 * t0 : 4 * (t0 + n)].bitcast(FP8X4),
                rhs_scale=dy_plane[:, t0 : t0 + n],
                start=True,
                stop=True,
            )
            if x in VECTOR_PRODUCTS:
                nc.vector.tensor_copy(dc[t][:, t0 : t0 + n], acc[:, :n])
            else:
                nc.scalar.copy(dc[t][:, t0 : t0 + n], acc[:, :n])

        gate_cols = keep.tile([P, BLOCKS - FIRST], F32, name="gate_cols", align_bytes=64)
        gates_turned = bank("gates_turned", 2)
        nc.tensor.transpose(gates_turned[:, :P], gate_blocks[:], identity[:])
        nc.vector.tensor_copy(gate_cols[:], gates_turned[:, : BLOCKS - FIRST])

        def gate_col(b):
            return gate_cols[:, b - FIRST : b - FIRST + 1]

        gate_spread = {}
        for blocks, where in GATE_BANKS:
            rows = bank("gate%d" % blocks[0], where)
            for j, b in enumerate(blocks):
                gate_spread[b] = (rows, j)
                nc.tensor.transpose(rows[:, j * P : (j + 1) * P], gate_col(b).to_broadcast([P, P]), identity[:])

        da = {0: place("da0", POOLED * H, BF16, 40)}
        plain = {}
        factor = {}

        def blocks_of(tiles, b0, n):
            first = max(b for b in tiles if b <= b0)
            return tiles[first][:, (b0 - first) * H : (b0 - first + n) * H]

        def scalar_gather(dst, src):
            nc.scalar.activation(dst, src, ACT.Copy)

        def gated_gather(dst, src):
            nc.vector.tensor_tensor(dst, src, gate_rows[:], ALU.mult)

        def gather(b0, n, planes, copy):
            for t in planes:
                copy(plain[b0][:, t * n * P : (t + 1) * n * P], dc[t][:].indirect(tokens(b0, n)))

        def planes_of(b, n):
            first = max(x for x in plain if x <= b)
            return plain[first][:].rearrange("p (t s) -> p t s", t=PACK)[:, :, (b - first) * P : (b - first + n) * P]

        def make_factor(b, n, tile=None):
            factor[b] = tile or keep.tile([P, n * H], F32, name="factor%d" % b, align_bytes=64)
            spread, j = gate_spread[b]
            rows = spread[:, j * P : (j + n) * P]
            made = factor[b][:].rearrange("p (t s) -> p t s", t=PACK)
            first = max(x for x in a_t if x <= b)
            values = a_t[first][:].rearrange("p (t s) -> p t s", t=PACK)[:, :, (b - first) * P : (b - first + n) * P]
            gates = rows.unsqueeze(1).to_broadcast([P, PACK, n * P])
            nc.vector.scalar_tensor_tensor(made, values, 0.0, gates, ALU.is_gt, ALU.mult)

        def multiply(b, n):
            first = max(x for x in factor if x <= b)
            factors = factor[first][:].rearrange("p (t s) -> p t s", t=PACK)[:, :, (b - first) * P : (b - first + n) * P]
            nc.vector.tensor_tensor(
                blocks_of(da, b, n).rearrange("p (r i t) -> p r t i", i=2, t=PACK),
                planes_of(b, n).rearrange("p t (r i) -> p r t i", i=2),
                factors.rearrange("p t (r i) -> p r t i", i=2),
                ALU.mult,
            )

        def weave(b, n=2):
            nc.gpsimd.tensor_tensor(
                blocks_of(da, b, n).rearrange("p (r i t) -> p r t i", i=PAIR, t=PACK),
                planes_of(b, n).rearrange("p t (r i) -> p r t i", i=PAIR),
                factor[b][:].rearrange("p (t r i) -> p r t i", i=PAIR, t=PACK),
                ALU.mult,
            )

        dx = keep.tile([P, S], F32, name="dx", align_bytes=64)
        plane = keep.tile([P, S], U8, name="plane", align_bytes=64)

        def codes_of(s0, s1):
            return codes[:, s0:s1].bitcast(FP8X4)

        def quantise(b0, n):
            s0, s1 = b0 * P, (b0 + n) * P
            nc.vector.quantize_mx(out=codes_of(s0, s1), scales=plane[:, s0:s1], in_=blocks_of(da, b0, n))

        sums = {}

        def experts(b0, n, where=None):
            if where is not None:
                sums[b0] = bank("sums%d" % b0, where)
            first = max(x for x in sums if x <= b0)
            s0 = first * P
            width = min(n * P, C)
            for v0 in range(b0 * P, (b0 + n) * P, width):
                e = v0 // C
                nc.tensor.matmul_mx(
                    out=sums[first][:, v0 - s0 : v0 - s0 + width],
                    lhsT=w1_codes[:, e, :].bitcast(FP4X4),
                    lhsT_scale=w1_plane[:, K * e : K * (e + 1)],
                    rhs=codes_of(v0, v0 + width),
                    rhs_scale=plane[:, v0 : v0 + width],
                    start=True,
                    stop=True,
                )

        def empty(b0, n, copy):
            copy(dx[:, b0 * P : (b0 + n) * P], sums[b0][:, : n * P])

        plain[0] = keep.tile([P, 2 * H], F32, name="plain0", align_bytes=64)
        gather(0, 2, range(2), gated_gather)
        gather(0, 2, range(2, PACK), scalar_gather)
        factor[0] = keep.tile([P, 2 * H], F32, name="factor0", align_bytes=64)
        nc.vector.tensor_scalar(factor[0][:, :H], a_t[0][:, :H], 0.0, None, ALU.is_gt)
        nc.vector.scalar_tensor_tensor(
            factor[0][:, H:].rearrange("p (t s) -> p t s", t=2),
            a_t[0][:, H:].rearrange("p (t s) -> p t s", t=2),
            0.0,
            gate_rows[:].unsqueeze(1).to_broadcast([P, 2, C]),
            ALU.is_gt,
            ALU.mult,
        )
        weave(0)
        plain[2] = place("plain2", 2 * H, F32, 20)
        gather(2, 2, range(PACK), scalar_gather)
        plain[4] = place("plain4", 4 * H, F32, 12)
        gather(4, 4, range(2), nc.vector.tensor_copy)
        gather(4, 4, range(2, PACK), scalar_gather)
        make_factor(2, 2)
        weave(2)
        make_factor(4, 4, place("factor4", 4 * H, F32, 48))
        weave(4, 4)
        plain[8] = place("plain8", 4 * H, F32, 24)
        gather(8, 4, range(PACK), scalar_gather)
        plain[12] = place("plain12", 4 * H, F32, 32)
        gather(12, 4, range(PACK), scalar_gather)
        make_factor(8, 4)
        plain[16] = place("plain16", 2 * H, F32, 56)
        gather(16, 2, range(PACK), scalar_gather)
        make_factor(12, 4)
        make_factor(16, 2)
        codes = place("codes", S, U32, 1)
        quantise(0, 8)
        experts(0, 4, 5)
        experts(4, 4, 6)
        da[8] = place("da8", 4 * H, BF16, 10)
        da[12] = place("da12", 4 * H, BF16, 44)
        da[16] = place("da16", 2 * H, BF16, 48)
        multiply(8, 2)
        multiply(10, 2)
        quantise(8, 2)
        quantise(10, 2)
        experts(8, 4, 7)
        multiply(12, 2)
        multiply(14, 2)
        quantise(12, 2)
        experts(12, 2, 2)
        multiply(16, 1)
        quantise(14, 2)
        experts(14, 2)
        multiply(17, 1)
        quantise(16, 1)
        quantise(17, 1)
        experts(16, 1, 1)
        experts(17, 1, 3)
        empty(0, 4, nc.scalar.copy)
        empty(4, 4, nc.scalar.copy)
        empty(8, 4, nc.scalar.copy)
        empty(12, 4, nc.scalar.copy)
        empty(16, 1, nc.vector.tensor_copy)
        empty(17, 1, nc.scalar.copy)

        def columns(t0, n):
            return slice(t0 // LIST_ROWS, (t0 + n) // LIST_ROWS)

        fetched = {}
        for t0, n in SHARED:
            for r in range(2):
                fetched[t0, r] = keep.tile([P, n], F32, name="fetched%d_%d" % (t0, r))
                nc.scalar.activation(fetched[t0, r][:], dx[:].indirect(pos_t[r][:, columns(t0, n)]), ACT.Copy)
        def fetch_third(t0, n):
            fetched[t0, 2] = keep.tile([P, n], F32, name="part%d" % t0)
            nc.vector.tensor_tensor(
                fetched[t0, 2][:], dx[:].indirect(pos_t[2][:, columns(t0, n)]), fetched[t0, 0][:], ALU.add
            )

        def finish(t0, n):
            whole = keep.tile([P, n], F32, name="whole%d" % t0)
            nc.vector.tensor_tensor(whole[:], fetched[t0, 2][:], fetched[t0, 1][:], ALU.add)
            nc.sync.dma_start(out[:, t0 : t0 + n], whole[:])

        t0, n = ALONE
        one = keep.tile([P, n], F32)
        two = keep.tile([P, n], F32)
        three = keep.tile([P, n], F32)
        nc.vector.tensor_copy(one[:], dx[:].indirect(pos_t[0][:, columns(t0, n)]))
        fetch_third(*SHARED[0])
        nc.vector.tensor_tensor(two[:], dx[:].indirect(pos_t[1][:, columns(t0, n)]), one[:], ALU.add)
        finish(*SHARED[0])
        nc.vector.tensor_tensor(three[:], dx[:].indirect(pos_t[2][:, columns(t0, n)]), two[:], ALU.add)
        nc.sync.dma_start(out[:, t0 : t0 + n], three[:])
        fetch_third(*SHARED[1])
        fetch_third(*SHARED[2])
        finish(*SHARED[1])
        finish(*SHARED[2])
